import numpy as np
import ml_dtypes


def mxq(x, axis, fmt="e4m3"):
    dtype, down = {"e4m3": (ml_dtypes.float8_e4m3fn, 7), "e5m2": (ml_dtypes.float8_e5m2, 14)}[fmt]
    v = np.moveaxis(np.asarray(x, np.float32).astype(ml_dtypes.bfloat16).astype(np.float64), axis, -1)
    blocks = v.reshape(v.shape[:-1] + (-1, 32))
    amax = np.abs(blocks).max(-1, keepdims=True)
    byte = np.maximum(np.where(amax > 0, np.frexp(amax)[1] - 1 + 127, 0) - down, 1)
    scale = np.exp2(byte - 127.0)
    codes = (blocks / scale).astype(np.float32).astype(dtype).astype(np.float64)
    return np.moveaxis((codes * scale).reshape(v.shape), -1, axis)


WIDE = False


def mx_kscale(k):
    if not WIDE:
        return np.ones(k)
    levels = np.array([10, -10, 5, -5, 0])
    if k % 512:
        return np.exp2(np.random.permutation(np.resize(levels, k // 32))).repeat(32)
    a = np.empty((k // 512, 16))
    for p in range(k // 512):
        a[p, :8] = np.random.permutation(np.resize(levels, 8))
        for g in range(8):
            far = levels[np.abs(levels - a[p, g]) >= 10]
            a[p, g + 8] = far[np.random.randint(len(far))]
    return np.exp2(a.ravel()).repeat(32)


def f64(x):
    return np.asarray(x).astype(np.float64)


def striped(idx):
    return np.tile(idx.reshape(-1, 16).T, (8, 1)).astype(np.uint16)


def unstriped(offs):
    return offs[:16].T.reshape(-1).astype(np.int64)


E2M1 = np.array([0.0, 0.5, 1.0, 1.5, 2.0, 3.0, 4.0, 6.0, -0.0, -0.5, -1.0, -1.5, -2.0, -3.0, -4.0, -6.0])


def pack_weight(w, fmt):
    k, n = w.shape
    w = f64(np.asarray(w, np.float32).astype(ml_dtypes.bfloat16)).reshape(k // 32, 32, n)
    amax = np.abs(w).max(1)
    if fmt == "e4m3":
        byte = np.frexp(amax)[1] - 1 + 127 - 7
    else:
        mant, ex = np.frexp(amax / 6.0)
        byte = np.where(mant > 0.5, ex, ex - 1) + 127
    byte = np.clip(np.where(amax > 0, byte, 1), 1, 254)
    scaled = (w * np.exp2(127.0 - byte)[:, None, :]).reshape(k, n).astype(np.float32)
    by_word = np.ascontiguousarray(scaled.reshape(k // 512, 128, 4, n).transpose(0, 1, 3, 2))
    if fmt == "e4m3":
        words = by_word.astype(ml_dtypes.float8_e4m3fn).view(np.uint8)
    else:
        c = by_word.astype(ml_dtypes.float4_e2m1fn).view(np.uint8) & 0xF
        words = (c[..., 0::2] | (c[..., 1::2] << 4)).reshape(k // 512, 128, 2 * n)
    return np.ascontiguousarray(words), np.ascontiguousarray(byte.astype(np.uint8).reshape(k // 512, 16, n))


def unpack_weight(words, scales, fmt):
    g, _, n = scales.shape
    words = np.ascontiguousarray(words).reshape(g, 128, n, -1)
    if fmt == "e4m3":
        vals = words.view(ml_dtypes.float8_e4m3fn).astype(np.float64)
    else:
        nib = np.empty((g, 128, n, 4), np.uint8)
        nib[..., 0::2] = words & 0xF
        nib[..., 1::2] = words >> 4
        vals = E2M1[nib]
    vals = vals * np.repeat(np.exp2(scales.astype(np.float64) - 127.0), 8, axis=1)[..., None]
    return vals.transpose(0, 1, 3, 2).reshape(g * 512, n)


def gelu(v):
    return 0.5 * v * (1.0 + np.tanh(np.sqrt(2.0 / np.pi) * (v + 0.044715 * v**3)))


K, T, S, M, N = 1024, 2048, 1024, 1024, 512

def setup_inputs():
    n = np.random.standard_normal
    s = mx_kscale(K)[:, None]
    u = mx_kscale(S)
    idx = np.random.permutation(T)[:S]
    v = 0.7 * n((K, T)) / np.sqrt(K) * s
    tab_words, tab_scales = pack_weight(v, "e4m3")
    w4_words, w4_scales = pack_weight(n((K, N)) / np.sqrt(K) * s, "e2m1")
    x = n((K, M)) / s
    g = np.exp(0.3 * n((S,))) * u
    wdT = 0.5 * n((N, T)) / np.sqrt(S)
    wdT[:, idx] /= u
    return {"tab_words": tab_words, "tab_scales": tab_scales,
            "offs": striped(idx), "x": x.astype(np.float32),
            "g": g.astype(np.float32), "wdT": wdT.astype(np.float32),
            "w4_words": w4_words, "w4_scales": w4_scales}

def reference(tab_words, tab_scales, offs, x, g, wdT, w4_words, w4_scales):
    v = unpack_weight(tab_words, tab_scales, "e4m3")[:, unstriped(offs)]
    w4 = unpack_weight(w4_words, w4_scales, "e2m1")
    wd = f64(wdT)[:, unstriped(offs)]
    xq = mxq(f64(x), 0, "e4m3")
    z = v.T @ xq
    m = np.maximum(1.0 - z, 0.0)
    h = np.square(m) * f64(g)[:, None]
    return mxq(wd, 1, "e4m3") @ mxq(h, 0, "e4m3") + w4.T @ xq

@@ -1,0 +1,432 @@
+from contextlib import ExitStack
+
+import concourse.mybir as mybir
+from concourse.masks import make_identity
+
+K, T, S, M, N = 1024, 2048, 1024, 1024, 512
+FLOPS = 2 * M * (K * S + S * N + K * N)
+
+F32 = mybir.dt.float32
+BF16 = mybir.dt.bfloat16
+I32 = mybir.dt.int32
+U32 = mybir.dt.uint32
+U16 = mybir.dt.uint16
+U8 = mybir.dt.uint8
+FP8X4 = mybir.dt.float8_e4m3fn_x4
+FP4X4 = mybir.dt.float4_e2m1fn_x4
+ALU = mybir.AluOpType
+ACT = mybir.ActivationFunctionType
+
+P = 128
+PACK = 4
+PASS = P * PACK
+KP = K // PASS
+JP = S // PASS
+NT = N // P
+HALF = 512
+CHUNKS = [(0, 256), (256, 256), (512, 512)]
+TINY = 2.0 ** -100
+
+
+def interleaved(dst, src):
+    return (
+        dst.rearrange("p (c k) t -> p c t k", k=4),
+        src.rearrange("p t (c k) -> p c t k", k=4),
+    )
+
+
+def tile_list_cardinality_margin_corrections_kernel(
+    tc, tab_words, tab_scales, offs, x, g, wdT, w4_words, w4_scales, out
+):
+    nc = tc.nc
+    with ExitStack() as ctx:
+        keep = ctx.enter_context(tc.tile_pool(name="keep", bufs=1))
+        psum = ctx.enter_context(tc.psum_pool(name="psum", bufs=1))
+
+        def bank(i):
+            return psum.tile([P, HALF], F32, name="bank%d" % i)
+
+        offsets = keep.tile([P, S // 16], U16, name="offsets")
+        gain = keep.tile([P, JP, PACK], F32, name="gain")
+        tsc = keep.tile([P, T], U8, name="tsc", align_bytes=64)
+        w4s = keep.tile([P, KP, N], U8, name="w4s", align_bytes=64)
+        w4w = keep.tile([P, KP, 2 * N], U8, name="w4w", align_bytes=64)
+        tab = [keep.tile([P, T], I32, name="tab%d" % a, align_bytes=64) for a in range(KP)]
+        wd = [keep.tile([P, T], F32, name="wd%d" % n, align_bytes=64) for n in range(NT)]
+        xraw = {}
+        for c, (m0, w) in enumerate(CHUNKS):
+            for a in range(KP):
+                xraw[c, a] = keep.tile([P, PACK, w], F32, name="xraw%d_%d" % (c, a), align_bytes=64)
+        ident = keep.tile([P, P], F32, name="ident")
+
+        nc.vector.memset(tsc[:].bitcast(I32), 0)
+        nc.vector.memset(w4s[:].bitcast(I32), 0)
+        make_identity(nc, ident[:])
+
+        def load_tab(a):
+            nc.sync.dma_start(tab[a][:], tab_words[a].rearrange("p t i -> p (t i)").bitcast(I32))
+
+        def load_x(c, a):
+            m0, w = CHUNKS[c]
+            rows = x[a * PASS : (a + 1) * PASS, m0 : m0 + w]
+            nc.sync.dma_start(xraw[c, a][:], rows.rearrange("(p i) m -> p i m", i=PACK))
+
+        def load_wd(n):
+            nc.sync.dma_start(wd[n][:], wdT[n * P : (n + 1) * P, :])
+
+        def load_w4():
+            for q in range(4):
+                nc.sync.dma_start(
+                    w4s[32 * q : 32 * q + 4, :, :].bitcast(I32),
+                    w4_scales[:, 4 * q : 4 * q + 4, :].rearrange("a r c -> r a c").bitcast(I32),
+                )
+            nc.sync.dma_start(w4w[:].bitcast(I32), w4_words.rearrange("a p c -> p a c").bitcast(I32))
+
+        def load_small():
+            nc.sync.dma_start(offsets[:], offs)
+            nc.sync.dma_start(gain[:], g.rearrange("(b p t) -> p b t", b=JP, t=PACK))
+            for q in range(4):
+                nc.sync.dma_start(
+                    tsc[32 * q : 32 * q + 4 * KP, :].bitcast(I32),
+                    tab_scales[:, 4 * q : 4 * q + 4, :].bitcast(I32),
+                )
+
+        load_small()
+        load_tab(0)
+        load_x(1, 1)
+        load_tab(1)
+        load_x(1, 0)
+        load_x(2, 0)
+        load_x(2, 1)
+        load_wd(0)
+        load_x(0, 0)
+        load_wd(3)
+        load_x(0, 1)
+        load_w4()
+        load_wd(2)
+        load_wd(1)
+
+        mag = keep.tile([P, JP, PACK], F32, name="mag")
+        root0 = keep.tile([P, JP, PACK], F32, name="root0")
+        inv = keep.tile([P, JP, PACK], F32, name="inv")
+        corr = keep.tile([P, JP, PACK], F32, name="corr")
+        root = keep.tile([P, JP, PACK], F32, name="root")
+        nroot = keep.tile([P, JP, PACK], F32, name="nroot")
+        sg0 = keep.tile([P, JP, PACK], F32, name="sg0")
+        sign = keep.tile([P, JP, PACK], BF16, name="sign")
+
+        def gains():
+            nc.vector.scalar_tensor_tensor(mag[:], gain[:], -1.0, gain[:], ALU.mult, ALU.max)
+            nc.scalar.activation(root0[:], mag[:], ACT.Sqrt, bias=TINY)
+            nc.gpsimd.tensor_scalar(sg0[:], gain[:], 0.0, 2.0, ALU.is_ge, ALU.mult)
+            nc.gpsimd.tensor_scalar(sign[:], sg0[:], 1.0, -1.0, ALU.mult, ALU.add)
+
+        def gains2():
+            nc.vector.reciprocal(inv[:], root0[:])
+            nc.vector.scalar_tensor_tensor(corr[:], mag[:], 0.5, inv[:], ALU.mult, ALU.mult)
+            nc.vector.scalar_tensor_tensor(root[:], root0[:], 0.5, corr[:], ALU.mult, ALU.add)
+            nc.scalar.activation(nroot[:], root[:], ACT.Copy, scale=-1.0)
+
+        tsg = keep.tile([P, S], U8, name="tsg", align_bytes=64)
+        tsp = keep.tile([P, JP, PACK, P], U8, name="tsp", align_bytes=64)
+
+        def gather_scales():
+            nc.vector.tensor_copy(tsg[:], tsc[:].indirect(offsets[:]))
+
+        def perm_scales():
+            nc.vector.tensor_copy(tsp[:], tsg[:].rearrange("p (b i t) -> p b t i", b=JP, t=PACK))
+
+        def piece(b):
+            return offsets[:, b * PASS // 16 : (b + 1) * PASS // 16]
+
+        tg = {}
+
+        def gather_tab(a, b):
+            tg[a, b] = keep.tile([P, PACK, P], U32, name="tg%d_%d" % (a, b), align_bytes=64)
+            nc.vector.tensor_copy(
+                tg[a, b][:].rearrange("p t i -> p i t"), tab[a][:].bitcast(U32).indirect(piece(b))
+            )
+
+        xq = [keep.tile([P, M], U32, name="xq%d" % a, align_bytes=64) for a in range(KP)]
+        xs = [keep.tile([P, M], U8, name="xs%d" % a, align_bytes=64) for a in range(KP)]
+        hq = [keep.tile([P, M], U32, name="hq%d" % b, align_bytes=64) for b in range(JP)]
+        hs = [keep.tile([P, M], U8, name="hs%d" % b, align_bytes=64) for b in range(JP)]
+        wq = [keep.tile([P, JP, P], U32, name="wq%d" % n, align_bytes=64) for n in range(NT)]
+        ws = [keep.tile([P, JP, P], U8, name="ws%d" % n, align_bytes=64) for n in range(NT)]
+        xb = {}
+
+        def cast_x(c, a, eng):
+            m0, w = CHUNKS[c]
+            xb[c, a] = keep.tile([P, w, PACK], BF16, name="xb%d_%d" % (c, a), align_bytes=64)
+            dst, src = interleaved(xb[c, a][:], xraw[c, a][:])
+            if eng == "s":
+                nc.scalar.copy(dst, src)
+            elif eng == "v":
+                nc.vector.tensor_copy(dst, src)
+            else:
+                nc.gpsimd.tensor_scalar(
+                    xb[c, a][:], xraw[c, a][:].rearrange("p t m -> p m t"), 1.0, 0.0, ALU.mult, ALU.add
+                )
+
+        def quant_x(c, a):
+            m0, w = CHUNKS[c]
+            nc.vector.quantize_mx(
+                xq[a][:, m0 : m0 + w].bitcast(FP8X4),
+                xs[a][:, m0 : m0 + w],
+                xb[c, a][:].rearrange("p m t -> p (m t)"),
+            )
+
+        act = {}
+        hb = {}
+        zb = {}
+        for c, (m0, w) in enumerate(CHUNKS):
+            for b in range(JP):
+                act[c, b] = keep.tile([P, PACK, w], F32, name="act%d_%d" % (c, b), align_bytes=64)
+                hb[c, b] = keep.tile([P, w, PACK], BF16, name="hb%d_%d" % (c, b), align_bytes=64)
+
+        def score(c, b, t0, bk):
+            m0, w = CHUNKS[c]
+            zb[c, b, t0] = bank(bk)
+            for u in range(HALF // w):
+                for a in range(KP):
+                    nc.tensor.matmul_mx(
+                        out=zb[c, b, t0][:, u * w : (u + 1) * w],
+                        lhsT=tg[a, b][:, t0 + u, :].bitcast(FP8X4),
+                        lhsT_scale=tsp[4 * a : P, b, t0 + u, :],
+                        rhs=xq[a][:, m0 : m0 + w].bitcast(FP8X4),
+                        rhs_scale=xs[a][:, m0 : m0 + w],
+                        start=(a == 0),
+                        stop=(a == KP - 1),
+                    )
+
+        def hinge(c, b, t0):
+            m0, w = CHUNKS[c]
+            for u in range(HALF // w):
+                t = t0 + u
+                nc.scalar.activation(
+                    act[c, b][:, t, :],
+                    zb[c, b, t0][:, u * w : (u + 1) * w],
+                    ACT.Relu,
+                    bias=root[:, b, t : t + 1],
+                    scale=nroot[:, b, t : t + 1],
+                )
+
+        def square(c, b, part, eng):
+            w = CHUNKS[c][1] // 2
+            cols = slice(part * w, (part + 1) * w)
+            dst, src = interleaved(hb[c, b][:, cols, :], act[c, b][:, :, cols])
+            if eng == "s":
+                nc.scalar.activation(dst, src, ACT.Square)
+            else:
+                nc.vector.tensor_tensor(dst, src, src, ALU.mult)
+
+        def quant_h(c, b):
+            m0, w = CHUNKS[c]
+            nc.vector.quantize_mx(
+                hq[b][:, m0 : m0 + w].bitcast(FP8X4),
+                hs[b][:, m0 : m0 + w],
+                hb[c, b][:].rearrange("p m t -> p (m t)"),
+            )
+
+        wg = {}
+        wt = {}
+        wb = [keep.tile([P, JP, P, PACK], BF16, name="wb%d" % n, align_bytes=64) for n in range(NT)]
+
+        def gather_wd(n, b):
+            wg[n, b] = keep.tile([P, 2, P, 2], BF16, name="wg%d_%d" % (n, b), align_bytes=64)
+            nc.vector.tensor_copy(wg[n, b][:].rearrange("p u i e -> p i u e"), wd[n][:].indirect(piece(b)))
+
+        def turn_wd(n, b, bk):
+            wt[n, b] = bank(bk)
+            words = wg[n, b][:].rearrange("p u i e -> p (u i e)").bitcast(F32)
+            for u in range(2):
+                nc.tensor.transpose(wt[n, b][:, u * P : (u + 1) * P], words[:, u * P : (u + 1) * P], ident[:])
+
+        def sign_wd(n, b):
+            nc.vector.tensor_tensor(
+                wb[n][:, b, :, :].rearrange("p c (u e) -> p c u e", u=2),
+                wt[n, b][:, 0 : 2 * P].bitcast(BF16).rearrange("p (u c e) -> p c u e", u=2, e=2),
+                sign[:, b : b + 1, :].rearrange("p o (u e) -> p o u e", u=2).to_broadcast([P, P, 2, 2]),
+                ALU.mult,
+            )
+
+        def quant_wd(n):
+            nc.vector.quantize_mx(
+                wq[n][:].rearrange("p b c -> p (b c)").bitcast(FP8X4),
+                ws[n][:].rearrange("p b c -> p (b c)"),
+                wb[n][:].rearrange("p b c t -> p (b c t)"),
+            )
+
+        acc = {}
+
+        def base(n, h, bk):
+            cols = slice(h * HALF, (h + 1) * HALF)
+            acc[n, h] = bank(bk)
+            for a in range(KP):
+                nc.tensor.matmul_mx(
+                    out=acc[n, h][:],
+                    lhsT=w4w[:, a, 2 * n * P : 2 * (n + 1) * P].bitcast(FP4X4),
+                    lhsT_scale=w4s[:, a, n * P : (n + 1) * P],
+                    rhs=xq[a][:, cols].bitcast(FP8X4),
+                    rhs_scale=xs[a][:, cols],
+                    start=(a == 0),
+                    stop=False,
+                )
+
+        def down(n, h, b):
+            cols = slice(h * HALF, (h + 1) * HALF)
+            nc.tensor.matmul_mx(
+                out=acc[n, h][:],
+                lhsT=wq[n][:, b, :].bitcast(FP8X4),
+                lhsT_scale=ws[n][:, b, :],
+                rhs=hq[b][:, cols].bitcast(FP8X4),
+                rhs_scale=hs[b][:, cols],
+                start=False,
+                stop=(b == JP - 1),
+            )
+
+        def store(n, h, eng):
+            cols = slice(h * HALF, (h + 1) * HALF)
+            res = keep.tile([P, HALF], F32, name="res%d_%d" % (n, h))
+            if eng == "s":
+                nc.scalar.copy(res[:], acc[n, h][:])
+            else:
+                nc.vector.tensor_copy(res[:], acc[n, h][:])
+            nc.sync.dma_start(out[n * P : (n + 1) * P, cols], res[:])
+
+        def whole(n, h, bk, eng):
+            base(n, h, bk)
+            down(n, h, 0)
+            down(n, h, 1)
+            store(n, h, eng)
+
+        gains()
+        gather_scales()
+        gather_tab(0, 0)
+        cast_x(1, 1, "s")
+        perm_scales()
+        gather_tab(0, 1)
+        quant_x(1, 1)
+        gather_tab(1, 0)
+        gather_tab(1, 1)
+        cast_x(1, 0, "s")
+        quant_x(1, 0)
+        gains2()
+        score(1, 1, 2, 2)
+        cast_x(2, 0, "v")
+        quant_x(2, 0)
+        score(1, 1, 0, 6)
+        hinge(1, 1, 2)
+        hinge(1, 1, 0)
+        score(1, 0, 2, 7)
+        hinge(1, 0, 2)
+        score(1, 0, 0, 4)
+        hinge(1, 0, 0)
+        cast_x(2, 1, "v")
+        square(1, 1, 1, "s")
+        square(1, 0, 0, "s")
+        quant_x(2, 1)
+        score(2, 0, 1, 2)
+        square(1, 0, 1, "s")
+        score(2, 1, 0, 5)
+        score(2, 0, 3, 6)
+        score(2, 0, 2, 7)
+        hinge(2, 0, 1)
+        score(2, 0, 0, 1)
+        hinge(2, 1, 0)
+        score(2, 1, 2, 0)
+        hinge(2, 0, 3)
+        gather_wd(0, 0)
+        cast_x(0, 0, "v")
+        gather_wd(0, 1)
+        quant_x(0, 0)
+        turn_wd(0, 1, 3)
+        score(2, 1, 1, 2)
+        hinge(2, 0, 2)
+        gather_wd(3, 0)
+        hinge(2, 0, 0)
+        hinge(2, 1, 2)
+        quant_h(1, 0)
+        square(2, 0, 0, "s")
+        score(2, 1, 3, 1)
+        cast_x(0, 1, "v")
+        square(2, 0, 1, "s")
+        turn_wd(3, 0, 6)
+        sign_wd(3, 0)
+        hinge(2, 1, 3)
+        base(1, 1, 4)
+        hinge(2, 1, 1)
+        quant_x(0, 1)
+        score(0, 1, 0, 7)
+        sign_wd(0, 1)
+        gather_wd(3, 1)
+        score(0, 0, 2, 5)
+        score(0, 1, 2, 2)
+        gather_wd(2, 0)
+        square(1, 1, 0, "s")
+        hinge(0, 0, 2)
+        hinge(0, 1, 2)
+        hinge(0, 1, 0)
+        quant_h(2, 0)
+        turn_wd(3, 1, 0)
+        turn_wd(2, 0, 5)
+        score(0, 0, 0, 1)
+        sign_wd(2, 0)
+        square(2, 1, 0, "s")
+        hinge(0, 0, 0)
+        turn_wd(0, 0, 6)
+        base(3, 0, 5)
+        square(2, 1, 1, "s")
+        gather_wd(1, 0)
+        square(0, 0, 1, "s")
+        base(0, 1, 3)
+        square(0, 0, 0, "s")
+        sign_wd(0, 0)
+        sign_wd(3, 1)
+        base(3, 1, 6)
+        base(0, 0, 1)
+        gather_wd(1, 1)
+        quant_wd(3)
+        turn_wd(1, 0, 2)
+        quant_wd(0)
+        base(2, 0, 7)
+        quant_h(1, 1)
+        sign_wd(1, 0)
+        base(2, 1, 0)
+        down(3, 1, 0)
+        down(0, 1, 0)
+        quant_h(2, 1)
+        turn_wd(1, 1, 2)
+        quant_h(0, 0)
+        down(0, 1, 1)
+        square(0, 1, 0, "s")
+        down(0, 0, 0)
+        down(3, 0, 0)
+        sign_wd(1, 1)
+        square(0, 1, 1, "s")
+        quant_h(0, 1)
+        gather_wd(2, 1)
+        store(0, 1, "s")
+        down(3, 1, 1)
+        down(0, 0, 1)
+        down(3, 0, 1)
+        store(3, 1, "s")
+        base(1, 0, 2)
+        turn_wd(2, 1, 3)
+        quant_wd(1)
+        sign_wd(2, 1)
+        store(3, 0, "s")
+        quant_wd(2)
+        store(0, 0, "s")
+        down(1, 1, 0)
+        down(1, 1, 1)
+        down(1, 0, 0)
+        store(1, 1, "s")
+        down(1, 0, 1)
+        down(2, 0, 0)
+        down(2, 0, 1)
+        store(1, 0, "v")
+        store(2, 0, "s")
+        down(2, 1, 0)
+        down(2, 1, 1)
+        store(2, 1, "v")

@@ -26,6 +26,7 @@ NT = N // P
 HALF = 512
 CHUNKS = [(0, 256), (256, 256), (512, 512)]
 TINY = 2.0 ** -100
+SLOT = {"act10": "xr01"}
 
 
 def interleaved(dst, src):
@@ -46,105 +47,114 @@ def tile_list_cardinality_margin_corrections_kernel(
         def bank(i):
             return psum.tile([P, HALF], F32, name="bank%d" % i)
 
+        def slot(name, shape, dtype):
+            return keep.tile(shape, dtype, name=name, tag=SLOT.get(name, name), align_bytes=64)
+
         offsets = keep.tile([P, S // 16], U16, name="offsets")
         gain = keep.tile([P, JP, PACK], F32, name="gain")
         tsc = keep.tile([P, T], U8, name="tsc", align_bytes=64)
         w4s = keep.tile([P, KP, N], U8, name="w4s", align_bytes=64)
         w4w = keep.tile([P, KP, 2 * N], U8, name="w4w", align_bytes=64)
-        tab = [keep.tile([P, T], I32, name="tab%d" % a, align_bytes=64) for a in range(KP)]
-        wd = [keep.tile([P, T], F32, name="wd%d" % n, align_bytes=64) for n in range(NT)]
+        tab = {}
+        wd = {}
         xraw = {}
-        for c, (m0, w) in enumerate(CHUNKS):
-            for a in range(KP):
-                xraw[c, a] = keep.tile([P, PACK, w], F32, name="xraw%d_%d" % (c, a), align_bytes=64)
         ident = keep.tile([P, P], F32, name="ident")
 
-        nc.vector.memset(tsc[:].bitcast(I32), 0)
-        nc.vector.memset(w4s[:].bitcast(I32), 0)
         make_identity(nc, ident[:])
 
+        def zero():
+            nc.vector.memset(tsc[:].bitcast(I32), 0)
+            nc.vector.memset(w4s[:].bitcast(I32), 0)
+
         def load_tab(a):
+            tab[a] = slot("tab%d" % a, [P, T], I32)
             nc.sync.dma_start(tab[a][:], tab_words[a].rearrange("p t i -> p (t i)").bitcast(I32))
 
         def load_x(c, a):
             m0, w = CHUNKS[c]
+            xraw[c, a] = slot("xr%d%d" % (c, a), [P, PACK, w], F32)
             rows = x[a * PASS : (a + 1) * PASS, m0 : m0 + w]
             nc.sync.dma_start(xraw[c, a][:], rows.rearrange("(p i) m -> p i m", i=PACK))
 
         def load_wd(n):
+            wd[n] = slot("wd%d" % n, [P, T], F32)
             nc.sync.dma_start(wd[n][:], wdT[n * P : (n + 1) * P, :])
 
-        def load_w4():
+        def load_w4s():
             for q in range(4):
                 nc.sync.dma_start(
                     w4s[32 * q : 32 * q + 4, :, :].bitcast(I32),
                     w4_scales[:, 4 * q : 4 * q + 4, :].rearrange("a r c -> r a c").bitcast(I32),
                 )
+
+        def load_w4w():
             nc.sync.dma_start(w4w[:].bitcast(I32), w4_words.rearrange("a p c -> p a c").bitcast(I32))
 
-        def load_small():
+        def load_offs():
             nc.sync.dma_start(offsets[:], offs)
+
+        def load_g():
             nc.sync.dma_start(gain[:], g.rearrange("(b p t) -> p b t", b=JP, t=PACK))
+
+        def load_tsc():
             for q in range(4):
                 nc.sync.dma_start(
                     tsc[32 * q : 32 * q + 4 * KP, :].bitcast(I32),
                     tab_scales[:, 4 * q : 4 * q + 4, :].bitcast(I32),
                 )
 
-        load_small()
-        load_tab(0)
-        load_x(1, 1)
-        load_tab(1)
-        load_x(1, 0)
-        load_x(2, 0)
-        load_x(2, 1)
-        load_wd(0)
-        load_x(0, 0)
-        load_wd(3)
-        load_x(0, 1)
-        load_w4()
-        load_wd(2)
-        load_wd(1)
 
-        mag = keep.tile([P, JP, PACK], F32, name="mag")
-        root0 = keep.tile([P, JP, PACK], F32, name="root0")
-        inv = keep.tile([P, JP, PACK], F32, name="inv")
-        corr = keep.tile([P, JP, PACK], F32, name="corr")
-        root = keep.tile([P, JP, PACK], F32, name="root")
-        nroot = keep.tile([P, JP, PACK], F32, name="nroot")
-        sg0 = keep.tile([P, JP, PACK], F32, name="sg0")
-        sign = keep.tile([P, JP, PACK], BF16, name="sign")
+        def small(name, dtype=F32):
+            return keep.tile([P, JP * PACK], dtype, name=name)
+
+        root = small("root")
+        nroot = small("nroot")
+        sign = small("sign", BF16)
 
         def gains():
-            nc.vector.scalar_tensor_tensor(mag[:], gain[:], -1.0, gain[:], ALU.mult, ALU.max)
-            nc.scalar.activation(root0[:], mag[:], ACT.Sqrt, bias=TINY)
-            nc.gpsimd.tensor_scalar(sg0[:], gain[:], 0.0, 2.0, ALU.is_ge, ALU.mult)
-            nc.gpsimd.tensor_scalar(sign[:], sg0[:], 1.0, -1.0, ALU.mult, ALU.add)
-
-        def gains2():
-            nc.vector.reciprocal(inv[:], root0[:])
-            nc.vector.scalar_tensor_tensor(corr[:], mag[:], 0.5, inv[:], ALU.mult, ALU.mult)
-            nc.vector.scalar_tensor_tensor(root[:], root0[:], 0.5, corr[:], ALU.mult, ALU.add)
-            nc.scalar.activation(nroot[:], root[:], ACT.Copy, scale=-1.0)
+            gv = gain[:].rearrange("p b t -> p (b t)")
+            step, sgn, mag, safe, power = small("step"), small("sgn"), small("mag"), small("safe"), small("power")
+            y0, y2, res, fix, y1 = small("y0"), small("y2"), small("res"), small("fix"), small("y1")
+            nc.gpsimd.memset(power[:], -0.5)
+            nc.gpsimd.tensor_scalar(step[:], gv, 0.0, 2.0, ALU.is_ge, ALU.mult)
+            nc.gpsimd.tensor_scalar(sgn[:], step[:], 1.0, -1.0, ALU.mult, ALU.add)
+            nc.gpsimd.tensor_tensor(mag[:], gv, sgn[:], ALU.mult)
+            nc.gpsimd.tensor_scalar(safe[:], mag[:], 1.0, TINY, ALU.mult, ALU.add)
+            nc.gpsimd.tensor_tensor(y0[:], safe[:], power[:], ALU.pow)
+            nc.gpsimd.tensor_tensor(y2[:], y0[:], safe[:], ALU.mult)
+            nc.gpsimd.tensor_tensor(res[:], y2[:], y0[:], ALU.mult)
+            nc.gpsimd.tensor_scalar(fix[:], res[:], -0.5, 1.5, ALU.mult, ALU.add)
+            nc.gpsimd.tensor_tensor(y1[:], y0[:], fix[:], ALU.mult)
+            nc.gpsimd.tensor_tensor(root[:], mag[:], y1[:], ALU.mult)
+            nc.gpsimd.tensor_scalar(nroot[:], root[:], -1.0, 0.0, ALU.mult, ALU.add)
+            nc.gpsimd.tensor_copy(sign[:], sgn[:])
 
         tsg = keep.tile([P, S], U8, name="tsg", align_bytes=64)
         tsp = keep.tile([P, JP, PACK, P], U8, name="tsp", align_bytes=64)
 
-        def gather_scales():
-            nc.vector.tensor_copy(tsg[:], tsc[:].indirect(offsets[:]))
+        def gather_scales(b):
+            nc.vector.tensor_copy(tsg[:, span(b, PASS)], tsc[:].indirect(offsets[:, span(b, PASS // 16)]))
 
-        def perm_scales():
-            nc.vector.tensor_copy(tsp[:], tsg[:].rearrange("p (b i t) -> p b t i", b=JP, t=PACK))
+        def perm_scales(b):
+            nc.vector.tensor_copy(
+                tsp[:, span(b, 1), :, :], tsg[:, span(b, PASS)].rearrange("p (b i t) -> p b t i", i=P, t=PACK)
+            )
 
-        def piece(b):
-            return offsets[:, b * PASS // 16 : (b + 1) * PASS // 16]
+        def span(b, width):
+            return slice(0, JP * width) if b == JP else slice(b * width, (b + 1) * width)
 
-        tg = {}
+        tp = [keep.tile([P, S], U32, name="tp%d" % a, align_bytes=64) for a in range(KP)]
+        tg = [keep.tile([P, JP, PACK, P], U32, name="tg%d" % a, align_bytes=64) for a in range(KP)]
 
         def gather_tab(a, b):
-            tg[a, b] = keep.tile([P, PACK, P], U32, name="tg%d_%d" % (a, b), align_bytes=64)
             nc.vector.tensor_copy(
-                tg[a, b][:].rearrange("p t i -> p i t"), tab[a][:].bitcast(U32).indirect(piece(b))
+                tp[a][:, span(b, PASS)], tab[a][:].bitcast(U32).indirect(offsets[:, span(b, PASS // 16)])
+            )
+
+        def perm_tab(a, b):
+            nc.vector.tensor_copy(
+                tg[a][:, span(b, 1), :, :].bitcast(I32).rearrange("p b t (c k) -> p b c t k", k=4),
+                tp[a][:, span(b, PASS)].bitcast(I32).rearrange("p (b c k t) -> p b c t k", c=P // 4, k=4, t=PACK),
             )
 
         xq = [keep.tile([P, M], U32, name="xq%d" % a, align_bytes=64) for a in range(KP)]
@@ -157,7 +167,7 @@ def tile_list_cardinality_margin_corrections_kernel(
 
         def cast_x(c, a, eng):
             m0, w = CHUNKS[c]
-            xb[c, a] = keep.tile([P, w, PACK], BF16, name="xb%d_%d" % (c, a), align_bytes=64)
+            xb[c, a] = slot("xb%d%d" % (c, a), [P, w, PACK], BF16)
             dst, src = interleaved(xb[c, a][:], xraw[c, a][:])
             if eng == "s":
                 nc.scalar.copy(dst, src)
@@ -179,10 +189,6 @@ def tile_list_cardinality_margin_corrections_kernel(
         act = {}
         hb = {}
         zb = {}
-        for c, (m0, w) in enumerate(CHUNKS):
-            for b in range(JP):
-                act[c, b] = keep.tile([P, PACK, w], F32, name="act%d_%d" % (c, b), align_bytes=64)
-                hb[c, b] = keep.tile([P, w, PACK], BF16, name="hb%d_%d" % (c, b), align_bytes=64)
 
         def score(c, b, t0, bk):
             m0, w = CHUNKS[c]
@@ -191,7 +197,7 @@ def tile_list_cardinality_margin_corrections_kernel(
                 for a in range(KP):
                     nc.tensor.matmul_mx(
                         out=zb[c, b, t0][:, u * w : (u + 1) * w],
-                        lhsT=tg[a, b][:, t0 + u, :].bitcast(FP8X4),
+                        lhsT=tg[a][:, b, t0 + u, :].bitcast(FP8X4),
                         lhsT_scale=tsp[4 * a : P, b, t0 + u, :],
                         rhs=xq[a][:, m0 : m0 + w].bitcast(FP8X4),
                         rhs_scale=xs[a][:, m0 : m0 + w],
@@ -201,18 +207,22 @@ def tile_list_cardinality_margin_corrections_kernel(
 
         def hinge(c, b, t0):
             m0, w = CHUNKS[c]
+            if (c, b) not in act:
+                act[c, b] = slot("act%d%d" % (c, b), [P, PACK, w], F32)
             for u in range(HALF // w):
                 t = t0 + u
                 nc.scalar.activation(
                     act[c, b][:, t, :],
                     zb[c, b, t0][:, u * w : (u + 1) * w],
                     ACT.Relu,
-                    bias=root[:, b, t : t + 1],
-                    scale=nroot[:, b, t : t + 1],
+                    bias=root[:, b * PACK + t : b * PACK + t + 1],
+                    scale=nroot[:, b * PACK + t : b * PACK + t + 1],
                 )
 
         def square(c, b, part, eng):
             w = CHUNKS[c][1] // 2
+            if (c, b) not in hb:
+                hb[c, b] = slot("hb%d%d" % (c, b), [P, 2 * w, PACK], BF16)
             cols = slice(part * w, (part + 1) * w)
             dst, src = interleaved(hb[c, b][:, cols, :], act[c, b][:, :, cols])
             if eng == "s":
@@ -230,23 +240,26 @@ def tile_list_cardinality_margin_corrections_kernel(
 
         wg = {}
         wt = {}
-        wb = [keep.tile([P, JP, P, PACK], BF16, name="wb%d" % n, align_bytes=64) for n in range(NT)]
+        wb = {}
 
-        def gather_wd(n, b):
-            wg[n, b] = keep.tile([P, 2, P, 2], BF16, name="wg%d_%d" % (n, b), align_bytes=64)
-            nc.vector.tensor_copy(wg[n, b][:].rearrange("p u i e -> p i u e"), wd[n][:].indirect(piece(b)))
+        def gather_wd(n):
+            wg[n] = slot("wg%d" % n, [P, JP, PASS + 32], BF16)
+            nc.vector.tensor_copy(wg[n][:, :, 0:PASS], wd[n][:].indirect(offsets[:]))
 
-        def turn_wd(n, b, bk):
-            wt[n, b] = bank(bk)
-            words = wg[n, b][:].rearrange("p u i e -> p (u i e)").bitcast(F32)
-            for u in range(2):
-                nc.tensor.transpose(wt[n, b][:, u * P : (u + 1) * P], words[:, u * P : (u + 1) * P], ident[:])
+        def turn_wd(n, bk):
+            wt[n] = bank(bk)
+            for b in range(JP):
+                words = wg[n][:, b, 0:PASS].bitcast(F32)
+                for u in range(2):
+                    at = (u * JP + b) * P
+                    nc.tensor.transpose(wt[n][:, at : at + P], words[:, u : 2 * P : 2], ident[:])
 
-        def sign_wd(n, b):
+        def sign_wd(n):
+            wb[n] = slot("wb%d" % n, [P, JP, P, PACK], BF16)
             nc.vector.tensor_tensor(
-                wb[n][:, b, :, :].rearrange("p c (u e) -> p c u e", u=2),
-                wt[n, b][:, 0 : 2 * P].bitcast(BF16).rearrange("p (u c e) -> p c u e", u=2, e=2),
-                sign[:, b : b + 1, :].rearrange("p o (u e) -> p o u e", u=2).to_broadcast([P, P, 2, 2]),
+                wb[n][:].rearrange("p b c (u e) -> p b c u e", u=2),
+                wt[n][:].bitcast(BF16).rearrange("p (u b c e) -> p b c u e", u=2, b=JP, e=2),
+                sign[:].rearrange("p (b o u e) -> p b o u e", b=JP, o=1, u=2).to_broadcast([P, JP, P, 2, 2]),
                 ALU.mult,
             )
 
@@ -287,146 +300,151 @@ def tile_list_cardinality_margin_corrections_kernel(
 
         def store(n, h, eng):
             cols = slice(h * HALF, (h + 1) * HALF)
-            res = keep.tile([P, HALF], F32, name="res%d_%d" % (n, h))
+            res = slot("res%d%d" % (n, h), [P, HALF], F32)
             if eng == "s":
                 nc.scalar.copy(res[:], acc[n, h][:])
             else:
                 nc.vector.tensor_copy(res[:], acc[n, h][:])
             nc.sync.dma_start(out[n * P : (n + 1) * P, cols], res[:])
 
-        def whole(n, h, bk, eng):
-            base(n, h, bk)
-            down(n, h, 0)
-            down(n, h, 1)
-            store(n, h, eng)
-
-        gains()
-        gather_scales()
-        gather_tab(0, 0)
-        cast_x(1, 1, "s")
-        perm_scales()
-        gather_tab(0, 1)
-        quant_x(1, 1)
+        zero()
+        load_x(1, 0)
+        load_tsc()
+        load_offs()
+        load_tab(0)
+        load_x(2, 0)
+        load_x(1, 1)
+        load_g()
+        load_tab(1)
+        load_x(0, 0)
+        cast_x(2, 0, "s")
         gather_tab(1, 0)
+        gather_scales(0)
+        cast_x(0, 0, "s")
+        cast_x(1, 0, "v")
+        load_w4s()
+        load_x(2, 1)
+        gather_tab(0, 0)
+        perm_scales(0)
+        perm_tab(0, 0)
+        load_x(0, 1)
         gather_tab(1, 1)
-        cast_x(1, 0, "s")
+        load_wd(1)
         quant_x(1, 0)
-        gains2()
-        score(1, 1, 2, 2)
-        cast_x(2, 0, "v")
-        quant_x(2, 0)
-        score(1, 1, 0, 6)
-        hinge(1, 1, 2)
-        hinge(1, 1, 0)
-        score(1, 0, 2, 7)
-        hinge(1, 0, 2)
-        score(1, 0, 0, 4)
-        hinge(1, 0, 0)
-        cast_x(2, 1, "v")
-        square(1, 1, 1, "s")
-        square(1, 0, 0, "s")
-        quant_x(2, 1)
-        score(2, 0, 1, 2)
-        square(1, 0, 1, "s")
-        score(2, 1, 0, 5)
-        score(2, 0, 3, 6)
-        score(2, 0, 2, 7)
-        hinge(2, 0, 1)
-        score(2, 0, 0, 1)
-        hinge(2, 1, 0)
-        score(2, 1, 2, 0)
-        hinge(2, 0, 3)
-        gather_wd(0, 0)
-        cast_x(0, 0, "v")
-        gather_wd(0, 1)
-        quant_x(0, 0)
-        turn_wd(0, 1, 3)
-        score(2, 1, 1, 2)
-        hinge(2, 0, 2)
-        gather_wd(3, 0)
-        hinge(2, 0, 0)
-        hinge(2, 1, 2)
-        quant_h(1, 0)
-        square(2, 0, 0, "s")
-        score(2, 1, 3, 1)
+        perm_tab(1, 0)
+        gains()
+        load_wd(2)
+        cast_x(1, 1, "s")
+        cast_x(2, 1, "s")
+        quant_x(1, 1)
         cast_x(0, 1, "v")
-        square(2, 0, 1, "s")
-        turn_wd(3, 0, 6)
-        sign_wd(3, 0)
-        hinge(2, 1, 3)
-        base(1, 1, 4)
-        hinge(2, 1, 1)
+        quant_x(2, 0)
+        score(1, 0, 2, 7)
         quant_x(0, 1)
-        score(0, 1, 0, 7)
-        sign_wd(0, 1)
-        gather_wd(3, 1)
-        score(0, 0, 2, 5)
-        score(0, 1, 2, 2)
-        gather_wd(2, 0)
-        square(1, 1, 0, "s")
-        hinge(0, 0, 2)
-        hinge(0, 1, 2)
-        hinge(0, 1, 0)
-        quant_h(2, 0)
-        turn_wd(3, 1, 0)
-        turn_wd(2, 0, 5)
-        score(0, 0, 0, 1)
-        sign_wd(2, 0)
-        square(2, 1, 0, "s")
+        score(1, 0, 0, 1)
+        hinge(1, 0, 0)
+        gather_tab(0, 1)
+        quant_x(0, 0)
+        load_w4w()
+        score(0, 0, 0, 4)
+        quant_x(2, 1)
+        gather_scales(1)
         hinge(0, 0, 0)
-        turn_wd(0, 0, 6)
-        base(3, 0, 5)
-        square(2, 1, 1, "s")
-        gather_wd(1, 0)
-        square(0, 0, 1, "s")
-        base(0, 1, 3)
+        load_wd(0)
+        score(0, 0, 2, 1)
+        perm_tab(1, 1)
+        perm_tab(0, 1)
+        hinge(0, 0, 2)
+        score(2, 0, 3, 0)
+        gather_wd(2)
+        hinge(1, 0, 2)
+        perm_scales(1)
+        score(2, 1, 0, 6)
+        square(1, 0, 0, "s")
+        hinge(2, 1, 0)
+        hinge(2, 0, 3)
+        score(1, 1, 0, 1)
+        score(2, 1, 2, 2)
+        square(1, 0, 1, "s")
+        hinge(1, 1, 0)
+        hinge(2, 1, 2)
         square(0, 0, 0, "s")
-        sign_wd(0, 0)
-        sign_wd(3, 1)
-        base(3, 1, 6)
-        base(0, 0, 1)
-        gather_wd(1, 1)
-        quant_wd(3)
-        turn_wd(1, 0, 2)
-        quant_wd(0)
-        base(2, 0, 7)
-        quant_h(1, 1)
-        sign_wd(1, 0)
-        base(2, 1, 0)
-        down(3, 1, 0)
-        down(0, 1, 0)
-        quant_h(2, 1)
-        turn_wd(1, 1, 2)
-        quant_h(0, 0)
-        down(0, 1, 1)
+        score(2, 1, 1, 6)
+        score(0, 1, 0, 5)
+        score(2, 0, 2, 7)
+        hinge(2, 0, 2)
+        score(2, 0, 1, 1)
+        load_wd(3)
+        score(2, 0, 0, 4)
+        hinge(2, 0, 0)
+        gather_wd(1)
+        hinge(2, 1, 1)
+        gather_wd(0)
+        hinge(0, 1, 0)
+        score(1, 1, 2, 6)
+        score(0, 1, 2, 5)
+        hinge(0, 1, 2)
+        gather_wd(3)
+        quant_h(1, 0)
+        hinge(2, 0, 1)
+        hinge(1, 1, 2)
+        score(2, 1, 3, 3)
+        base(2, 1, 2)
+        square(1, 1, 0, "v")
         square(0, 1, 0, "s")
-        down(0, 0, 0)
+        turn_wd(3, 6)
+        turn_wd(0, 1)
+        hinge(2, 1, 3)
+        square(0, 0, 1, "s")
+        square(1, 1, 1, "s")
+        sign_wd(3)
+        square(2, 0, 1, "s")
+        base(0, 0, 7)
+        quant_wd(3)
+        sign_wd(0)
+        square(2, 1, 1, "s")
+        turn_wd(2, 5)
+        base(1, 0, 0)
+        turn_wd(1, 1)
+        square(0, 1, 1, "v")
+        sign_wd(2)
+        base(1, 1, 3)
+        quant_h(0, 0)
+        base(3, 0, 6)
+        quant_wd(0)
         down(3, 0, 0)
-        sign_wd(1, 1)
-        square(0, 1, 1, "s")
         quant_h(0, 1)
-        gather_wd(2, 1)
-        store(0, 1, "s")
-        down(3, 1, 1)
+        square(2, 0, 0, "s")
+        quant_h(1, 1)
+        quant_h(2, 0)
+        sign_wd(1)
+        base(2, 0, 4)
+        base(0, 1, 1)
+        down(0, 0, 0)
         down(0, 0, 1)
-        down(3, 0, 1)
-        store(3, 1, "s")
-        base(1, 0, 2)
-        turn_wd(2, 1, 3)
-        quant_wd(1)
-        sign_wd(2, 1)
-        store(3, 0, "s")
+        square(2, 1, 0, "s")
         quant_wd(2)
-        store(0, 0, "s")
-        down(1, 1, 0)
-        down(1, 1, 1)
-        down(1, 0, 0)
-        store(1, 1, "s")
-        down(1, 0, 1)
-        down(2, 0, 0)
-        down(2, 0, 1)
-        store(1, 0, "v")
-        store(2, 0, "s")
         down(2, 1, 0)
+        quant_h(2, 1)
+        quant_wd(1)
+        down(0, 1, 0)
+        down(1, 0, 0)
+        down(2, 0, 0)
+        down(0, 1, 1)
+        store(0, 0, "s")
+        store(0, 1, "v")
+        base(3, 1, 5)
+        down(3, 1, 0)
+        down(2, 0, 1)
         down(2, 1, 1)
-        store(2, 1, "v")
+        store(2, 1, "s")
+        down(1, 0, 1)
+        down(3, 1, 1)
+        store(3, 1, "v")
+        down(1, 1, 0)
+        store(1, 0, "v")
+        down(3, 0, 1)
+        down(1, 1, 1)
+        store(1, 1, "s")
+        store(3, 0, "v")
+        store(2, 0, "s")

@@ -24,9 +24,9 @@ KP = K // PASS
 JP = S // PASS
 NT = N // P
 HALF = 512
-CHUNKS = [(0, 256), (256, 256), (512, 512)]
+CHUNKS = [(0, 512), (512, 512)]
 TINY = 2.0 ** -100
-SLOT = {"act10": "xr01"}
+SLOT = {"hb00": "xb10", "hb01": "wg1", "wb0": "wd2", "wb2": "act01"}
 
 
 def interleaved(dst, src):
@@ -143,18 +143,12 @@ def tile_list_cardinality_margin_corrections_kernel(
         def span(b, width):
             return slice(0, JP * width) if b == JP else slice(b * width, (b + 1) * width)
 
-        tp = [keep.tile([P, S], U32, name="tp%d" % a, align_bytes=64) for a in range(KP)]
         tg = [keep.tile([P, JP, PACK, P], U32, name="tg%d" % a, align_bytes=64) for a in range(KP)]
 
         def gather_tab(a, b):
             nc.vector.tensor_copy(
-                tp[a][:, span(b, PASS)], tab[a][:].bitcast(U32).indirect(offsets[:, span(b, PASS // 16)])
-            )
-
-        def perm_tab(a, b):
-            nc.vector.tensor_copy(
-                tg[a][:, span(b, 1), :, :].bitcast(I32).rearrange("p b t (c k) -> p b c t k", k=4),
-                tp[a][:, span(b, PASS)].bitcast(I32).rearrange("p (b c k t) -> p b c t k", c=P // 4, k=4, t=PACK),
+                tg[a][:, span(b, 1), :, :].rearrange("p b t i -> p b i t"),
+                tab[a][:].bitcast(U32).indirect(offsets[:, span(b, PASS // 16)]),
             )
 
         xq = [keep.tile([P, M], U32, name="xq%d" % a, align_bytes=64) for a in range(KP)]
@@ -243,16 +237,14 @@ def tile_list_cardinality_margin_corrections_kernel(
         wb = {}
 
         def gather_wd(n):
-            wg[n] = slot("wg%d" % n, [P, JP, PASS + 32], BF16)
-            nc.vector.tensor_copy(wg[n][:, :, 0:PASS], wd[n][:].indirect(offsets[:]))
+            wg[n] = slot("wg%d" % n, [P, 2, JP * P, 2], BF16)
+            nc.vector.tensor_copy(wg[n][:].rearrange("p u i e -> p i u e"), wd[n][:].indirect(offsets[:]))
 
         def turn_wd(n, bk):
             wt[n] = bank(bk)
-            for b in range(JP):
-                words = wg[n][:, b, 0:PASS].bitcast(F32)
-                for u in range(2):
-                    at = (u * JP + b) * P
-                    nc.tensor.transpose(wt[n][:, at : at + P], words[:, u : 2 * P : 2], ident[:])
+            words = wg[n][:].rearrange("p u i e -> p (u i e)").bitcast(F32)
+            for at in range(0, 2 * JP * P, P):
+                nc.tensor.transpose(wt[n][:, at : at + P], words[:, at : at + P], ident[:])
 
         def sign_wd(n):
             wb[n] = slot("wb%d" % n, [P, JP, P, PACK], BF16)
@@ -308,143 +300,127 @@ def tile_list_cardinality_margin_corrections_kernel(
             nc.sync.dma_start(out[n * P : (n + 1) * P, cols], res[:])
 
         zero()
-        load_x(1, 0)
-        load_tsc()
-        load_offs()
-        load_tab(0)
-        load_x(2, 0)
-        load_x(1, 1)
-        load_g()
-        load_tab(1)
         load_x(0, 0)
-        cast_x(2, 0, "s")
-        gather_tab(1, 0)
-        gather_scales(0)
-        cast_x(0, 0, "s")
-        cast_x(1, 0, "v")
-        load_w4s()
-        load_x(2, 1)
-        gather_tab(0, 0)
-        perm_scales(0)
-        perm_tab(0, 0)
+        load_offs()
+        load_tsc()
+        load_g()
         load_x(0, 1)
-        gather_tab(1, 1)
-        load_wd(1)
-        quant_x(1, 0)
-        perm_tab(1, 0)
+        load_tab(0)
+        gather_scales(0)
+        cast_x(0, 0, "v")
+        load_tab(1)
+        gather_tab(0, 0)
         gains()
-        load_wd(2)
-        cast_x(1, 1, "s")
-        cast_x(2, 1, "s")
-        quant_x(1, 1)
-        cast_x(0, 1, "v")
-        quant_x(2, 0)
-        score(1, 0, 2, 7)
+        perm_scales(0)
+        load_x(1, 1)
+        cast_x(0, 1, "s")
         quant_x(0, 1)
-        score(1, 0, 0, 1)
-        hinge(1, 0, 0)
-        gather_tab(0, 1)
         quant_x(0, 0)
-        load_w4w()
-        score(0, 0, 0, 4)
-        quant_x(2, 1)
-        gather_scales(1)
-        hinge(0, 0, 0)
-        load_wd(0)
-        score(0, 0, 2, 1)
-        perm_tab(1, 1)
-        perm_tab(0, 1)
-        hinge(0, 0, 2)
-        score(2, 0, 3, 0)
-        gather_wd(2)
-        hinge(1, 0, 2)
-        perm_scales(1)
-        score(2, 1, 0, 6)
-        square(1, 0, 0, "s")
-        hinge(2, 1, 0)
-        hinge(2, 0, 3)
-        score(1, 1, 0, 1)
-        score(2, 1, 2, 2)
-        square(1, 0, 1, "s")
-        hinge(1, 1, 0)
-        hinge(2, 1, 2)
-        square(0, 0, 0, "s")
-        score(2, 1, 1, 6)
-        score(0, 1, 0, 5)
-        score(2, 0, 2, 7)
-        hinge(2, 0, 2)
-        score(2, 0, 1, 1)
+        gather_tab(1, 0)
+        load_x(1, 0)
+        cast_x(1, 1, "v")
+        cast_x(1, 0, "v")
+        quant_x(1, 1)
         load_wd(3)
-        score(2, 0, 0, 4)
-        hinge(2, 0, 0)
-        gather_wd(1)
-        hinge(2, 1, 1)
-        gather_wd(0)
-        hinge(0, 1, 0)
-        score(1, 1, 2, 6)
-        score(0, 1, 2, 5)
-        hinge(0, 1, 2)
-        gather_wd(3)
-        quant_h(1, 0)
-        hinge(2, 0, 1)
-        hinge(1, 1, 2)
-        score(2, 1, 3, 3)
-        base(2, 1, 2)
-        square(1, 1, 0, "v")
-        square(0, 1, 0, "s")
-        turn_wd(3, 6)
-        turn_wd(0, 1)
-        hinge(2, 1, 3)
+        quant_x(1, 0)
+        score(1, 0, 3, 3)
+        hinge(1, 0, 3)
+        score(0, 0, 3, 4)
+        score(0, 0, 0, 1)
+        hinge(0, 0, 3)
+        hinge(0, 0, 0)
+        score(1, 0, 1, 2)
+        score(0, 0, 1, 0)
+        gather_tab(1, 1)
+        score(0, 0, 2, 7)
+        gather_tab(0, 1)
+        hinge(0, 0, 2)
+        gather_scales(1)
+        perm_scales(1)
+        score(0, 1, 3, 6)
+        load_wd(1)
+        hinge(0, 0, 1)
+        square(0, 0, 0, "s")
+        score(0, 1, 0, 4)
+        load_w4s()
+        load_w4w()
+        hinge(0, 1, 3)
         square(0, 0, 1, "s")
-        square(1, 1, 1, "s")
-        sign_wd(3)
-        square(2, 0, 1, "s")
-        base(0, 0, 7)
-        quant_wd(3)
-        sign_wd(0)
-        square(2, 1, 1, "s")
-        turn_wd(2, 5)
-        base(1, 0, 0)
-        turn_wd(1, 1)
-        square(0, 1, 1, "v")
-        sign_wd(2)
-        base(1, 1, 3)
+        hinge(0, 1, 0)
+        score(1, 0, 0, 4)
+        score(0, 1, 2, 5)
+        score(0, 1, 1, 7)
+        hinge(1, 0, 0)
         quant_h(0, 0)
-        base(3, 0, 6)
+        load_wd(0)
+        score(1, 1, 0, 1)
+        gather_wd(3)
+        hinge(1, 0, 1)
+        hinge(0, 1, 2)
+        gather_wd(1)
+        turn_wd(3, 3)
+        load_wd(2)
+        score(1, 0, 2, 5)
+        turn_wd(1, 4)
+        score(1, 1, 3, 0)
+        hinge(1, 1, 0)
+        hinge(1, 1, 3)
+        sign_wd(3)
+        hinge(0, 1, 1)
+        hinge(1, 0, 2)
+        score(1, 1, 1, 7)
+        score(1, 1, 2, 2)
+        quant_wd(3)
+        base(0, 0, 1)
+        hinge(1, 1, 1)
+        gather_wd(0)
+        gather_wd(2)
+        hinge(1, 1, 2)
+        turn_wd(0, 6)
+        sign_wd(0)
+        square(0, 1, 0, "s")
+        base(3, 1, 7)
         quant_wd(0)
-        down(3, 0, 0)
-        quant_h(0, 1)
-        square(2, 0, 0, "s")
-        quant_h(1, 1)
-        quant_h(2, 0)
-        sign_wd(1)
-        base(2, 0, 4)
-        base(0, 1, 1)
+        base(1, 0, 3)
         down(0, 0, 0)
-        down(0, 0, 1)
-        square(2, 1, 0, "s")
-        quant_wd(2)
-        down(2, 1, 0)
-        quant_h(2, 1)
+        base(1, 1, 2)
+        sign_wd(1)
+        turn_wd(2, 4)
+        base(0, 1, 6)
         quant_wd(1)
-        down(0, 1, 0)
-        down(1, 0, 0)
-        down(2, 0, 0)
-        down(0, 1, 1)
-        store(0, 0, "s")
-        store(0, 1, "v")
-        base(3, 1, 5)
-        down(3, 1, 0)
-        down(2, 0, 1)
+        square(1, 1, 1, "s")
+        square(0, 1, 1, "s")
+        quant_h(0, 1)
+        base(2, 0, 5)
+        square(1, 1, 0, "s")
+        sign_wd(2)
+        square(1, 0, 0, "s")
+        base(3, 0, 0)
+        square(1, 0, 1, "s")
+        quant_h(1, 0)
+        quant_wd(2)
+        quant_h(1, 1)
+        down(3, 0, 0)
+        base(2, 1, 4)
+        down(2, 1, 0)
+        down(0, 0, 1)
         down(2, 1, 1)
-        store(2, 1, "s")
-        down(1, 0, 1)
-        down(3, 1, 1)
-        store(3, 1, "v")
-        down(1, 1, 0)
-        store(1, 0, "v")
         down(3, 0, 1)
-        down(1, 1, 1)
-        store(1, 1, "s")
-        store(3, 0, "v")
+        store(3, 0, "s")
+        down(2, 0, 0)
+        down(0, 1, 0)
+        store(2, 1, "v")
+        down(1, 0, 0)
+        down(1, 0, 1)
+        store(1, 0, "s")
+        down(0, 1, 1)
+        down(1, 1, 0)
+        store(0, 1, "s")
+        store(0, 0, "s")
+        down(2, 0, 1)
         store(2, 0, "s")
+        down(1, 1, 1)
+        down(3, 1, 0)
+        down(3, 1, 1)
+        store(1, 1, "s")
+        store(3, 1, "v")

@@ -24,9 +24,9 @@ KP = K // PASS
 JP = S // PASS
 NT = N // P
 HALF = 512
-CHUNKS = [(0, 512), (512, 512)]
+CHUNKS = [(0, 256), (256, 256), (512, 512)]
 TINY = 2.0 ** -100
-SLOT = {"hb00": "xb10", "hb01": "wg1", "wb0": "wd2", "wb2": "act01"}
+SLOT = {"hb10": "xb21", "wb0": "xb20", "hb01": "xr21", "wb3": "act20", "wb2": "act20", "act00": "xb11"}
 
 
 def interleaved(dst, src):
@@ -111,23 +111,22 @@ def tile_list_cardinality_margin_corrections_kernel(
         nroot = small("nroot")
         sign = small("sign", BF16)
 
+        gv = gain[:].rearrange("p b t -> p (b t)")
+        mag, root0, inv, corr, step = small("mag"), small("root0"), small("inv"), small("corr"), small("step")
+
         def gains():
-            gv = gain[:].rearrange("p b t -> p (b t)")
-            step, sgn, mag, safe, power = small("step"), small("sgn"), small("mag"), small("safe"), small("power")
-            y0, y2, res, fix, y1 = small("y0"), small("y2"), small("res"), small("fix"), small("y1")
-            nc.gpsimd.memset(power[:], -0.5)
-            nc.gpsimd.tensor_scalar(step[:], gv, 0.0, 2.0, ALU.is_ge, ALU.mult)
-            nc.gpsimd.tensor_scalar(sgn[:], step[:], 1.0, -1.0, ALU.mult, ALU.add)
-            nc.gpsimd.tensor_tensor(mag[:], gv, sgn[:], ALU.mult)
-            nc.gpsimd.tensor_scalar(safe[:], mag[:], 1.0, TINY, ALU.mult, ALU.add)
-            nc.gpsimd.tensor_tensor(y0[:], safe[:], power[:], ALU.pow)
-            nc.gpsimd.tensor_tensor(y2[:], y0[:], safe[:], ALU.mult)
-            nc.gpsimd.tensor_tensor(res[:], y2[:], y0[:], ALU.mult)
-            nc.gpsimd.tensor_scalar(fix[:], res[:], -0.5, 1.5, ALU.mult, ALU.add)
-            nc.gpsimd.tensor_tensor(y1[:], y0[:], fix[:], ALU.mult)
-            nc.gpsimd.tensor_tensor(root[:], mag[:], y1[:], ALU.mult)
-            nc.gpsimd.tensor_scalar(nroot[:], root[:], -1.0, 0.0, ALU.mult, ALU.add)
-            nc.gpsimd.tensor_copy(sign[:], sgn[:])
+            nc.vector.scalar_tensor_tensor(mag[:], gv, -1.0, gv, ALU.mult, ALU.max)
+            nc.scalar.activation(root0[:], mag[:], ACT.Sqrt, bias=TINY)
+
+        def gains2():
+            nc.vector.reciprocal(inv[:], root0[:])
+            nc.vector.scalar_tensor_tensor(corr[:], mag[:], 0.5, inv[:], ALU.mult, ALU.mult)
+            nc.vector.scalar_tensor_tensor(root[:], root0[:], 0.5, corr[:], ALU.mult, ALU.add)
+            nc.scalar.activation(nroot[:], root[:], ACT.Copy, scale=-1.0)
+
+        def gains3():
+            nc.vector.tensor_scalar(step[:], gv, 0.0, 2.0, ALU.is_ge, ALU.mult)
+            nc.vector.tensor_scalar_add(sign[:], step[:], -1.0)
 
         tsg = keep.tile([P, S], U8, name="tsg", align_bytes=64)
         tsp = keep.tile([P, JP, PACK, P], U8, name="tsp", align_bytes=64)
@@ -143,12 +142,18 @@ def tile_list_cardinality_margin_corrections_kernel(
         def span(b, width):
             return slice(0, JP * width) if b == JP else slice(b * width, (b + 1) * width)
 
+        tp = [keep.tile([P, S], U32, name="tp%d" % a, align_bytes=64) for a in range(KP)]
         tg = [keep.tile([P, JP, PACK, P], U32, name="tg%d" % a, align_bytes=64) for a in range(KP)]
 
         def gather_tab(a, b):
             nc.vector.tensor_copy(
-                tg[a][:, span(b, 1), :, :].rearrange("p b t i -> p b i t"),
-                tab[a][:].bitcast(U32).indirect(offsets[:, span(b, PASS // 16)]),
+                tp[a][:, span(b, PASS)], tab[a][:].bitcast(U32).indirect(offsets[:, span(b, PASS // 16)])
+            )
+
+        def perm_tab(a, b):
+            nc.vector.tensor_copy(
+                tg[a][:, span(b, 1), :, :].bitcast(I32).rearrange("p b t (c k) -> p b c t k", k=4),
+                tp[a][:, span(b, PASS)].bitcast(I32).rearrange("p (b c k t) -> p b c t k", c=P // 4, k=4, t=PACK),
             )
 
         xq = [keep.tile([P, M], U32, name="xq%d" % a, align_bytes=64) for a in range(KP)]
@@ -237,14 +242,16 @@ def tile_list_cardinality_margin_corrections_kernel(
         wb = {}
 
         def gather_wd(n):
-            wg[n] = slot("wg%d" % n, [P, 2, JP * P, 2], BF16)
-            nc.vector.tensor_copy(wg[n][:].rearrange("p u i e -> p i u e"), wd[n][:].indirect(offsets[:]))
+            wg[n] = slot("wg%d" % n, [P, JP, PASS + 32], BF16)
+            nc.vector.tensor_copy(wg[n][:, :, 0:PASS], wd[n][:].indirect(offsets[:]))
 
         def turn_wd(n, bk):
             wt[n] = bank(bk)
-            words = wg[n][:].rearrange("p u i e -> p (u i e)").bitcast(F32)
-            for at in range(0, 2 * JP * P, P):
-                nc.tensor.transpose(wt[n][:, at : at + P], words[:, at : at + P], ident[:])
+            for b in range(JP):
+                words = wg[n][:, b, 0:PASS].bitcast(F32)
+                for u in range(2):
+                    at = (u * JP + b) * P
+                    nc.tensor.transpose(wt[n][:, at : at + P], words[:, u : 2 * P : 2], ident[:])
 
         def sign_wd(n):
             wb[n] = slot("wb%d" % n, [P, JP, P, PACK], BF16)
@@ -300,127 +307,145 @@ def tile_list_cardinality_margin_corrections_kernel(
             nc.sync.dma_start(out[n * P : (n + 1) * P, cols], res[:])
 
         zero()
-        load_x(0, 0)
+        load_g()
+        gains()
+        load_tab(0)
         load_offs()
         load_tsc()
-        load_g()
-        load_x(0, 1)
-        load_tab(0)
-        gather_scales(0)
-        cast_x(0, 0, "v")
+        gather_scales(1)
+        load_x(0, 0)
         load_tab(1)
-        gather_tab(0, 0)
-        gains()
-        perm_scales(0)
+        gather_scales(0)
+        load_x(0, 1)
+        perm_scales(1)
+        gains2()
         load_x(1, 1)
+        cast_x(0, 0, "s")
+        cast_x(1, 1, "s")
+        perm_scales(0)
         cast_x(0, 1, "s")
-        quant_x(0, 1)
         quant_x(0, 0)
         gather_tab(1, 0)
-        load_x(1, 0)
-        cast_x(1, 1, "v")
-        cast_x(1, 0, "v")
-        quant_x(1, 1)
-        load_wd(3)
-        quant_x(1, 0)
-        score(1, 0, 3, 3)
-        hinge(1, 0, 3)
-        score(0, 0, 3, 4)
-        score(0, 0, 0, 1)
-        hinge(0, 0, 3)
-        hinge(0, 0, 0)
-        score(1, 0, 1, 2)
-        score(0, 0, 1, 0)
-        gather_tab(1, 1)
-        score(0, 0, 2, 7)
         gather_tab(0, 1)
-        hinge(0, 0, 2)
-        gather_scales(1)
-        perm_scales(1)
-        score(0, 1, 3, 6)
-        load_wd(1)
-        hinge(0, 0, 1)
-        square(0, 0, 0, "s")
-        score(0, 1, 0, 4)
-        load_w4s()
-        load_w4w()
-        hinge(0, 1, 3)
-        square(0, 0, 1, "s")
-        hinge(0, 1, 0)
-        score(1, 0, 0, 4)
-        score(0, 1, 2, 5)
-        score(0, 1, 1, 7)
-        hinge(1, 0, 0)
-        quant_h(0, 0)
+        load_x(1, 0)
+        cast_x(1, 0, "s")
         load_wd(0)
-        score(1, 1, 0, 1)
-        gather_wd(3)
-        hinge(1, 0, 1)
-        hinge(0, 1, 2)
-        gather_wd(1)
-        turn_wd(3, 3)
-        load_wd(2)
-        score(1, 0, 2, 5)
-        turn_wd(1, 4)
-        score(1, 1, 3, 0)
-        hinge(1, 1, 0)
-        hinge(1, 1, 3)
-        sign_wd(3)
-        hinge(0, 1, 1)
-        hinge(1, 0, 2)
-        score(1, 1, 1, 7)
-        score(1, 1, 2, 2)
-        quant_wd(3)
-        base(0, 0, 1)
-        hinge(1, 1, 1)
+        perm_tab(1, 0)
+        load_x(2, 0)
+        load_x(2, 1)
+        cast_x(2, 1, "v")
+        gather_tab(0, 0)
+        gather_tab(1, 1)
+        quant_x(2, 1)
+        load_wd(1)
+        quant_x(1, 0)
         gather_wd(0)
-        gather_wd(2)
-        hinge(1, 1, 2)
-        turn_wd(0, 6)
+        quant_x(1, 1)
+        perm_tab(0, 0)
+        perm_tab(0, 1)
+        load_w4w()
+        score(1, 0, 2, 5)
+        cast_x(2, 0, "v")
+        quant_x(0, 1)
+        quant_x(2, 0)
+        perm_tab(1, 1)
+        score(1, 1, 0, 3)
+        score(1, 0, 0, 1)
+        hinge(1, 0, 0)
+        gains3()
+        score(1, 1, 2, 4)
+        hinge(1, 0, 2)
+        turn_wd(0, 2)
+        gather_wd(1)
+        score(0, 0, 0, 6)
         sign_wd(0)
-        square(0, 1, 0, "s")
-        base(3, 1, 7)
-        quant_wd(0)
-        base(1, 0, 3)
-        down(0, 0, 0)
-        base(1, 1, 2)
-        sign_wd(1)
-        turn_wd(2, 4)
-        base(0, 1, 6)
-        quant_wd(1)
-        square(1, 1, 1, "s")
-        square(0, 1, 1, "s")
-        quant_h(0, 1)
-        base(2, 0, 5)
-        square(1, 1, 0, "s")
-        sign_wd(2)
-        square(1, 0, 0, "s")
-        base(3, 0, 0)
+        hinge(0, 0, 0)
         square(1, 0, 1, "s")
+        score(0, 1, 2, 0)
+        score(0, 0, 2, 1)
+        hinge(0, 0, 2)
+        hinge(1, 1, 0)
+        hinge(1, 1, 2)
+        square(1, 1, 0, "s")
+        square(0, 0, 1, "s")
+        score(2, 1, 3, 7)
+        score(2, 0, 0, 4)
+        score(0, 1, 0, 3)
+        hinge(0, 1, 2)
+        hinge(2, 1, 3)
+        score(2, 0, 1, 2)
+        score(2, 0, 2, 0)
+        square(1, 0, 0, "s")
+        score(2, 1, 1, 5)
+        score(2, 1, 2, 6)
+        hinge(2, 0, 0)
+        hinge(0, 1, 0)
+        score(2, 1, 0, 1)
+        hinge(2, 1, 2)
+        load_w4s()
+        load_wd(3)
+        hinge(2, 1, 0)
+        score(2, 0, 3, 7)
+        turn_wd(1, 6)
+        gather_wd(3)
+        hinge(2, 1, 1)
+        sign_wd(1)
+        base(0, 0, 6)
+        load_wd(2)
+        quant_wd(1)
+        hinge(2, 0, 3)
+        square(0, 1, 1, "v")
+        hinge(2, 0, 1)
+        hinge(2, 0, 2)
+        square(0, 1, 0, "v")
+        base(3, 1, 7)
+        base(3, 0, 2)
+        square(2, 0, 1, "s")
+        base(0, 1, 1)
+        square(2, 0, 0, "s")
+        square(2, 1, 1, "s")
+        quant_h(2, 0)
         quant_h(1, 0)
-        quant_wd(2)
-        quant_h(1, 1)
-        down(3, 0, 0)
-        base(2, 1, 4)
-        down(2, 1, 0)
-        down(0, 0, 1)
-        down(2, 1, 1)
-        down(3, 0, 1)
-        store(3, 0, "s")
-        down(2, 0, 0)
-        down(0, 1, 0)
-        store(2, 1, "v")
-        down(1, 0, 0)
-        down(1, 0, 1)
-        store(1, 0, "s")
-        down(0, 1, 1)
+        base(1, 1, 0)
         down(1, 1, 0)
-        store(0, 1, "s")
-        store(0, 0, "s")
-        down(2, 0, 1)
-        store(2, 0, "s")
+        base(1, 0, 4)
+        quant_wd(0)
+        gather_wd(2)
+        square(0, 0, 0, "s")
+        square(2, 1, 0, "s")
+        quant_h(0, 0)
+        turn_wd(3, 3)
+        quant_h(2, 1)
+        down(0, 1, 0)
+        sign_wd(3)
+        down(0, 1, 1)
         down(1, 1, 1)
+        down(1, 0, 0)
+        store(0, 1, "s")
+        quant_h(0, 1)
+        square(1, 1, 1, "s")
+        quant_h(1, 1)
+        quant_wd(3)
+        down(0, 0, 0)
+        down(1, 0, 1)
+        turn_wd(2, 5)
         down(3, 1, 0)
+        sign_wd(2)
+        base(2, 0, 3)
+        down(3, 0, 0)
+        quant_wd(2)
         down(3, 1, 1)
         store(1, 1, "s")
+        down(3, 0, 1)
+        base(2, 1, 1)
+        down(2, 0, 0)
+        down(2, 0, 1)
+        down(0, 0, 1)
+        store(1, 0, "s")
+        store(2, 0, "s")
+        down(2, 1, 0)
+        store(0, 0, "s")
         store(3, 1, "v")
+        down(2, 1, 1)
+        store(3, 0, "s")
+        store(2, 1, "v")

@@ -26,7 +26,7 @@ NT = N // P
 HALF = 512
 CHUNKS = [(0, 256), (256, 256), (512, 512)]
 TINY = 2.0 ** -100
-SLOT = {"hb10": "xb21", "wb0": "xb20", "hb01": "xr21", "wb3": "act20", "wb2": "act20", "act00": "xb11"}
+SLOT = {"hb10": "xb21", "wb0": "xb20", "wb3": "act20", "act00": "xr11", "wb1": "wd3", "hb01": "xr21", "hb00": "wg0"}
 
 
 def interleaved(dst, src):
@@ -142,18 +142,12 @@ def tile_list_cardinality_margin_corrections_kernel(
         def span(b, width):
             return slice(0, JP * width) if b == JP else slice(b * width, (b + 1) * width)
 
-        tp = [keep.tile([P, S], U32, name="tp%d" % a, align_bytes=64) for a in range(KP)]
         tg = [keep.tile([P, JP, PACK, P], U32, name="tg%d" % a, align_bytes=64) for a in range(KP)]
 
         def gather_tab(a, b):
             nc.vector.tensor_copy(
-                tp[a][:, span(b, PASS)], tab[a][:].bitcast(U32).indirect(offsets[:, span(b, PASS // 16)])
-            )
-
-        def perm_tab(a, b):
-            nc.vector.tensor_copy(
-                tg[a][:, span(b, 1), :, :].bitcast(I32).rearrange("p b t (c k) -> p b c t k", k=4),
-                tp[a][:, span(b, PASS)].bitcast(I32).rearrange("p (b c k t) -> p b c t k", c=P // 4, k=4, t=PACK),
+                tg[a][:, b, :, :].rearrange("p t i -> p i t"),
+                tab[a][:].bitcast(U32).indirect(offsets[:, span(b, PASS // 16)]),
             )
 
         xq = [keep.tile([P, M], U32, name="xq%d" % a, align_bytes=64) for a in range(KP)]
@@ -307,145 +301,141 @@ def tile_list_cardinality_margin_corrections_kernel(
             nc.sync.dma_start(out[n * P : (n + 1) * P, cols], res[:])
 
         zero()
-        load_g()
-        gains()
-        load_tab(0)
-        load_offs()
         load_tsc()
-        gather_scales(1)
-        load_x(0, 0)
-        load_tab(1)
-        gather_scales(0)
+        load_g()
+        gains3()
         load_x(0, 1)
-        perm_scales(1)
-        gains2()
+        cast_x(0, 1, "v")
+        load_offs()
+        load_x(0, 0)
+        load_tab(0)
+        load_tab(1)
         load_x(1, 1)
         cast_x(0, 0, "s")
+        gather_scales(0)
         cast_x(1, 1, "s")
-        perm_scales(0)
-        cast_x(0, 1, "s")
-        quant_x(0, 0)
-        gather_tab(1, 0)
-        gather_tab(0, 1)
+        quant_x(0, 1)
+        gather_tab(0, 0)
         load_x(1, 0)
         cast_x(1, 0, "s")
+        perm_scales(0)
         load_wd(0)
-        perm_tab(1, 0)
+        gather_scales(1)
+        gains()
+        perm_scales(1)
         load_x(2, 0)
-        load_x(2, 1)
-        cast_x(2, 1, "v")
-        gather_tab(0, 0)
-        gather_tab(1, 1)
-        quant_x(2, 1)
-        load_wd(1)
-        quant_x(1, 0)
-        gather_wd(0)
-        quant_x(1, 1)
-        perm_tab(0, 0)
-        perm_tab(0, 1)
-        load_w4w()
-        score(1, 0, 2, 5)
+        gather_tab(1, 0)
+        gather_tab(0, 1)
         cast_x(2, 0, "v")
-        quant_x(0, 1)
+        load_x(2, 1)
+        gather_tab(1, 1)
+        gains2()
+        cast_x(2, 1, "v")
+        quant_x(0, 0)
+        load_wd(1)
+        quant_x(1, 1)
+        quant_x(2, 1)
+        quant_x(1, 0)
         quant_x(2, 0)
-        perm_tab(1, 1)
-        score(1, 1, 0, 3)
-        score(1, 0, 0, 1)
-        hinge(1, 0, 0)
-        gains3()
-        score(1, 1, 2, 4)
-        hinge(1, 0, 2)
-        turn_wd(0, 2)
-        gather_wd(1)
-        score(0, 0, 0, 6)
-        sign_wd(0)
-        hinge(0, 0, 0)
-        square(1, 0, 1, "s")
-        score(0, 1, 2, 0)
-        score(0, 0, 2, 1)
-        hinge(0, 0, 2)
-        hinge(1, 1, 0)
+        gather_wd(0)
+        score(1, 0, 2, 6)
+        score(1, 1, 2, 3)
         hinge(1, 1, 2)
-        square(1, 1, 0, "s")
-        square(0, 0, 1, "s")
-        score(2, 1, 3, 7)
-        score(2, 0, 0, 4)
-        score(0, 1, 0, 3)
-        hinge(0, 1, 2)
-        hinge(2, 1, 3)
-        score(2, 0, 1, 2)
-        score(2, 0, 2, 0)
-        square(1, 0, 0, "s")
-        score(2, 1, 1, 5)
-        score(2, 1, 2, 6)
-        hinge(2, 0, 0)
-        hinge(0, 1, 0)
-        score(2, 1, 0, 1)
-        hinge(2, 1, 2)
+        hinge(1, 0, 2)
+        score(1, 1, 0, 4)
         load_w4s()
-        load_wd(3)
-        hinge(2, 1, 0)
-        score(2, 0, 3, 7)
-        turn_wd(1, 6)
-        gather_wd(3)
-        hinge(2, 1, 1)
-        sign_wd(1)
-        base(0, 0, 6)
-        load_wd(2)
-        quant_wd(1)
-        hinge(2, 0, 3)
-        square(0, 1, 1, "v")
-        hinge(2, 0, 1)
-        hinge(2, 0, 2)
-        square(0, 1, 0, "v")
-        base(3, 1, 7)
-        base(3, 0, 2)
-        square(2, 0, 1, "s")
-        base(0, 1, 1)
-        square(2, 0, 0, "s")
-        square(2, 1, 1, "s")
-        quant_h(2, 0)
-        quant_h(1, 0)
-        base(1, 1, 0)
-        down(1, 1, 0)
-        base(1, 0, 4)
-        quant_wd(0)
-        gather_wd(2)
+        gather_wd(1)
+        load_w4w()
+        score(0, 0, 2, 7)
+        hinge(0, 0, 2)
+        score(0, 1, 0, 7)
+        score(1, 0, 0, 2)
+        score(2, 0, 1, 3)
+        turn_wd(0, 5)
+        hinge(0, 1, 0)
+        score(0, 0, 0, 0)
+        hinge(1, 0, 0)
+        score(2, 0, 0, 1)
+        sign_wd(0)
+        score(0, 1, 2, 7)
+        score(2, 0, 2, 5)
+        hinge(2, 0, 0)
+        hinge(0, 0, 0)
+        hinge(0, 1, 2)
         square(0, 0, 0, "s")
-        square(2, 1, 0, "s")
-        quant_h(0, 0)
-        turn_wd(3, 3)
-        quant_h(2, 1)
-        down(0, 1, 0)
-        sign_wd(3)
-        down(0, 1, 1)
-        down(1, 1, 1)
-        down(1, 0, 0)
-        store(0, 1, "s")
-        quant_h(0, 1)
-        square(1, 1, 1, "s")
-        quant_h(1, 1)
-        quant_wd(3)
-        down(0, 0, 0)
-        down(1, 0, 1)
-        turn_wd(2, 5)
-        down(3, 1, 0)
-        sign_wd(2)
+        score(2, 1, 0, 2)
+        square(1, 0, 1, "s")
+        score(2, 0, 3, 0)
+        score(2, 1, 3, 6)
+        hinge(2, 0, 1)
+        hinge(2, 0, 3)
+        score(2, 1, 1, 7)
+        load_wd(3)
+        square(1, 0, 0, "s")
+        hinge(2, 1, 0)
+        base(1, 1, 0)
+        hinge(2, 1, 3)
+        square(0, 0, 1, "s")
+        base(0, 0, 6)
+        hinge(2, 1, 1)
+        square(0, 1, 1, "s")
+        quant_h(1, 0)
+        score(2, 1, 2, 3)
+        hinge(1, 1, 0)
+        gather_wd(3)
+        square(0, 1, 0, "v")
+        quant_wd(0)
+        hinge(2, 1, 2)
+        hinge(2, 0, 2)
+        square(2, 0, 0, "s")
+        square(1, 1, 0, "s")
+        square(2, 0, 1, "s")
+        turn_wd(3, 7)
         base(2, 0, 3)
+        sign_wd(3)
+        turn_wd(1, 4)
+        base(3, 0, 2)
+        square(1, 1, 1, "s")
+        quant_h(0, 1)
+        base(2, 1, 5)
+        quant_h(1, 1)
+        quant_h(0, 0)
+        sign_wd(1)
+        quant_wd(3)
+        load_wd(2)
+        base(1, 0, 4)
+        down(0, 0, 0)
         down(3, 0, 0)
-        quant_wd(2)
-        down(3, 1, 1)
-        store(1, 1, "s")
-        down(3, 0, 1)
-        base(2, 1, 1)
-        down(2, 0, 0)
-        down(2, 0, 1)
         down(0, 0, 1)
-        store(1, 0, "s")
-        store(2, 0, "s")
-        down(2, 1, 0)
+        quant_wd(1)
+        gather_wd(2)
+        square(2, 1, 0, "s")
+        turn_wd(2, 7)
+        quant_h(2, 0)
         store(0, 0, "s")
-        store(3, 1, "v")
+        base(0, 1, 1)
+        base(3, 1, 6)
+        sign_wd(2)
+        down(1, 0, 0)
+        down(3, 0, 1)
+        down(1, 1, 0)
+        square(2, 1, 1, "s")
+        quant_wd(2)
+        quant_h(2, 1)
+        down(1, 1, 1)
+        down(0, 1, 0)
+        down(1, 0, 1)
+        down(0, 1, 1)
+        down(3, 1, 0)
+        down(3, 1, 1)
+        store(1, 0, "s")
+        down(2, 1, 0)
         down(2, 1, 1)
-        store(3, 0, "s")
         store(2, 1, "v")
+        down(2, 0, 0)
+        store(0, 1, "v")
+        store(1, 1, "s")
+        store(3, 0, "s")
+        down(2, 0, 1)
+        store(3, 1, "s")
+        store(2, 0, "s")

@@ -23,10 +23,13 @@ PASS = P * PACK
 KP = K // PASS
 JP = S // PASS
 NT = N // P
-HALF = 512
-CHUNKS = [(0, 256), (256, 256), (512, 512)]
+BANK = 512
+W = 256
+NC = M // W
 TINY = 2.0 ** -100
-SLOT = {"hb10": "xb21", "wb0": "xb20", "wb3": "act20", "act00": "xr11", "wb1": "wd3", "hb01": "xr21", "hb00": "wg0"}
+SCORE_BANKS = (0, 1, 2, 3)
+TURN_BANK = 4
+SUM_BANKS = (5, 6, 7)
 
 
 def interleaved(dst, src):
@@ -42,400 +45,290 @@ def tile_list_cardinality_margin_corrections_kernel(
     nc = tc.nc
     with ExitStack() as ctx:
         keep = ctx.enter_context(tc.tile_pool(name="keep", bufs=1))
+        reuse = ctx.enter_context(tc.tile_pool(name="reuse", bufs=1))
         psum = ctx.enter_context(tc.psum_pool(name="psum", bufs=1))
 
         def bank(i):
-            return psum.tile([P, HALF], F32, name="bank%d" % i)
+            return psum.tile([P, BANK], F32, name="bank%d" % i)
 
-        def slot(name, shape, dtype):
-            return keep.tile(shape, dtype, name=name, tag=SLOT.get(name, name), align_bytes=64)
+        def sb(name, shape, dtype, tag=None):
+            return keep.tile(shape, dtype, name=name, tag=tag or name, align_bytes=64)
+
+        place = {"end": 0}
+
+        def shared(name, shape, dtype, size, over=None, shift=0):
+            if over is None:
+                place[name] = place["end"]
+                place["end"] = place["end"] + size
+            else:
+                place[name] = place[over] + shift
+            return reuse.tile(shape, dtype, name=name, align_bytes=64, offset=place[name])
+
+        def list_part(b):
+            return offsets[:, b * (PASS // 16) : (b + 1) * (PASS // 16)]
 
         offsets = keep.tile([P, S // 16], U16, name="offsets")
-        gain = keep.tile([P, JP, PACK], F32, name="gain")
-        tsc = keep.tile([P, T], U8, name="tsc", align_bytes=64)
-        w4s = keep.tile([P, KP, N], U8, name="w4s", align_bytes=64)
-        w4w = keep.tile([P, KP, 2 * N], U8, name="w4w", align_bytes=64)
-        tab = {}
-        wd = {}
-        xraw = {}
-        ident = keep.tile([P, P], F32, name="ident")
+        gain = sb("gain", [P, JP, PACK], F32)
+        tsc = sb("tsc", [P, T], U8)
+        w4s = sb("w4s", [P, KP, N], U8)
+        w4w = sb("w4w", [P, KP, 2 * N], U8)
+        ident = sb("ident", [P, P], F32)
+        tab = [sb("tab%d" % a, [P, T], I32) for a in range(KP)]
+        wd = [shared("wd%d" % n, [P, T], F32, 4 * T) for n in range(NT)]
+        xraw = {(c, a): shared("xr%d%d" % (c, a), [P, PACK, W], F32, 16 * W) for c in range(NC) for a in range(KP)}
 
-        make_identity(nc, ident[:])
+        nc.vector.memset(tsc[:].bitcast(I32), 0)
+        nc.gpsimd.memset(w4s[:].bitcast(I32), 0)
 
-        def zero():
-            nc.vector.memset(tsc[:].bitcast(I32), 0)
-            nc.vector.memset(w4s[:].bitcast(I32), 0)
+        def load_x(c):
+            for a in range(KP):
+                rows = x[a * PASS : (a + 1) * PASS, c * W : (c + 1) * W]
+                nc.sync.dma_start(xraw[c, a][:], rows.rearrange("(p i) m -> p i m", i=PACK))
 
         def load_tab(a):
-            tab[a] = slot("tab%d" % a, [P, T], I32)
             nc.sync.dma_start(tab[a][:], tab_words[a].rearrange("p t i -> p (t i)").bitcast(I32))
 
-        def load_x(c, a):
-            m0, w = CHUNKS[c]
-            xraw[c, a] = slot("xr%d%d" % (c, a), [P, PACK, w], F32)
-            rows = x[a * PASS : (a + 1) * PASS, m0 : m0 + w]
-            nc.sync.dma_start(xraw[c, a][:], rows.rearrange("(p i) m -> p i m", i=PACK))
-
         def load_wd(n):
-            wd[n] = slot("wd%d" % n, [P, T], F32)
             nc.sync.dma_start(wd[n][:], wdT[n * P : (n + 1) * P, :])
 
-        def load_w4s():
-            for q in range(4):
-                nc.sync.dma_start(
-                    w4s[32 * q : 32 * q + 4, :, :].bitcast(I32),
-                    w4_scales[:, 4 * q : 4 * q + 4, :].rearrange("a r c -> r a c").bitcast(I32),
-                )
-
-        def load_w4w():
-            nc.sync.dma_start(w4w[:].bitcast(I32), w4_words.rearrange("a p c -> p a c").bitcast(I32))
-
-        def load_offs():
-            nc.sync.dma_start(offsets[:], offs)
-
-        def load_g():
-            nc.sync.dma_start(gain[:], g.rearrange("(b p t) -> p b t", b=JP, t=PACK))
-
-        def load_tsc():
-            for q in range(4):
-                nc.sync.dma_start(
-                    tsc[32 * q : 32 * q + 4 * KP, :].bitcast(I32),
-                    tab_scales[:, 4 * q : 4 * q + 4, :].bitcast(I32),
-                )
-
+        nc.sync.dma_start(offsets[:], offs)
+        nc.sync.dma_start(gain[:], g.rearrange("(b p t) -> p b t", b=JP, t=PACK))
+        for q in range(4):
+            nc.sync.dma_start(
+                tsc[32 * q : 32 * q + 4 * KP, :].bitcast(I32),
+                tab_scales[:, 4 * q : 4 * q + 4, :].bitcast(I32),
+            )
+        load_tab(0)
+        load_x(0)
+        load_tab(1)
+        load_wd(0)
+        load_x(1)
+        for q in range(4):
+            nc.sync.dma_start(
+                w4s[32 * q : 32 * q + 4, :, :].bitcast(I32),
+                w4_scales[:, 4 * q : 4 * q + 4, :].rearrange("a r c -> r a c").bitcast(I32),
+            )
+        nc.sync.dma_start(w4w[:].bitcast(I32), w4_words.rearrange("a p c -> p a c").bitcast(I32))
+        load_wd(1)
+        load_x(2)
+        load_wd(2)
+        load_x(3)
+        load_wd(3)
+        make_identity(nc, ident[:])
 
         def small(name, dtype=F32):
-            return keep.tile([P, JP * PACK], dtype, name=name)
+            return sb(name, [P, JP * PACK], dtype)
 
-        root = small("root")
-        nroot = small("nroot")
-        sign = small("sign", BF16)
-
-        gv = gain[:].rearrange("p b t -> p (b t)")
+        root, nroot, sign = small("root"), small("nroot"), small("sign", BF16)
         mag, root0, inv, corr, step = small("mag"), small("root0"), small("inv"), small("corr"), small("step")
+        gv = gain[:].rearrange("p b t -> p (b t)")
+        nc.vector.scalar_tensor_tensor(mag[:], gv, -1.0, gv, ALU.mult, ALU.max)
+        nc.scalar.activation(root0[:], mag[:], ACT.Sqrt, bias=TINY)
+        nc.vector.tensor_scalar(step[:], gv, 0.0, 2.0, ALU.is_ge, ALU.mult)
+        nc.vector.tensor_scalar_add(sign[:], step[:], -1.0)
+        nc.vector.reciprocal(inv[:], root0[:])
+        nc.vector.scalar_tensor_tensor(corr[:], mag[:], 0.5, inv[:], ALU.mult, ALU.mult)
+        nc.vector.scalar_tensor_tensor(root[:], root0[:], 0.5, corr[:], ALU.mult, ALU.add)
+        nc.scalar.activation(nroot[:], root[:], ACT.Copy, scale=-1.0)
 
-        def gains():
-            nc.vector.scalar_tensor_tensor(mag[:], gv, -1.0, gv, ALU.mult, ALU.max)
-            nc.scalar.activation(root0[:], mag[:], ACT.Sqrt, bias=TINY)
+        tsg, tsp, tg = {}, {}, {}
 
-        def gains2():
-            nc.vector.reciprocal(inv[:], root0[:])
-            nc.vector.scalar_tensor_tensor(corr[:], mag[:], 0.5, inv[:], ALU.mult, ALU.mult)
-            nc.vector.scalar_tensor_tensor(root[:], root0[:], 0.5, corr[:], ALU.mult, ALU.add)
-            nc.scalar.activation(nroot[:], root[:], ACT.Copy, scale=-1.0)
+        def gather_scales(b, over=None):
+            tsg[b] = shared("tsg%d" % b, [P, PASS], U8, PASS, over)
+            tsp[b] = sb("tsp%d" % b, [P, PACK, P], U8)
+            nc.vector.tensor_copy(tsg[b][:], tsc[:].indirect(list_part(b)))
 
-        def gains3():
-            nc.vector.tensor_scalar(step[:], gv, 0.0, 2.0, ALU.is_ge, ALU.mult)
-            nc.vector.tensor_scalar_add(sign[:], step[:], -1.0)
+        def sort_scales(b):
+            nc.vector.tensor_copy(tsp[b][:], tsg[b][:].rearrange("p (i t) -> p t i", t=PACK))
 
-        tsg = keep.tile([P, S], U8, name="tsg", align_bytes=64)
-        tsp = keep.tile([P, JP, PACK, P], U8, name="tsp", align_bytes=64)
-
-        def gather_scales(b):
-            nc.vector.tensor_copy(tsg[:, span(b, PASS)], tsc[:].indirect(offsets[:, span(b, PASS // 16)]))
-
-        def perm_scales(b):
+        def gather_tab(a, b, over=None):
+            tg[a, b] = shared("tg%d%d" % (a, b), [P, PACK, P], U32, 4 * PASS, over)
             nc.vector.tensor_copy(
-                tsp[:, span(b, 1), :, :], tsg[:, span(b, PASS)].rearrange("p (b i t) -> p b t i", i=P, t=PACK)
+                tg[a, b][:].rearrange("p t i -> p i t"), tab[a][:].bitcast(U32).indirect(list_part(b))
             )
 
-        def span(b, width):
-            return slice(0, JP * width) if b == JP else slice(b * width, (b + 1) * width)
-
-        tg = [keep.tile([P, JP, PACK, P], U32, name="tg%d" % a, align_bytes=64) for a in range(KP)]
-
-        def gather_tab(a, b):
-            nc.vector.tensor_copy(
-                tg[a][:, b, :, :].rearrange("p t i -> p i t"),
-                tab[a][:].bitcast(U32).indirect(offsets[:, span(b, PASS // 16)]),
-            )
-
-        xq = [keep.tile([P, M], U32, name="xq%d" % a, align_bytes=64) for a in range(KP)]
-        xs = [keep.tile([P, M], U8, name="xs%d" % a, align_bytes=64) for a in range(KP)]
-        hq = [keep.tile([P, M], U32, name="hq%d" % b, align_bytes=64) for b in range(JP)]
-        hs = [keep.tile([P, M], U8, name="hs%d" % b, align_bytes=64) for b in range(JP)]
-        wq = [keep.tile([P, JP, P], U32, name="wq%d" % n, align_bytes=64) for n in range(NT)]
-        ws = [keep.tile([P, JP, P], U8, name="ws%d" % n, align_bytes=64) for n in range(NT)]
         xb = {}
+        xq_half = {}
+        xq = {}
+        xs = [sb("xs%d" % a, [P, M], U8) for a in range(KP)]
+        hq = {}
+        hs = [sb("hs%d" % b, [P, M], U8) for b in range(JP)]
 
-        def cast_x(c, a, eng):
-            m0, w = CHUNKS[c]
-            xb[c, a] = slot("xb%d%d" % (c, a), [P, w, PACK], BF16)
-            dst, src = interleaved(xb[c, a][:], xraw[c, a][:])
-            if eng == "s":
-                nc.scalar.copy(dst, src)
-            elif eng == "v":
-                nc.vector.tensor_copy(dst, src)
-            else:
-                nc.gpsimd.tensor_scalar(
-                    xb[c, a][:], xraw[c, a][:].rearrange("p t m -> p m t"), 1.0, 0.0, ALU.mult, ALU.add
-                )
+        def chunk(c):
+            return slice(c * W, (c + 1) * W)
 
-        def quant_x(c, a):
-            m0, w = CHUNKS[c]
-            nc.vector.quantize_mx(
-                xq[a][:, m0 : m0 + w].bitcast(FP8X4),
-                xs[a][:, m0 : m0 + w],
-                xb[c, a][:].rearrange("p m t -> p (m t)"),
-            )
-
-        act = {}
-        hb = {}
-        zb = {}
-
-        def score(c, b, t0, bk):
-            m0, w = CHUNKS[c]
-            zb[c, b, t0] = bank(bk)
-            for u in range(HALF // w):
-                for a in range(KP):
-                    nc.tensor.matmul_mx(
-                        out=zb[c, b, t0][:, u * w : (u + 1) * w],
-                        lhsT=tg[a][:, b, t0 + u, :].bitcast(FP8X4),
-                        lhsT_scale=tsp[4 * a : P, b, t0 + u, :],
-                        rhs=xq[a][:, m0 : m0 + w].bitcast(FP8X4),
-                        rhs_scale=xs[a][:, m0 : m0 + w],
-                        start=(a == 0),
-                        stop=(a == KP - 1),
+        def cast_x(c, a, engines, over=None, shift=0):
+            xb[c, a] = shared("xb%d%d" % (c, a), [P, W, PACK], BF16, 8 * W, over, shift)[:]
+            w = W // len(engines)
+            for i, eng in enumerate(engines):
+                cols = slice(i * w, (i + 1) * w)
+                dst, src = interleaved(xb[c, a][:, cols, :], xraw[c, a][:, :, cols])
+                if eng == "s":
+                    nc.scalar.copy(dst, src)
+                elif eng == "v":
+                    nc.vector.tensor_copy(dst, src)
+                else:
+                    nc.gpsimd.tensor_scalar(
+                        xb[c, a][:, cols, :],
+                        xraw[c, a][:, :, cols].rearrange("p t m -> p m t"),
+                        1.0,
+                        0.0,
+                        ALU.mult,
+                        ALU.add,
                     )
 
-        def hinge(c, b, t0):
-            m0, w = CHUNKS[c]
-            if (c, b) not in act:
-                act[c, b] = slot("act%d%d" % (c, b), [P, PACK, w], F32)
-            for u in range(HALF // w):
-                t = t0 + u
-                nc.scalar.activation(
-                    act[c, b][:, t, :],
-                    zb[c, b, t0][:, u * w : (u + 1) * w],
-                    ACT.Relu,
-                    bias=root[:, b * PACK + t : b * PACK + t + 1],
-                    scale=nroot[:, b * PACK + t : b * PACK + t + 1],
-                )
+        def quantize(codes, scales, values):
+            nc.vector.quantize_mx(codes.bitcast(FP8X4), scales, values.rearrange("p m t -> p (m t)"))
 
-        def square(c, b, part, eng):
-            w = CHUNKS[c][1] // 2
-            if (c, b) not in hb:
-                hb[c, b] = slot("hb%d%d" % (c, b), [P, 2 * w, PACK], BF16)
-            cols = slice(part * w, (part + 1) * w)
-            dst, src = interleaved(hb[c, b][:, cols, :], act[c, b][:, :, cols])
-            if eng == "s":
-                nc.scalar.activation(dst, src, ACT.Square)
-            else:
-                nc.vector.tensor_tensor(dst, src, src, ALU.mult)
+        def quant_x(c):
+            for a in range(KP):
+                if c % 2 == 0:
+                    xq_half[c, a] = shared("xq%d%d" % (c, a), [P, 2 * W], U32, 8 * W, None)
+                xq[c, a] = xq_half[c - c % 2, a][:, chunk(c % 2)]
+                quantize(xq[c, a], xs[a][:, chunk(c)], xb[c, a])
 
-        def quant_h(c, b):
-            m0, w = CHUNKS[c]
-            nc.vector.quantize_mx(
-                hq[b][:, m0 : m0 + w].bitcast(FP8X4),
-                hs[b][:, m0 : m0 + w],
-                hb[c, b][:].rearrange("p m t -> p (m t)"),
-            )
+        hb_of = {}
 
-        wg = {}
-        wt = {}
-        wb = {}
+        def hidden(c, b, banks):
+            act = sb("act%d%d" % (c, b), [P, PACK, W], F32)
+            hb = shared("hb%d%d" % (c, b), [P, W, PACK], BF16, 8 * W)
+            per = PACK // len(banks)
+            for i, bk in enumerate(banks):
+                z = bank(bk)
+                for u in range(per):
+                    for a in range(KP):
+                        nc.tensor.matmul_mx(
+                            out=z[:, u * W : (u + 1) * W],
+                            lhsT=tg[a, b][:, per * i + u, :].bitcast(FP8X4),
+                            lhsT_scale=tsp[b][4 * a : P, per * i + u, :],
+                            rhs=xq[c, a].bitcast(FP8X4),
+                            rhs_scale=xs[a][:, chunk(c)],
+                            start=(a == 0),
+                            stop=(a == KP - 1),
+                        )
+                for u in range(per):
+                    at = b * PACK + per * i + u
+                    nc.scalar.activation(
+                        act[:, per * i + u, :],
+                        z[:, u * W : (u + 1) * W],
+                        ACT.Relu,
+                        bias=root[:, at : at + 1],
+                        scale=nroot[:, at : at + 1],
+                    )
+            dst, src = interleaved(hb[:], act[:])
+            nc.scalar.activation(dst, src, ACT.Square)
+            hb_of[c, b] = hb
 
-        def gather_wd(n):
-            wg[n] = slot("wg%d" % n, [P, JP, PASS + 32], BF16)
-            nc.vector.tensor_copy(wg[n][:, :, 0:PASS], wd[n][:].indirect(offsets[:]))
+        def quant_h(c, b, over, shift=0):
+            hq[c, b] = shared("hq%d%d" % (c, b), [P, W], U32, 4 * W, over, shift)
+            quantize(hq[c, b][:], hs[b][:, chunk(c)], hb_of[c, b][:])
 
-        def turn_wd(n, bk):
-            wt[n] = bank(bk)
-            for b in range(JP):
-                words = wg[n][:, b, 0:PASS].bitcast(F32)
+        wt, wb, wq = {}, {}, {}
+        ws = [sb("ws%d" % n, [P, JP * P], U8) for n in range(NT)]
+
+        def gather_wd(n, b0, b1, over, bk):
+            wg = shared("wg%d%d" % (n, b0), [P, b1 - b0, PASS], BF16, 2 * S, over)
+            picks = offsets[:, b0 * (PASS // 16) : b1 * (PASS // 16)]
+            nc.vector.tensor_copy(wg[:].rearrange("p b j -> p (b j)"), wd[n][:].indirect(picks))
+            wt[n, b0] = bank(bk)
+            for b in range(b1 - b0):
+                words = wg[:, b, :].bitcast(F32)
                 for u in range(2):
-                    at = (u * JP + b) * P
-                    nc.tensor.transpose(wt[n][:, at : at + P], words[:, u : 2 * P : 2], ident[:])
+                    at = (u * (b1 - b0) + b) * P
+                    nc.tensor.transpose(wt[n, b0][:, at : at + P], words[:, u : 2 * P : 2], ident[:])
 
-        def sign_wd(n):
-            wb[n] = slot("wb%d" % n, [P, JP, P, PACK], BF16)
+        def sign_wd(n, b0, b1, over=None):
+            nb = b1 - b0
+            wb[n, b0] = shared("wb%d%d" % (n, b0), [P, nb * P, PACK], BF16, 2 * S, over)
             nc.vector.tensor_tensor(
-                wb[n][:].rearrange("p b c (u e) -> p b c u e", u=2),
-                wt[n][:].bitcast(BF16).rearrange("p (u b c e) -> p b c u e", u=2, b=JP, e=2),
-                sign[:].rearrange("p (b o u e) -> p b o u e", b=JP, o=1, u=2).to_broadcast([P, JP, P, 2, 2]),
+                wb[n, b0][:].rearrange("p (b c) (u e) -> p b c u e", b=nb, u=2),
+                wt[n, b0][:, 0 : nb * 2 * P].bitcast(BF16).rearrange("p (u b c e) -> p b c u e", u=2, b=nb, e=2),
+                sign[:, b0 * PACK : b1 * PACK]
+                .rearrange("p (b o u e) -> p b o u e", b=nb, o=1, u=2)
+                .to_broadcast([P, nb, P, 2, 2]),
                 ALU.mult,
             )
 
-        def quant_wd(n):
-            nc.vector.quantize_mx(
-                wq[n][:].rearrange("p b c -> p (b c)").bitcast(FP8X4),
-                ws[n][:].rearrange("p b c -> p (b c)"),
-                wb[n][:].rearrange("p b c t -> p (b c t)"),
-            )
+        def quant_wd(n, b0, b1, over=None, shift=0):
+            codes = shared("wq%d%d" % (n, b0), [P, (b1 - b0) * P], U32, 4 * JP * P, over, shift)
+            quantize(codes[:], ws[n][:, b0 * P : b1 * P], wb[n, b0][:])
+            for b in range(b0, b1):
+                wq[n, b] = codes[:, (b - b0) * P : (b - b0 + 1) * P]
 
         acc = {}
 
-        def base(n, h, bk):
-            cols = slice(h * HALF, (h + 1) * HALF)
+        def sums(n, h, bk):
             acc[n, h] = bank(bk)
             for a in range(KP):
                 nc.tensor.matmul_mx(
                     out=acc[n, h][:],
                     lhsT=w4w[:, a, 2 * n * P : 2 * (n + 1) * P].bitcast(FP4X4),
                     lhsT_scale=w4s[:, a, n * P : (n + 1) * P],
-                    rhs=xq[a][:, cols].bitcast(FP8X4),
-                    rhs_scale=xs[a][:, cols],
+                    rhs=xq_half[2 * h, a][:].bitcast(FP8X4),
+                    rhs_scale=xs[a][:, h * BANK : (h + 1) * BANK],
                     start=(a == 0),
                     stop=False,
                 )
+            for b in range(JP):
+                for i in range(2):
+                    nc.tensor.matmul_mx(
+                        out=acc[n, h][:, chunk(i)],
+                        lhsT=wq[n, b].bitcast(FP8X4),
+                        lhsT_scale=ws[n][:, b * P : (b + 1) * P],
+                        rhs=hq[2 * h + i, b][:].bitcast(FP8X4),
+                        rhs_scale=hs[b][:, chunk(2 * h + i)],
+                        start=False,
+                        stop=(b == JP - 1 and i == 1),
+                    )
 
-        def down(n, h, b):
-            cols = slice(h * HALF, (h + 1) * HALF)
-            nc.tensor.matmul_mx(
-                out=acc[n, h][:],
-                lhsT=wq[n][:, b, :].bitcast(FP8X4),
-                lhsT_scale=ws[n][:, b, :],
-                rhs=hq[b][:, cols].bitcast(FP8X4),
-                rhs_scale=hs[b][:, cols],
-                start=False,
-                stop=(b == JP - 1),
-            )
-
-        def store(n, h, eng):
-            cols = slice(h * HALF, (h + 1) * HALF)
-            res = slot("res%d%d" % (n, h), [P, HALF], F32)
+        def store(n, h, eng, over=None, shift=0):
+            res = shared("res%d%d" % (n, h), [P, BANK], F32, 4 * BANK, over, shift)
             if eng == "s":
                 nc.scalar.copy(res[:], acc[n, h][:])
             else:
                 nc.vector.tensor_copy(res[:], acc[n, h][:])
-            nc.sync.dma_start(out[n * P : (n + 1) * P, cols], res[:])
+            nc.sync.dma_start(out[n * P : (n + 1) * P, h * BANK : (h + 1) * BANK], res[:])
 
-        zero()
-        load_tsc()
-        load_g()
-        gains3()
-        load_x(0, 1)
-        cast_x(0, 1, "v")
-        load_offs()
-        load_x(0, 0)
-        load_tab(0)
-        load_tab(1)
-        load_x(1, 1)
-        cast_x(0, 0, "s")
-        gather_scales(0)
-        cast_x(1, 1, "s")
-        quant_x(0, 1)
-        gather_tab(0, 0)
-        load_x(1, 0)
-        cast_x(1, 0, "s")
-        perm_scales(0)
-        load_wd(0)
-        gather_scales(1)
-        gains()
-        perm_scales(1)
-        load_x(2, 0)
-        gather_tab(1, 0)
-        gather_tab(0, 1)
-        cast_x(2, 0, "v")
-        load_x(2, 1)
-        gather_tab(1, 1)
-        gains2()
-        cast_x(2, 1, "v")
-        quant_x(0, 0)
-        load_wd(1)
-        quant_x(1, 1)
-        quant_x(2, 1)
-        quant_x(1, 0)
-        quant_x(2, 0)
-        gather_wd(0)
-        score(1, 0, 2, 6)
-        score(1, 1, 2, 3)
-        hinge(1, 1, 2)
-        hinge(1, 0, 2)
-        score(1, 1, 0, 4)
-        load_w4s()
-        gather_wd(1)
-        load_w4w()
-        score(0, 0, 2, 7)
-        hinge(0, 0, 2)
-        score(0, 1, 0, 7)
-        score(1, 0, 0, 2)
-        score(2, 0, 1, 3)
-        turn_wd(0, 5)
-        hinge(0, 1, 0)
-        score(0, 0, 0, 0)
-        hinge(1, 0, 0)
-        score(2, 0, 0, 1)
-        sign_wd(0)
-        score(0, 1, 2, 7)
-        score(2, 0, 2, 5)
-        hinge(2, 0, 0)
-        hinge(0, 0, 0)
-        hinge(0, 1, 2)
-        square(0, 0, 0, "s")
-        score(2, 1, 0, 2)
-        square(1, 0, 1, "s")
-        score(2, 0, 3, 0)
-        score(2, 1, 3, 6)
-        hinge(2, 0, 1)
-        hinge(2, 0, 3)
-        score(2, 1, 1, 7)
-        load_wd(3)
-        square(1, 0, 0, "s")
-        hinge(2, 1, 0)
-        base(1, 1, 0)
-        hinge(2, 1, 3)
-        square(0, 0, 1, "s")
-        base(0, 0, 6)
-        hinge(2, 1, 1)
-        square(0, 1, 1, "s")
-        quant_h(1, 0)
-        score(2, 1, 2, 3)
-        hinge(1, 1, 0)
-        gather_wd(3)
-        square(0, 1, 0, "v")
-        quant_wd(0)
-        hinge(2, 1, 2)
-        hinge(2, 0, 2)
-        square(2, 0, 0, "s")
-        square(1, 1, 0, "s")
-        square(2, 0, 1, "s")
-        turn_wd(3, 7)
-        base(2, 0, 3)
-        sign_wd(3)
-        turn_wd(1, 4)
-        base(3, 0, 2)
-        square(1, 1, 1, "s")
-        quant_h(0, 1)
-        base(2, 1, 5)
-        quant_h(1, 1)
-        quant_h(0, 0)
-        sign_wd(1)
-        quant_wd(3)
-        load_wd(2)
-        base(1, 0, 4)
-        down(0, 0, 0)
-        down(3, 0, 0)
-        down(0, 0, 1)
-        quant_wd(1)
-        gather_wd(2)
-        square(2, 1, 0, "s")
-        turn_wd(2, 7)
-        quant_h(2, 0)
-        store(0, 0, "s")
-        base(0, 1, 1)
-        base(3, 1, 6)
-        sign_wd(2)
-        down(1, 0, 0)
-        down(3, 0, 1)
-        down(1, 1, 0)
-        square(2, 1, 1, "s")
-        quant_wd(2)
-        quant_h(2, 1)
-        down(1, 1, 1)
-        down(0, 1, 0)
-        down(1, 0, 1)
-        down(0, 1, 1)
-        down(3, 1, 0)
-        down(3, 1, 1)
-        store(1, 0, "s")
-        down(2, 1, 0)
-        down(2, 1, 1)
-        store(2, 1, "v")
-        down(2, 0, 0)
-        store(0, 1, "v")
-        store(1, 1, "s")
+        for b in range(JP):
+            gather_scales(b)
+        for b in range(JP):
+            sort_scales(b)
+        for b in range(JP):
+            gather_tab(0, b)
+        for a in range(KP):
+            cast_x(0, a, "s")
+        quant_x(0)
+        for b in range(JP):
+            gather_tab(1, b)
+        hidden(0, 0, (TURN_BANK,) + SCORE_BANKS[0:3])
+        hidden(0, 1, SCORE_BANKS[3:4] + SUM_BANKS)
+        for n in range(NT - 1):
+            c = n + 1
+            gather_wd(n, 0, JP, "xb%d1" % n if n else None, TURN_BANK)
+            quant_h(n // 2 if n else 0, n % 2 if n < 2 else 1, "wd%d" % n)
+            for a in range(KP):
+                cast_x(c, a, "g")
+            quant_x(c)
+            sign_wd(n, 0, JP, "xr%d1" % c)
+            if n:
+                quant_h(n, 0, "xr%d1" % c, 8 * W)
+            quant_wd(n, 0, JP)
+            hidden(c, 0, SCORE_BANKS[0:2])
+            hidden(c, 1, SCORE_BANKS[2:4])
+        for n in range(NT - 1):
+            sums(n, 0, SUM_BANKS[n])
+        gather_wd(3, 0, JP, "xb31", TURN_BANK)
+        quant_h(2, 1, "wd3")
+        sign_wd(3, 0, JP)
+        store(0, 0, "v", "wd3", 4 * W)
+        quant_wd(3, 0, JP)
+        quant_h(3, 0, "wb30")
+        store(1, 0, "v", "wd3", 12 * W)
+        store(2, 0, "v", "wd3", 20 * W)
+        sums(3, 0, TURN_BANK)
+        quant_h(3, 1, "wb30", 4 * W)
         store(3, 0, "s")
-        down(2, 0, 1)
-        store(3, 1, "s")
-        store(2, 0, "s")
+        for n, bk in enumerate((SCORE_BANKS[0], SCORE_BANKS[1], SUM_BANKS[0], SCORE_BANKS[2])):
+            sums(n, 1, bk)
+        for n in range(NT):
+            store(n, 1, "vs"[n % 2])

@@ -190,7 +190,7 @@ def tile_list_cardinality_margin_corrections_kernel(
         hb_of = {}
 
         def hidden(c, b, banks):
-            act = sb("act%d%d" % (c, b), [P, PACK, W], F32)
+            act = shared("act%d%d" % (c, b), [P, PACK, W], F32, 16 * W)
             hb = shared("hb%d%d" % (c, b), [P, W, PACK], BF16, 8 * W)
             per = PACK // len(banks)
             for i, bk in enumerate(banks):
@@ -269,17 +269,19 @@ def tile_list_cardinality_margin_corrections_kernel(
                     start=(a == 0),
                     stop=False,
                 )
-            for b in range(JP):
-                for i in range(2):
-                    nc.tensor.matmul_mx(
-                        out=acc[n, h][:, chunk(i)],
-                        lhsT=wq[n, b].bitcast(FP8X4),
-                        lhsT_scale=ws[n][:, b * P : (b + 1) * P],
-                        rhs=hq[2 * h + i, b][:].bitcast(FP8X4),
-                        rhs_scale=hs[b][:, chunk(2 * h + i)],
-                        start=False,
-                        stop=(b == JP - 1 and i == 1),
-                    )
+            for b, i in ((0, 0), (0, 1), (1, 0)):
+                down(n, h, b, i)
+
+        def down(n, h, b, i):
+            nc.tensor.matmul_mx(
+                out=acc[n, h][:, chunk(i)],
+                lhsT=wq[n, b].bitcast(FP8X4),
+                lhsT_scale=ws[n][:, b * P : (b + 1) * P],
+                rhs=hq[2 * h + i, b][:].bitcast(FP8X4),
+                rhs_scale=hs[b][:, chunk(2 * h + i)],
+                start=False,
+                stop=(b == JP - 1 and i == 1),
+            )
 
         def store(n, h, eng, over=None, shift=0):
             res = shared("res%d%d" % (n, h), [P, BANK], F32, 4 * BANK, over, shift)
@@ -306,8 +308,8 @@ def tile_list_cardinality_margin_corrections_kernel(
             c = n + 1
             gather_wd(n, 0, JP, "xb%d1" % n if n else None, TURN_BANK)
             quant_h(n // 2 if n else 0, n % 2 if n < 2 else 1, "wd%d" % n)
-            for a in range(KP):
-                cast_x(c, a, "g")
+            cast_x(c, 0, "g")
+            cast_x(c, 1, "v")
             quant_x(c)
             sign_wd(n, 0, JP, "xr%d1" % c)
             if n:
@@ -317,18 +319,22 @@ def tile_list_cardinality_margin_corrections_kernel(
             hidden(c, 1, SCORE_BANKS[2:4])
         for n in range(NT - 1):
             sums(n, 0, SUM_BANKS[n])
-        gather_wd(3, 0, JP, "xb31", TURN_BANK)
+            down(n, 0, 1, 1)
+        gather_wd(3, 0, JP, "xb31", SCORE_BANKS[3])
         quant_h(2, 1, "wd3")
+        store(0, 0, "v", "wd3", 8 * W)
         sign_wd(3, 0, JP)
-        store(0, 0, "v", "wd3", 4 * W)
+        quant_h(3, 0, "wg30")
         quant_wd(3, 0, JP)
-        quant_h(3, 0, "wb30")
-        store(1, 0, "v", "wd3", 12 * W)
-        store(2, 0, "v", "wd3", 20 * W)
+        quant_h(3, 1, "wb30")
+        store(1, 0, "s", "act31")
+        store(2, 0, "s", "act31", 4 * BANK)
         sums(3, 0, TURN_BANK)
-        quant_h(3, 1, "wb30", 4 * W)
-        store(3, 0, "s")
+        down(3, 0, 1, 1)
+        store(3, 0, "v")
         for n, bk in enumerate((SCORE_BANKS[0], SCORE_BANKS[1], SUM_BANKS[0], SCORE_BANKS[2])):
             sums(n, 1, bk)
+        for n in range(NT):
+            down(n, 1, 1, 1)
         for n in range(NT):
             store(n, 1, "vs"[n % 2])

@@ -315,24 +315,29 @@ def tile_list_cardinality_margin_corrections_kernel(
             if n:
                 quant_h(n, 0, "xr%d1" % c, 8 * W)
             quant_wd(n, 0, JP)
+            if c == NC - 1:
+                for m in range(2):
+                    sums(m, 0, SUM_BANKS[m])
+                    down(m, 0, 1, 1)
+                    store(m, 0, "s", "act21", m * 4 * BANK)
             hidden(c, 0, SCORE_BANKS[0:2])
             hidden(c, 1, SCORE_BANKS[2:4])
-        for n in range(NT - 1):
-            sums(n, 0, SUM_BANKS[n])
-            down(n, 0, 1, 1)
-        gather_wd(3, 0, JP, "xb31", SCORE_BANKS[3])
-        quant_h(2, 1, "wd3")
-        store(0, 0, "v", "wd3", 8 * W)
-        sign_wd(3, 0, JP)
-        quant_h(3, 0, "wg30")
-        quant_wd(3, 0, JP)
+        sums(2, 0, SUM_BANKS[2])
+        down(2, 0, 1, 1)
+        gather_wd(3, 0, 1, "xb31", SCORE_BANKS[2])
+        gather_wd(3, 1, 2, None, SCORE_BANKS[3])
+        quant_h(2, 1, "hb20")
+        sign_wd(3, 0, 1)
+        quant_h(3, 0, "wd3")
+        sign_wd(3, 1, 2)
+        quant_wd(3, 0, 1)
+        quant_wd(3, 1, 2)
         quant_h(3, 1, "wb30")
-        store(1, 0, "s", "act31")
-        store(2, 0, "s", "act31", 4 * BANK)
+        store(2, 0, "s", "act31")
         sums(3, 0, TURN_BANK)
         down(3, 0, 1, 1)
-        store(3, 0, "v")
-        for n, bk in enumerate((SCORE_BANKS[0], SCORE_BANKS[1], SUM_BANKS[0], SCORE_BANKS[2])):
+        store(3, 0, "s")
+        for n, bk in enumerate(SUM_BANKS[0:2] + SCORE_BANKS[0:2]):
             sums(n, 1, bk)
         for n in range(NT):
             down(n, 1, 1, 1)

@@ -227,15 +227,13 @@ def tile_list_cardinality_margin_corrections_kernel(
         ws = [sb("ws%d" % n, [P, JP * P], U8) for n in range(NT)]
 
         def gather_wd(n, b0, b1, over, bk):
-            wg = shared("wg%d%d" % (n, b0), [P, b1 - b0, PASS], BF16, 2 * S, over)
+            wg = shared("wg%d%d" % (n, b0), [P, 2, (b1 - b0) * P, 2], BF16, 2 * S, over)
             picks = offsets[:, b0 * (PASS // 16) : b1 * (PASS // 16)]
-            nc.vector.tensor_copy(wg[:].rearrange("p b j -> p (b j)"), wd[n][:].indirect(picks))
+            nc.vector.tensor_copy(wg[:].rearrange("p u i e -> p i u e"), wd[n][:].indirect(picks))
             wt[n, b0] = bank(bk)
-            for b in range(b1 - b0):
-                words = wg[:, b, :].bitcast(F32)
-                for u in range(2):
-                    at = (u * (b1 - b0) + b) * P
-                    nc.tensor.transpose(wt[n, b0][:, at : at + P], words[:, u : 2 * P : 2], ident[:])
+            words = wg[:].rearrange("p u i e -> p (u i e)").bitcast(F32)
+            for at in range(0, 2 * (b1 - b0) * P, P):
+                nc.tensor.transpose(wt[n, b0][:, at : at + P], words[:, at : at + P], ident[:])
 
         def sign_wd(n, b0, b1, over=None):
             nb = b1 - b0

@@ -27,9 +27,8 @@ BANK = 512
 W = 256
 NC = M // W
 TINY = 2.0 ** -100
-SCORE_BANKS = (0, 1, 2, 3)
-TURN_BANK = 4
-SUM_BANKS = (5, 6, 7)
+RING = (0, 1, 2, 3)
+SUMS = (4, 5, 6, 7)
 
 
 def interleaved(dst, src):
@@ -51,68 +50,77 @@ def tile_list_cardinality_margin_corrections_kernel(
         def bank(i):
             return psum.tile([P, BANK], F32, name="bank%d" % i)
 
-        def sb(name, shape, dtype, tag=None):
-            return keep.tile(shape, dtype, name=name, tag=tag or name, align_bytes=64)
+        def sb(name, shape, dtype):
+            return keep.tile(shape, dtype, name=name, align_bytes=64)
 
         place = {"end": 0}
 
-        def shared(name, shape, dtype, size, over=None, shift=0):
+        def shared(name, shape, dtype, size, over=None):
             if over is None:
                 place[name] = place["end"]
                 place["end"] = place["end"] + size
             else:
-                place[name] = place[over] + shift
+                place[name] = place[over[0]] + over[1]
             return reuse.tile(shape, dtype, name=name, align_bytes=64, offset=place[name])
 
-        def list_part(b):
-            return offsets[:, b * (PASS // 16) : (b + 1) * (PASS // 16)]
+        def list_part(b0, b1):
+            return offsets[:, b0 * (PASS // 16) : b1 * (PASS // 16)]
 
         offsets = keep.tile([P, S // 16], U16, name="offsets")
         gain = sb("gain", [P, JP, PACK], F32)
-        tsc = sb("tsc", [P, T], U8)
+        tsc = shared("tsc", [P, T], U8, T)
         w4s = sb("w4s", [P, KP, N], U8)
         w4w = sb("w4w", [P, KP, 2 * N], U8)
         ident = sb("ident", [P, P], F32)
-        tab = [sb("tab%d" % a, [P, T], I32) for a in range(KP)]
+        tab = [shared("tab%d" % a, [P, T], I32, 4 * T) for a in range(KP)]
         wd = [shared("wd%d" % n, [P, T], F32, 4 * T) for n in range(NT)]
         xraw = {(c, a): shared("xr%d%d" % (c, a), [P, PACK, W], F32, 16 * W) for c in range(NC) for a in range(KP)}
 
         nc.vector.memset(tsc[:].bitcast(I32), 0)
         nc.gpsimd.memset(w4s[:].bitcast(I32), 0)
 
-        def load_x(c):
-            for a in range(KP):
+        def load_x(c, passes=range(KP)):
+            for a in passes:
                 rows = x[a * PASS : (a + 1) * PASS, c * W : (c + 1) * W]
                 nc.sync.dma_start(xraw[c, a][:], rows.rearrange("(p i) m -> p i m", i=PACK))
 
         def load_tab(a):
             nc.sync.dma_start(tab[a][:], tab_words[a].rearrange("p t i -> p (t i)").bitcast(I32))
 
+        def load_tab_scales():
+            for q in range(4):
+                nc.sync.dma_start(
+                    tsc[32 * q : 32 * q + 4 * KP, :].bitcast(I32),
+                    tab_scales[:, 4 * q : 4 * q + 4, :].bitcast(I32),
+                )
+
+        def load_gain():
+            nc.sync.dma_start(gain[:], g.rearrange("(b p t) -> p b t", b=JP, t=PACK))
+
         def load_wd(n):
             nc.sync.dma_start(wd[n][:], wdT[n * P : (n + 1) * P, :])
 
+        def load_w4():
+            for q in range(4):
+                nc.sync.dma_start(
+                    w4s[32 * q : 32 * q + 4, :, :].bitcast(I32),
+                    w4_scales[:, 4 * q : 4 * q + 4, :].rearrange("a r c -> r a c").bitcast(I32),
+                )
+            nc.sync.dma_start(w4w[:].bitcast(I32), w4_words.rearrange("a p c -> p a c").bitcast(I32))
+
         nc.sync.dma_start(offsets[:], offs)
-        nc.sync.dma_start(gain[:], g.rearrange("(b p t) -> p b t", b=JP, t=PACK))
-        for q in range(4):
-            nc.sync.dma_start(
-                tsc[32 * q : 32 * q + 4 * KP, :].bitcast(I32),
-                tab_scales[:, 4 * q : 4 * q + 4, :].bitcast(I32),
-            )
+        load_gain()
+        load_tab_scales()
         load_tab(0)
         load_x(0)
         load_tab(1)
-        load_wd(0)
         load_x(1)
-        for q in range(4):
-            nc.sync.dma_start(
-                w4s[32 * q : 32 * q + 4, :, :].bitcast(I32),
-                w4_scales[:, 4 * q : 4 * q + 4, :].rearrange("a r c -> r a c").bitcast(I32),
-            )
-        nc.sync.dma_start(w4w[:].bitcast(I32), w4_words.rearrange("a p c -> p a c").bitcast(I32))
-        load_wd(1)
+        load_wd(0)
         load_x(2)
-        load_wd(2)
+        load_w4()
+        load_wd(1)
         load_x(3)
+        load_wd(2)
         load_wd(3)
         make_identity(nc, ident[:])
 
@@ -120,45 +128,33 @@ def tile_list_cardinality_margin_corrections_kernel(
             return sb(name, [P, JP * PACK], dtype)
 
         root, nroot, sign = small("root"), small("nroot"), small("sign", BF16)
+
         mag, root0, inv, corr, step = small("mag"), small("root0"), small("inv"), small("corr"), small("step")
         gv = gain[:].rearrange("p b t -> p (b t)")
-        nc.vector.scalar_tensor_tensor(mag[:], gv, -1.0, gv, ALU.mult, ALU.max)
-        nc.scalar.activation(root0[:], mag[:], ACT.Sqrt, bias=TINY)
-        nc.vector.tensor_scalar(step[:], gv, 0.0, 2.0, ALU.is_ge, ALU.mult)
-        nc.vector.tensor_scalar_add(sign[:], step[:], -1.0)
-        nc.vector.reciprocal(inv[:], root0[:])
-        nc.vector.scalar_tensor_tensor(corr[:], mag[:], 0.5, inv[:], ALU.mult, ALU.mult)
-        nc.vector.scalar_tensor_tensor(root[:], root0[:], 0.5, corr[:], ALU.mult, ALU.add)
-        nc.scalar.activation(nroot[:], root[:], ACT.Copy, scale=-1.0)
 
         tsg, tsp, tg = {}, {}, {}
 
         def gather_scales(b, over=None):
             tsg[b] = shared("tsg%d" % b, [P, PASS], U8, PASS, over)
-            tsp[b] = sb("tsp%d" % b, [P, PACK, P], U8)
-            nc.vector.tensor_copy(tsg[b][:], tsc[:].indirect(list_part(b)))
+            nc.vector.tensor_copy(tsg[b][:], tsc[:].indirect(list_part(b, b + 1)))
 
-        def sort_scales(b):
+        def sort_scales(b, over=None):
+            tsp[b] = shared("tsp%d" % b, [P, PACK, P], U8, PASS, over)
             nc.vector.tensor_copy(tsp[b][:], tsg[b][:].rearrange("p (i t) -> p t i", t=PACK))
 
         def gather_tab(a, b, over=None):
             tg[a, b] = shared("tg%d%d" % (a, b), [P, PACK, P], U32, 4 * PASS, over)
             nc.vector.tensor_copy(
-                tg[a, b][:].rearrange("p t i -> p i t"), tab[a][:].bitcast(U32).indirect(list_part(b))
+                tg[a, b][:].rearrange("p t i -> p i t"), tab[a][:].bitcast(U32).indirect(list_part(b, b + 1))
             )
 
-        xb = {}
-        xq_half = {}
-        xq = {}
-        xs = [sb("xs%d" % a, [P, M], U8) for a in range(KP)]
-        hq = {}
-        hs = [sb("hs%d" % b, [P, M], U8) for b in range(JP)]
+        xb, xq, xs, hb, hq, hs, act, score = {}, {}, {}, {}, {}, {}, {}, {}
 
         def chunk(c):
             return slice(c * W, (c + 1) * W)
 
-        def cast_x(c, a, engines, over=None, shift=0):
-            xb[c, a] = shared("xb%d%d" % (c, a), [P, W, PACK], BF16, 8 * W, over, shift)[:]
+        def cast_x(c, a, engines, over=None):
+            xb[c, a] = shared("xb%d%d" % (c, a), [P, W, PACK], BF16, 8 * W, over)[:]
             w = W // len(engines)
             for i, eng in enumerate(engines):
                 cols = slice(i * w, (i + 1) * w)
@@ -180,58 +176,75 @@ def tile_list_cardinality_margin_corrections_kernel(
         def quantize(codes, scales, values):
             nc.vector.quantize_mx(codes.bitcast(FP8X4), scales, values.rearrange("p m t -> p (m t)"))
 
-        def quant_x(c):
-            for a in range(KP):
-                if c % 2 == 0:
-                    xq_half[c, a] = shared("xq%d%d" % (c, a), [P, 2 * W], U32, 8 * W, None)
-                xq[c, a] = xq_half[c - c % 2, a][:, chunk(c % 2)]
-                quantize(xq[c, a], xs[a][:, chunk(c)], xb[c, a])
+        def quant_x(c, a, over=None):
+            h = c // 2
+            if c % 2 == 0:
+                xq[h, a] = shared("xq%d%d" % (h, a), [P, BANK], U32, 4 * BANK, over)
+                xs[h, a] = shared("xs%d%d" % (h, a), [P, BANK], U8, BANK)
+            quantize(xq[h, a][:, chunk(c % 2)], xs[h, a][:, chunk(c % 2)], xb[c, a])
 
-        hb_of = {}
-
-        def hidden(c, b, banks):
-            act = shared("act%d%d" % (c, b), [P, PACK, W], F32, 16 * W)
-            hb = shared("hb%d%d" % (c, b), [P, W, PACK], BF16, 8 * W)
-            per = PACK // len(banks)
-            for i, bk in enumerate(banks):
-                z = bank(bk)
-                for u in range(per):
-                    for a in range(KP):
-                        nc.tensor.matmul_mx(
-                            out=z[:, u * W : (u + 1) * W],
-                            lhsT=tg[a, b][:, per * i + u, :].bitcast(FP8X4),
-                            lhsT_scale=tsp[b][4 * a : P, per * i + u, :],
-                            rhs=xq[c, a].bitcast(FP8X4),
-                            rhs_scale=xs[a][:, chunk(c)],
-                            start=(a == 0),
-                            stop=(a == KP - 1),
-                        )
-                for u in range(per):
-                    at = b * PACK + per * i + u
-                    nc.scalar.activation(
-                        act[:, per * i + u, :],
-                        z[:, u * W : (u + 1) * W],
-                        ACT.Relu,
-                        bias=root[:, at : at + 1],
-                        scale=nroot[:, at : at + 1],
+        def scores(u, bk):
+            c, b, i = u // 4, u // 2 % 2, u % 2
+            score[u] = bank(bk)
+            for e in range(2):
+                for a in reversed(range(KP)):
+                    nc.tensor.matmul_mx(
+                        out=score[u][:, chunk(e)],
+                        lhsT=tg[a, b][:, 2 * i + e, :].bitcast(FP8X4),
+                        lhsT_scale=tsp[b][4 * a : P, 2 * i + e, :],
+                        rhs=xq[c // 2, a][:, chunk(c % 2)].bitcast(FP8X4),
+                        rhs_scale=xs[c // 2, a][:, chunk(c % 2)],
+                        start=(a == KP - 1),
+                        stop=(a == 0),
                     )
-            dst, src = interleaved(hb[:], act[:])
+
+        def first_scores(a, b, banks):
+            for t in range(PACK):
+                if a == 0:
+                    score[b, t] = bank(banks[t])
+                nc.tensor.matmul_mx(
+                    out=score[b, t][:, 0:W],
+                    lhsT=tg[a, b][:, t, :].bitcast(FP8X4),
+                    lhsT_scale=tsp[b][4 * a : P, t, :],
+                    rhs=xq[0, a][:, 0:W].bitcast(FP8X4),
+                    rhs_scale=xs[0, a][:, 0:W],
+                    start=(a == 0),
+                    stop=(a == KP - 1),
+                )
+
+        def hinge(u, over=None):
+            r, i = u // 2, u % 2
+            if i == 0:
+                act[r] = shared("act%d" % r, [P, PACK, W], F32, 16 * W, over)
+            for e in range(2):
+                at = r % 2 * PACK + 2 * i + e
+                nc.scalar.activation(
+                    act[r][:, 2 * i + e, :],
+                    score[u][:, chunk(e)] if u in score else score[r, 2 * i + e][:, 0:W],
+                    ACT.Relu,
+                    bias=root[:, at : at + 1],
+                    scale=nroot[:, at : at + 1],
+                )
+
+        def square(r, over=None):
+            hb[r] = shared("hb%d" % r, [P, W, PACK], BF16, 8 * W, over)
+            dst, src = interleaved(hb[r][:], act[r][:])
             nc.scalar.activation(dst, src, ACT.Square)
-            hb_of[c, b] = hb
 
-        def quant_h(c, b, over, shift=0):
-            hq[c, b] = shared("hq%d%d" % (c, b), [P, W], U32, 4 * W, over, shift)
-            quantize(hq[c, b][:], hs[b][:, chunk(c)], hb_of[c, b][:])
+        def quant_h(r, over=None, over_s=None):
+            hq[r] = shared("hq%d" % r, [P, W], U32, 4 * W, over)
+            hs[r] = shared("hs%d" % r, [P, W], U8, W, over_s)
+            quantize(hq[r][:], hs[r][:], hb[r][:])
 
-        wt, wb, wq = {}, {}, {}
-        ws = [sb("ws%d" % n, [P, JP * P], U8) for n in range(NT)]
+        wg, wt, wb, wq, ws = {}, {}, {}, {}, {}
 
-        def gather_wd(n, b0, b1, over, bk):
-            wg = shared("wg%d%d" % (n, b0), [P, 2, (b1 - b0) * P, 2], BF16, 2 * S, over)
-            picks = offsets[:, b0 * (PASS // 16) : b1 * (PASS // 16)]
-            nc.vector.tensor_copy(wg[:].rearrange("p u i e -> p i u e"), wd[n][:].indirect(picks))
+        def gather_wd(n, b0, b1, over=None):
+            wg[n, b0] = shared("wg%d%d" % (n, b0), [P, 2, (b1 - b0) * P, 2], BF16, 2 * S, over)
+            nc.vector.tensor_copy(wg[n, b0][:].rearrange("p u i e -> p i u e"), wd[n][:].indirect(list_part(b0, b1)))
+
+        def turn_wd(n, b0, b1, bk):
             wt[n, b0] = bank(bk)
-            words = wg[:].rearrange("p u i e -> p (u i e)").bitcast(F32)
+            words = wg[n, b0][:].rearrange("p u i e -> p (u i e)").bitcast(F32)
             for at in range(0, 2 * (b1 - b0) * P, P):
                 nc.tensor.transpose(wt[n, b0][:, at : at + P], words[:, at : at + P], ident[:])
 
@@ -247,97 +260,184 @@ def tile_list_cardinality_margin_corrections_kernel(
                 ALU.mult,
             )
 
-        def quant_wd(n, b0, b1, over=None, shift=0):
-            codes = shared("wq%d%d" % (n, b0), [P, (b1 - b0) * P], U32, 4 * JP * P, over, shift)
-            quantize(codes[:], ws[n][:, b0 * P : b1 * P], wb[n, b0][:])
+        def quant_wd(n, b0, b1, over=None, over_s=None):
+            codes = shared("wq%d%d" % (n, b0), [P, (b1 - b0) * P], U32, 4 * JP * P, over)
+            scales = shared("ws%d%d" % (n, b0), [P, (b1 - b0) * P], U8, JP * P, over_s)
+            quantize(codes[:], scales[:], wb[n, b0][:])
             for b in range(b0, b1):
                 wq[n, b] = codes[:, (b - b0) * P : (b - b0 + 1) * P]
+                ws[n, b] = scales[:, (b - b0) * P : (b - b0 + 1) * P]
 
         acc = {}
 
-        def sums(n, h, bk):
+        def base(n, h, bk):
             acc[n, h] = bank(bk)
-            for a in range(KP):
+            for a in reversed(range(KP)):
                 nc.tensor.matmul_mx(
                     out=acc[n, h][:],
                     lhsT=w4w[:, a, 2 * n * P : 2 * (n + 1) * P].bitcast(FP4X4),
                     lhsT_scale=w4s[:, a, n * P : (n + 1) * P],
-                    rhs=xq_half[2 * h, a][:].bitcast(FP8X4),
-                    rhs_scale=xs[a][:, h * BANK : (h + 1) * BANK],
-                    start=(a == 0),
+                    rhs=xq[h, a][:].bitcast(FP8X4),
+                    rhs_scale=xs[h, a][:],
+                    start=(a == KP - 1),
                     stop=False,
                 )
-            for b, i in ((0, 0), (0, 1), (1, 0)):
-                down(n, h, b, i)
 
-        def down(n, h, b, i):
-            nc.tensor.matmul_mx(
-                out=acc[n, h][:, chunk(i)],
-                lhsT=wq[n, b].bitcast(FP8X4),
-                lhsT_scale=ws[n][:, b * P : (b + 1) * P],
-                rhs=hq[2 * h + i, b][:].bitcast(FP8X4),
-                rhs_scale=hs[b][:, chunk(2 * h + i)],
-                start=False,
-                stop=(b == JP - 1 and i == 1),
-            )
+        def down(n, rs, last):
+            for r in rs:
+                c, b = r // 2, r % 2
+                nc.tensor.matmul_mx(
+                    out=acc[n, c // 2][:, chunk(c % 2)],
+                    lhsT=wq[n, b].bitcast(FP8X4),
+                    lhsT_scale=ws[n, b],
+                    rhs=hq[r][:].bitcast(FP8X4),
+                    rhs_scale=hs[r][:],
+                    start=False,
+                    stop=(last and r == rs[-1]),
+                )
 
-        def store(n, h, eng, over=None, shift=0):
-            res = shared("res%d%d" % (n, h), [P, BANK], F32, 4 * BANK, over, shift)
+        def store(n, h, eng, over=None):
+            res = shared("res%d%d" % (n, h), [P, BANK], F32, 4 * BANK, over)
             if eng == "s":
                 nc.scalar.copy(res[:], acc[n, h][:])
             else:
                 nc.vector.tensor_copy(res[:], acc[n, h][:])
             nc.sync.dma_start(out[n * P : (n + 1) * P, h * BANK : (h + 1) * BANK], res[:])
 
-        for b in range(JP):
-            gather_scales(b)
-        for b in range(JP):
-            sort_scales(b)
-        for b in range(JP):
-            gather_tab(0, b)
-        for a in range(KP):
-            cast_x(0, a, "s")
-        quant_x(0)
-        for b in range(JP):
-            gather_tab(1, b)
-        hidden(0, 0, (TURN_BANK,) + SCORE_BANKS[0:3])
-        hidden(0, 1, SCORE_BANKS[3:4] + SUM_BANKS)
-        for n in range(NT - 1):
-            c = n + 1
-            gather_wd(n, 0, JP, "xb%d1" % n if n else None, TURN_BANK)
-            quant_h(n // 2 if n else 0, n % 2 if n < 2 else 1, "wd%d" % n)
-            cast_x(c, 0, "g")
-            cast_x(c, 1, "v")
-            quant_x(c)
-            sign_wd(n, 0, JP, "xr%d1" % c)
-            if n:
-                quant_h(n, 0, "xr%d1" % c, 8 * W)
-            quant_wd(n, 0, JP)
-            if c == NC - 1:
-                for m in range(2):
-                    sums(m, 0, SUM_BANKS[m])
-                    down(m, 0, 1, 1)
-                    store(m, 0, "s", "act21", m * 4 * BANK)
-            hidden(c, 0, SCORE_BANKS[0:2])
-            hidden(c, 1, SCORE_BANKS[2:4])
-        sums(2, 0, SUM_BANKS[2])
-        down(2, 0, 1, 1)
-        gather_wd(3, 0, 1, "xb31", SCORE_BANKS[2])
-        gather_wd(3, 1, 2, None, SCORE_BANKS[3])
-        quant_h(2, 1, "hb20")
+        turn = {"next": 0}
+
+        def ring():
+            bk = RING[turn["next"] % len(RING)]
+            turn["next"] = turn["next"] + 1
+            return bk
+
+        def unit(u):
+            scores(u, ring())
+            hinge(u)
+
+        nc.vector.scalar_tensor_tensor(mag[:], gv, -1.0, gv, ALU.mult, ALU.max)
+        nc.vector.tensor_scalar(step[:], gv, 0.0, 2.0, ALU.is_ge, ALU.mult)
+        nc.scalar.activation(root0[:], mag[:], ACT.Sqrt, bias=TINY)
+        gather_scales(0)
+        nc.vector.tensor_scalar_add(sign[:], step[:], -1.0)
+        nc.vector.reciprocal(inv[:], root0[:])
+        gather_scales(1)
+        nc.vector.scalar_tensor_tensor(corr[:], mag[:], 0.5, inv[:], ALU.mult, ALU.mult)
+        sort_scales(0)
+        nc.vector.scalar_tensor_tensor(root[:], root0[:], 0.5, corr[:], ALU.mult, ALU.add)
+        sort_scales(1)
+        nc.scalar.activation(nroot[:], root[:], ACT.Copy, scale=-1.0)
+        gather_tab(0, 0)
+        gather_tab(0, 1)
+        cast_x(0, 0, "s")
+        cast_x(0, 1, "s")
+        quant_x(0, 0)
+        quant_x(0, 1)
+        first_scores(0, 0, RING)
+        first_scores(0, 1, SUMS)
+        gather_tab(1, 0, ("xb00", 0))
+        gather_tab(1, 1, ("xb01", 0))
+        first_scores(1, 0, None)
+        first_scores(1, 1, None)
+
+        hinge(0)
+        hinge(1)
+        hinge(2)
+        square(0)
+        hinge(3)
+        cast_x(1, 0, "g")
+        cast_x(1, 1, "v")
+        quant_x(1, 0)
+        quant_x(1, 1)
+        unit(4)
+        square(1)
+        unit(5)
+        unit(6)
+        square(2)
+        gather_wd(0, 0, 2, ("xb10", 0))
+        cast_x(2, 0, "g")
+        cast_x(2, 1, "v")
+        unit(7)
+        turn_wd(0, 0, 2, ring())
+        quant_x(2, 0)
+        quant_x(2, 1)
+        sign_wd(0, 0, 2, ("xb20", 0))
+        quant_h(0, ("xb21", 0))
+        quant_wd(0, 0, 2)
+        quant_h(1, ("xb21", 4 * W))
+        quant_h(2, ("hb0", 0))
+        unit(8)
+        square(3)
+        base(0, 0, SUMS[0])
+        unit(9)
+        base(1, 0, SUMS[1])
+        unit(10)
+        square(4)
+        base(2, 0, SUMS[2])
+        gather_wd(1, 0, 2, ("hb1", 0))
+        cast_x(3, 0, "g")
+        cast_x(3, 1, "v")
+        unit(11)
+        square(5)
+        base(3, 0, SUMS[3])
+        down(0, [0, 1, 2], False)
+        turn_wd(1, 0, 2, ring())
+        quant_x(3, 0)
+        quant_x(3, 1)
+        quant_h(3, ("xb30", 0))
+        sign_wd(1, 0, 2, ("xb31", 0))
+        unit(12)
+        down(0, [3], True)
+        store(0, 0, "s")
+        quant_h(4, ("hb3", 0))
+        quant_wd(1, 0, 2)
+        unit(13)
+        unit(14)
+        down(1, [0, 1, 2, 3], True)
+        store(1, 0, "s")
+        square(6)
+        unit(15)
+        square(7)
+        gather_wd(2, 0, 1, ("hb4", 0))
+        gather_wd(2, 1, 2)
+        turn_wd(2, 0, 1, ring())
+        base(0, 1, SUMS[0])
+        turn_wd(2, 1, 2, ring())
+        sign_wd(2, 0, 1)
+        quant_h(5, ("wb10", 0))
+        quant_wd(2, 0, 1)
+        sign_wd(2, 1, 2)
+        quant_wd(2, 1, 2)
+        base(1, 1, SUMS[1])
+        base(2, 1, ring())
+        down(0, [4, 5], False)
+        down(1, [4, 5], False)
+        down(2, [0, 2, 1, 3], True)
+        gather_wd(3, 0, 1)
+        quant_h(6, ("wb21", 0))
+        gather_wd(3, 1, 2)
+        last = ring()
+        turn_wd(3, 0, 1, ring())
+        base(3, 1, last)
+        down(2, [4, 5, 6], False)
+        down(0, [6], False)
+        down(1, [6], False)
+        turn_wd(3, 1, 2, ring())
         sign_wd(3, 0, 1)
-        quant_h(3, 0, "wd3")
-        sign_wd(3, 1, 2)
+        quant_h(7, ("wd3", 0))
         quant_wd(3, 0, 1)
+        sign_wd(3, 1, 2)
         quant_wd(3, 1, 2)
-        quant_h(3, 1, "wb30")
-        store(2, 0, "s", "act31")
-        sums(3, 0, TURN_BANK)
-        down(3, 0, 1, 1)
+        down(0, [7], True)
+        down(1, [7], True)
+        down(2, [7], True)
+        down(3, [0, 2], False)
+        down(3, [4, 6], False)
+        down(3, [1, 3], True)
+        down(3, [5, 7], True)
+        store(2, 0, "s", ("act7", 0))
+        store(0, 1, "s")
+        store(1, 1, "s")
+        store(2, 1, "v")
         store(3, 0, "s")
-        for n, bk in enumerate(SUM_BANKS[0:2] + SCORE_BANKS[0:2]):
-            sums(n, 1, bk)
-        for n in range(NT):
-            down(n, 1, 1, 1)
-        for n in range(NT):
-            store(n, 1, "vs"[n % 2])
+        store(3, 1, "v")

@@ -27,8 +27,8 @@ BANK = 512
 W = 256
 NC = M // W
 TINY = 2.0 ** -100
-RING = (0, 1, 2, 3)
-SUMS = (4, 5, 6, 7)
+RING = (0, 1, 2)
+SUMS = (3, 4, 5, 6, 7)
 
 
 def interleaved(dst, src):
@@ -116,8 +116,8 @@ def tile_list_cardinality_margin_corrections_kernel(
         load_tab(1)
         load_x(1)
         load_wd(0)
-        load_x(2)
         load_w4()
+        load_x(2)
         load_wd(1)
         load_x(3)
         load_wd(2)
@@ -127,26 +127,31 @@ def tile_list_cardinality_margin_corrections_kernel(
         def small(name, dtype=F32):
             return sb(name, [P, JP * PACK], dtype)
 
-        root, nroot, sign = small("root"), small("nroot"), small("sign", BF16)
+        root, nroot = small("root"), small("nroot")
 
-        mag, root0, inv, corr, step = small("mag"), small("root0"), small("inv"), small("corr"), small("step")
+        root0, corr = small("root0"), small("corr")
+        mag = shared("mag", [P, JP * PACK], F32, 64)
+        inv = shared("inv", [P, JP * PACK], F32, 64, ("tsc", 0))
+        sign = shared("sign", [P, JP * PACK], BF16, 64, ("mag", 0))
         gv = gain[:].rearrange("p b t -> p (b t)")
 
         tsg, tsp, tg = {}, {}, {}
 
-        def gather_scales(b, over=None):
-            tsg[b] = shared("tsg%d" % b, [P, PASS], U8, PASS, over)
+        def gather_scales(b):
+            tsg[b] = sb("tsg%d" % b, [P, PASS], U8)
             nc.vector.tensor_copy(tsg[b][:], tsc[:].indirect(list_part(b, b + 1)))
 
-        def sort_scales(b, over=None):
-            tsp[b] = shared("tsp%d" % b, [P, PACK, P], U8, PASS, over)
+        def sort_scales(b):
+            tsp[b] = sb("tsp%d" % b, [P, PACK, P], U8)
             nc.vector.tensor_copy(tsp[b][:], tsg[b][:].rearrange("p (i t) -> p t i", t=PACK))
 
-        def gather_tab(a, b, over=None):
-            tg[a, b] = shared("tg%d%d" % (a, b), [P, PACK, P], U32, 4 * PASS, over)
+        def gather_tab(a, b0, b1, over=None):
+            words = shared("tg%d%d" % (a, b0), [P, b1 - b0, PACK, P], U32, 4 * PASS * (b1 - b0), over)
             nc.vector.tensor_copy(
-                tg[a, b][:].rearrange("p t i -> p i t"), tab[a][:].bitcast(U32).indirect(list_part(b, b + 1))
+                words[:].rearrange("p b t i -> p b i t"), tab[a][:].bitcast(U32).indirect(list_part(b0, b1))
             )
+            for b in range(b0, b1):
+                tg[a, b] = words[:, b - b0]
 
         xb, xq, xs, hb, hq, hs, act, score = {}, {}, {}, {}, {}, {}, {}, {}
 
@@ -226,10 +231,16 @@ def tile_list_cardinality_margin_corrections_kernel(
                     scale=nroot[:, at : at + 1],
                 )
 
-        def square(r, over=None):
+        def square(r, eng="s", over=None):
             hb[r] = shared("hb%d" % r, [P, W, PACK], BF16, 8 * W, over)
             dst, src = interleaved(hb[r][:], act[r][:])
-            nc.scalar.activation(dst, src, ACT.Square)
+            if eng == "s":
+                nc.scalar.activation(dst, src, ACT.Square)
+            elif eng == "v":
+                nc.vector.tensor_tensor(dst, src, src, ALU.mult)
+            else:
+                src = act[r][:].rearrange("p t m -> p m t")
+                nc.gpsimd.tensor_tensor(hb[r][:], src, src, ALU.mult)
 
         def quant_h(r, over=None, over_s=None):
             hq[r] = shared("hq%d" % r, [P, W], U32, 4 * W, over)
@@ -271,10 +282,12 @@ def tile_list_cardinality_margin_corrections_kernel(
         acc = {}
 
         def base(n, h, bk):
-            acc[n, h] = bank(bk)
+            tile = bank(bk)
+            for i in range(2):
+                acc[n, 2 * h + i] = tile[:, chunk(i)]
             for a in reversed(range(KP)):
                 nc.tensor.matmul_mx(
-                    out=acc[n, h][:],
+                    out=tile[:],
                     lhsT=w4w[:, a, 2 * n * P : 2 * (n + 1) * P].bitcast(FP4X4),
                     lhsT_scale=w4s[:, a, n * P : (n + 1) * P],
                     rhs=xq[h, a][:].bitcast(FP8X4),
@@ -282,12 +295,32 @@ def tile_list_cardinality_margin_corrections_kernel(
                     start=(a == KP - 1),
                     stop=False,
                 )
+            return tile
+
+        def base_pair(n0, c, bk):
+            tile = bank(bk)
+            for i in range(2):
+                n = n0 + i
+                acc[n, c] = tile[:, chunk(i)]
+                for a in reversed(range(KP)):
+                    for e in range(0, W, P):
+                        cols = slice(c % 2 * W + e, c % 2 * W + e + P)
+                        nc.tensor.matmul_mx(
+                            out=tile[:, i * W + e : i * W + e + P],
+                            lhsT=w4w[:, a, 2 * n * P : 2 * (n + 1) * P].bitcast(FP4X4),
+                            lhsT_scale=w4s[:, a, n * P : (n + 1) * P],
+                            rhs=xq[c // 2, a][:, cols].bitcast(FP8X4),
+                            rhs_scale=xs[c // 2, a][:, cols],
+                            start=(i == 0 and a == KP - 1 and e == 0),
+                            stop=False,
+                        )
+            return tile
 
         def down(n, rs, last):
             for r in rs:
                 c, b = r // 2, r % 2
                 nc.tensor.matmul_mx(
-                    out=acc[n, c // 2][:, chunk(c % 2)],
+                    out=acc[n, c],
                     lhsT=wq[n, b].bitcast(FP8X4),
                     lhsT_scale=ws[n, b],
                     rhs=hq[r][:].bitcast(FP8X4),
@@ -296,13 +329,19 @@ def tile_list_cardinality_margin_corrections_kernel(
                     stop=(last and r == rs[-1]),
                 )
 
-        def store(n, h, eng, over=None):
-            res = shared("res%d%d" % (n, h), [P, BANK], F32, 4 * BANK, over)
+        def store(name, tile, dst, eng, over=None):
+            res = shared(name, [P, BANK], F32, 4 * BANK, over)
             if eng == "s":
-                nc.scalar.copy(res[:], acc[n, h][:])
+                nc.scalar.copy(res[:], tile[:])
             else:
-                nc.vector.tensor_copy(res[:], acc[n, h][:])
-            nc.sync.dma_start(out[n * P : (n + 1) * P, h * BANK : (h + 1) * BANK], res[:])
+                nc.vector.tensor_copy(res[:], tile[:])
+            nc.sync.dma_start(dst, res[:].rearrange("p (n m) -> p n m", n=dst.shape[1]))
+
+        def rows(n, h):
+            return out[n * P : (n + 1) * P, h * BANK : (h + 1) * BANK].rearrange("p (n m) -> p n m", n=1)
+
+        def pair_rows(n0, c):
+            return out[n0 * P : (n0 + 2) * P, chunk(c)].rearrange("(n p) m -> p n m", n=2)
 
         turn = {"next": 0}
 
@@ -316,27 +355,26 @@ def tile_list_cardinality_margin_corrections_kernel(
             hinge(u)
 
         nc.vector.scalar_tensor_tensor(mag[:], gv, -1.0, gv, ALU.mult, ALU.max)
-        nc.vector.tensor_scalar(step[:], gv, 0.0, 2.0, ALU.is_ge, ALU.mult)
         nc.scalar.activation(root0[:], mag[:], ACT.Sqrt, bias=TINY)
         gather_scales(0)
-        nc.vector.tensor_scalar_add(sign[:], step[:], -1.0)
-        nc.vector.reciprocal(inv[:], root0[:])
         gather_scales(1)
-        nc.vector.scalar_tensor_tensor(corr[:], mag[:], 0.5, inv[:], ALU.mult, ALU.mult)
         sort_scales(0)
-        nc.vector.scalar_tensor_tensor(root[:], root0[:], 0.5, corr[:], ALU.mult, ALU.add)
+        nc.vector.reciprocal(inv[:], root0[:])
         sort_scales(1)
-        nc.scalar.activation(nroot[:], root[:], ACT.Copy, scale=-1.0)
-        gather_tab(0, 0)
-        gather_tab(0, 1)
+        nc.vector.scalar_tensor_tensor(corr[:], mag[:], 0.5, inv[:], ALU.mult, ALU.mult)
+        gather_tab(0, 0, 1)
+        nc.scalar.activation(sign[:], gv, ACT.Sign)
+        nc.vector.scalar_tensor_tensor(root[:], root0[:], 0.5, corr[:], ALU.mult, ALU.add)
+        nc.vector.scalar_tensor_tensor(nroot[:], root0[:], -0.5, corr[:], ALU.mult, ALU.subtract)
+        gather_tab(0, 1, 2)
         cast_x(0, 0, "s")
         cast_x(0, 1, "s")
         quant_x(0, 0)
         quant_x(0, 1)
-        first_scores(0, 0, RING)
-        first_scores(0, 1, SUMS)
-        gather_tab(1, 0, ("xb00", 0))
-        gather_tab(1, 1, ("xb01", 0))
+        first_scores(0, 0, RING + SUMS[0:1])
+        first_scores(0, 1, SUMS[1:])
+        gather_tab(1, 0, 1, ("xb00", 0))
+        gather_tab(1, 1, 2, ("xb01", 0))
         first_scores(1, 0, None)
         first_scores(1, 1, None)
 
@@ -354,90 +392,86 @@ def tile_list_cardinality_margin_corrections_kernel(
         unit(5)
         unit(6)
         square(2)
+        scores(7, SUMS[0])
+        hinge(7)
         gather_wd(0, 0, 2, ("xb10", 0))
         cast_x(2, 0, "g")
         cast_x(2, 1, "v")
-        unit(7)
-        turn_wd(0, 0, 2, ring())
+        turn_wd(0, 0, 2, SUMS[4])
+        s00 = base(0, 0, SUMS[1])
+        s10 = base(1, 0, SUMS[2])
         quant_x(2, 0)
         quant_x(2, 1)
         sign_wd(0, 0, 2, ("xb20", 0))
         quant_h(0, ("xb21", 0))
         quant_wd(0, 0, 2)
         quant_h(1, ("xb21", 4 * W))
-        quant_h(2, ("hb0", 0))
         unit(8)
         square(3)
-        base(0, 0, SUMS[0])
         unit(9)
-        base(1, 0, SUMS[1])
+        s20 = base(2, 0, SUMS[3])
         unit(10)
         square(4)
-        base(2, 0, SUMS[2])
-        gather_wd(1, 0, 2, ("hb1", 0))
-        cast_x(3, 0, "g")
+        p2 = base_pair(0, 2, SUMS[0])
+        down(0, [0, 1], False)
+        gather_wd(1, 0, 2, ("hb0", 0))
+        cast_x(3, 0, "g", ("hb1", 0))
         cast_x(3, 1, "v")
-        unit(11)
-        square(5)
-        base(3, 0, SUMS[3])
-        down(0, [0, 1, 2], False)
-        turn_wd(1, 0, 2, ring())
+        turn_wd(1, 0, 2, SUMS[4])
         quant_x(3, 0)
         quant_x(3, 1)
-        quant_h(3, ("xb30", 0))
-        sign_wd(1, 0, 2, ("xb31", 0))
-        unit(12)
-        down(0, [3], True)
-        store(0, 0, "s")
-        quant_h(4, ("hb3", 0))
+        sign_wd(1, 0, 2, ("xb30", 0))
+        quant_h(2, ("xb31", 0))
         quant_wd(1, 0, 2)
-        unit(13)
-        unit(14)
+        quant_h(3, ("xb31", 4 * W))
+        unit(11)
+        s30 = base(3, 0, SUMS[4])
+        unit(12)
+        down(0, [2, 3], True)
         down(1, [0, 1, 2, 3], True)
-        store(1, 0, "s")
+        store("res00", s00, rows(0, 0), "s")
+        square(5)
+        unit(13)
+        store("res10", s10, rows(1, 0), "s")
+        unit(14)
         square(6)
         unit(15)
         square(7)
-        gather_wd(2, 0, 1, ("hb4", 0))
-        gather_wd(2, 1, 2)
-        turn_wd(2, 0, 1, ring())
-        base(0, 1, SUMS[0])
-        turn_wd(2, 1, 2, ring())
-        sign_wd(2, 0, 1)
-        quant_h(5, ("wb10", 0))
-        quant_wd(2, 0, 1)
-        sign_wd(2, 1, 2)
-        quant_wd(2, 1, 2)
-        base(1, 1, SUMS[1])
-        base(2, 1, ring())
-        down(0, [4, 5], False)
-        down(1, [4, 5], False)
-        down(2, [0, 2, 1, 3], True)
-        gather_wd(3, 0, 1)
-        quant_h(6, ("wb21", 0))
+        p3 = base_pair(0, 3, SUMS[1])
+        s21 = base(2, 1, SUMS[2])
+        gather_wd(2, 0, 2, ("hb2", 0))
+        turn_wd(2, 0, 2, RING[2])
+        quant_h(4, ("hb3", 0))
+        quant_h(5, ("wd2", 0))
+        sign_wd(2, 0, 2, ("wd2", 8 * W))
+        gather_wd(3, 0, 1, ("hb4", 0))
+        quant_wd(2, 0, 2, ("hb5", 0))
         gather_wd(3, 1, 2)
-        last = ring()
-        turn_wd(3, 0, 1, ring())
-        base(3, 1, last)
-        down(2, [4, 5, 6], False)
-        down(0, [6], False)
-        down(1, [6], False)
-        turn_wd(3, 1, 2, ring())
-        sign_wd(3, 0, 1)
-        quant_h(7, ("wd3", 0))
+        down(0, [4, 5], False)
+        down(1, [4, 5], True)
+        turn_wd(3, 0, 1, RING[0])
+        down(2, [0, 2, 1, 3], True)
+        down(2, [4, 5], False)
+        turn_wd(3, 1, 2, RING[2])
+        s31 = base(3, 1, RING[1])
+        quant_h(6, ("wb20", 0))
+        sign_wd(3, 0, 1, ("wd3", 0))
         quant_wd(3, 0, 1)
         sign_wd(3, 1, 2)
+        quant_h(7, ("wb30", 0))
         quant_wd(3, 1, 2)
-        down(0, [7], True)
-        down(1, [7], True)
-        down(2, [7], True)
+        for n in range(3):
+            down(n, [6], False)
         down(3, [0, 2], False)
         down(3, [4, 6], False)
+        down(0, [7], False)
+        down(1, [7], True)
+        down(2, [7], True)
         down(3, [1, 3], True)
         down(3, [5, 7], True)
-        store(2, 0, "s", ("act7", 0))
-        store(0, 1, "s")
-        store(1, 1, "s")
-        store(2, 1, "v")
-        store(3, 0, "s")
-        store(3, 1, "v")
+        store("resp2", p2, pair_rows(0, 2), "s", ("act7", 0))
+        store("res20", s20, rows(2, 0), "s", ("act7", 4 * BANK))
+        store("resp3", p3, pair_rows(0, 3), "v")
+        store("res21", s21, rows(2, 1), "s")
+        store("res30", s30, rows(3, 0), "v")
+        store("res31", s31, rows(3, 1), "s")

@@ -100,12 +100,14 @@ def tile_list_cardinality_margin_corrections_kernel(
         def load_wd(n):
             nc.sync.dma_start(wd[n][:], wdT[n * P : (n + 1) * P, :])
 
-        def load_w4():
+        def load_w4_scales():
             for q in range(4):
                 nc.sync.dma_start(
                     w4s[32 * q : 32 * q + 4, :, :].bitcast(I32),
                     w4_scales[:, 4 * q : 4 * q + 4, :].rearrange("a r c -> r a c").bitcast(I32),
                 )
+
+        def load_w4_words():
             nc.sync.dma_start(w4w[:].bitcast(I32), w4_words.rearrange("a p c -> p a c").bitcast(I32))
 
         nc.sync.dma_start(offsets[:], offs)
@@ -114,10 +116,11 @@ def tile_list_cardinality_margin_corrections_kernel(
         load_tab(0)
         load_x(0)
         load_tab(1)
+        load_w4_scales()
         load_x(1)
         load_wd(0)
-        load_w4()
         load_x(2)
+        load_w4_words()
         load_wd(1)
         load_x(3)
         load_wd(2)
@@ -231,21 +234,19 @@ def tile_list_cardinality_margin_corrections_kernel(
                     scale=nroot[:, at : at + 1],
                 )
 
-        def square(r, eng="s", over=None):
-            hb[r] = shared("hb%d" % r, [P, W, PACK], BF16, 8 * W, over)
-            dst, src = interleaved(hb[r][:], act[r][:])
-            if eng == "s":
-                nc.scalar.activation(dst, src, ACT.Square)
-            elif eng == "v":
-                nc.vector.tensor_tensor(dst, src, src, ALU.mult)
-            else:
-                src = act[r][:].rearrange("p t m -> p m t")
-                nc.gpsimd.tensor_tensor(hb[r][:], src, src, ALU.mult)
+        def square(r):
+            if r % 2 == 0:
+                hb[r // 2] = shared("hb%d" % (r // 2), [P, JP, W, PACK], BF16, 8 * W * JP)
+            dst, src = interleaved(hb[r // 2][:, r % 2], act[r][:])
+            nc.scalar.activation(dst, src, ACT.Square)
 
-        def quant_h(r, over=None, over_s=None):
-            hq[r] = shared("hq%d" % r, [P, W], U32, 4 * W, over)
-            hs[r] = shared("hs%d" % r, [P, W], U8, W, over_s)
-            quantize(hq[r][:], hs[r][:], hb[r][:])
+        def quant_h(c, over=None):
+            codes = shared("hq%d" % c, [P, JP * W], U32, 4 * W * JP, over)
+            scales = shared("hs%d" % c, [P, JP * W], U8, W * JP)
+            quantize(codes[:], scales[:], hb[c][:].rearrange("p b m t -> p (b m) t"))
+            for b in range(JP):
+                hq[2 * c + b] = codes[:, chunk(b)]
+                hs[2 * c + b] = scales[:, chunk(b)]
 
         wg, wt, wb, wq, ws = {}, {}, {}, {}, {}
 
@@ -323,8 +324,8 @@ def tile_list_cardinality_margin_corrections_kernel(
                     out=acc[n, c],
                     lhsT=wq[n, b].bitcast(FP8X4),
                     lhsT_scale=ws[n, b],
-                    rhs=hq[r][:].bitcast(FP8X4),
-                    rhs_scale=hs[r][:],
+                    rhs=hq[r].bitcast(FP8X4),
+                    rhs_scale=hs[r],
                     start=False,
                     stop=(last and r == rs[-1]),
                 )
@@ -405,7 +406,6 @@ def tile_list_cardinality_margin_corrections_kernel(
         sign_wd(0, 0, 2, ("xb20", 0))
         quant_h(0, ("xb21", 0))
         quant_wd(0, 0, 2)
-        quant_h(1, ("xb21", 4 * W))
         unit(8)
         square(3)
         unit(9)
@@ -415,15 +415,14 @@ def tile_list_cardinality_margin_corrections_kernel(
         p2 = base_pair(0, 2, SUMS[0])
         down(0, [0, 1], False)
         gather_wd(1, 0, 2, ("hb0", 0))
-        cast_x(3, 0, "g", ("hb1", 0))
+        cast_x(3, 0, "g", ("wb00", 0))
         cast_x(3, 1, "v")
         turn_wd(1, 0, 2, SUMS[4])
         quant_x(3, 0)
         quant_x(3, 1)
         sign_wd(1, 0, 2, ("xb30", 0))
-        quant_h(2, ("xb31", 0))
+        quant_h(1, ("xb31", 0))
         quant_wd(1, 0, 2)
-        quant_h(3, ("xb31", 4 * W))
         unit(11)
         s30 = base(3, 0, SUMS[4])
         unit(12)
@@ -435,43 +434,40 @@ def tile_list_cardinality_margin_corrections_kernel(
         store("res10", s10, rows(1, 0), "s")
         unit(14)
         square(6)
-        unit(15)
+        gather_wd(2, 0, 2, ("hb1", 0))
+        turn_wd(2, 0, 2, RING[1])
+        scores(15, RING[2])
+        hinge(15)
         square(7)
         p3 = base_pair(0, 3, SUMS[1])
         s21 = base(2, 1, SUMS[2])
-        gather_wd(2, 0, 2, ("hb2", 0))
-        turn_wd(2, 0, 2, RING[2])
-        quant_h(4, ("hb3", 0))
-        quant_h(5, ("wd2", 0))
-        sign_wd(2, 0, 2, ("wd2", 8 * W))
-        gather_wd(3, 0, 1, ("hb4", 0))
-        quant_wd(2, 0, 2, ("hb5", 0))
-        gather_wd(3, 1, 2)
+        quant_h(2, ("wb10", 0))
+        sign_wd(2, 0, 2, ("wd2", 0))
+        gather_wd(3, 0, 1, ("wg20", 0))
+        quant_wd(2, 0, 2)
+        gather_wd(3, 1, 2, ("hb2", 0))
         down(0, [4, 5], False)
         down(1, [4, 5], True)
         turn_wd(3, 0, 1, RING[0])
         down(2, [0, 2, 1, 3], True)
         down(2, [4, 5], False)
-        turn_wd(3, 1, 2, RING[2])
-        s31 = base(3, 1, RING[1])
-        quant_h(6, ("wb20", 0))
-        sign_wd(3, 0, 1, ("wd3", 0))
-        quant_wd(3, 0, 1)
-        sign_wd(3, 1, 2)
-        quant_h(7, ("wb30", 0))
+        turn_wd(3, 1, 2, RING[1])
+        s31 = base(3, 1, RING[2])
+        sign_wd(3, 0, 1)
+        quant_h(3, ("wd3", 0))
+        sign_wd(3, 1, 2, ("hb3", 0))
+        quant_wd(3, 0, 1, ("hb3", 8 * W))
         quant_wd(3, 1, 2)
-        for n in range(3):
-            down(n, [6], False)
+        for r in (6, 7):
+            for n in range(3):
+                down(n, [r], r == 7 and n > 0)
         down(3, [0, 2], False)
         down(3, [4, 6], False)
-        down(0, [7], False)
-        down(1, [7], True)
-        down(2, [7], True)
         down(3, [1, 3], True)
         down(3, [5, 7], True)
         store("resp2", p2, pair_rows(0, 2), "s", ("act7", 0))
         store("res20", s20, rows(2, 0), "s", ("act7", 4 * BANK))
-        store("resp3", p3, pair_rows(0, 3), "v")
-        store("res21", s21, rows(2, 1), "s")
+        store("resp3", p3, pair_rows(0, 3), "s")
+        store("res21", s21, rows(2, 1), "v")
         store("res30", s30, rows(3, 0), "v")
         store("res31", s31, rows(3, 1), "s")

@@ -234,19 +234,30 @@ def tile_list_cardinality_margin_corrections_kernel(
                     scale=nroot[:, at : at + 1],
                 )
 
-        def square(r):
-            if r % 2 == 0:
-                hb[r // 2] = shared("hb%d" % (r // 2), [P, JP, W, PACK], BF16, 8 * W * JP)
-            dst, src = interleaved(hb[r // 2][:, r % 2], act[r][:])
-            nc.scalar.activation(dst, src, ACT.Square)
+        def rounded(r0, r1, over=None):
+            tile = shared("hb%d" % r0, [P, r1 - r0, W, PACK], BF16, 8 * W * (r1 - r0), over)
+            for r in range(r0, r1):
+                hb[r] = (tile, r - r0)
 
-        def quant_h(c, over=None):
-            codes = shared("hq%d" % c, [P, JP * W], U32, 4 * W * JP, over)
-            scales = shared("hs%d" % c, [P, JP * W], U8, W * JP)
-            quantize(codes[:], scales[:], hb[c][:].rearrange("p b m t -> p (b m) t"))
-            for b in range(JP):
-                hq[2 * c + b] = codes[:, chunk(b)]
-                hs[2 * c + b] = scales[:, chunk(b)]
+        def square(r, eng="s"):
+            tile, i = hb[r]
+            dst, src = interleaved(tile[:, i], act[r][:])
+            if eng == "s":
+                nc.scalar.activation(dst, src, ACT.Square)
+            elif eng == "v":
+                nc.vector.tensor_tensor(dst, src, src, ALU.mult)
+            else:
+                src = act[r][:].rearrange("p t m -> p m t")
+                nc.gpsimd.tensor_tensor(tile[:, i], src, src, ALU.mult)
+
+        def quant_h(r0, r1, over=None):
+            tile, i = hb[r0]
+            codes = shared("hq%d" % r0, [P, (r1 - r0) * W], U32, 4 * W * (r1 - r0), over)
+            scales = shared("hs%d" % r0, [P, (r1 - r0) * W], U8, W * (r1 - r0))
+            quantize(codes[:], scales[:], tile[:, i : i + r1 - r0].rearrange("p b m t -> p (b m) t"))
+            for r in range(r0, r1):
+                hq[r] = codes[:, chunk(r - r0)]
+                hs[r] = scales[:, chunk(r - r0)]
 
         wg, wt, wb, wq, ws = {}, {}, {}, {}, {}
 
@@ -382,16 +393,18 @@ def tile_list_cardinality_margin_corrections_kernel(
         hinge(0)
         hinge(1)
         hinge(2)
-        square(0)
         hinge(3)
         cast_x(1, 0, "g")
         cast_x(1, 1, "v")
         quant_x(1, 0)
         quant_x(1, 1)
+        rounded(0, 2, ("xr11", 0))
+        square(0, "v")
         unit(4)
         square(1)
         unit(5)
         unit(6)
+        rounded(2, 4)
         square(2)
         scores(7, SUMS[0])
         hinge(7)
@@ -404,13 +417,14 @@ def tile_list_cardinality_margin_corrections_kernel(
         quant_x(2, 0)
         quant_x(2, 1)
         sign_wd(0, 0, 2, ("xb20", 0))
-        quant_h(0, ("xb21", 0))
+        quant_h(0, 2, ("xb21", 0))
         quant_wd(0, 0, 2)
         unit(8)
         square(3)
         unit(9)
         s20 = base(2, 0, SUMS[3])
         unit(10)
+        rounded(4, 6)
         square(4)
         p2 = base_pair(0, 2, SUMS[0])
         down(0, [0, 1], False)
@@ -421,7 +435,7 @@ def tile_list_cardinality_margin_corrections_kernel(
         quant_x(3, 0)
         quant_x(3, 1)
         sign_wd(1, 0, 2, ("xb30", 0))
-        quant_h(1, ("xb31", 0))
+        quant_h(2, 4, ("xb31", 0))
         quant_wd(1, 0, 2)
         unit(11)
         s30 = base(3, 0, SUMS[4])
@@ -433,41 +447,44 @@ def tile_list_cardinality_margin_corrections_kernel(
         unit(13)
         store("res10", s10, rows(1, 0), "s")
         unit(14)
+        rounded(6, 8)
         square(6)
-        gather_wd(2, 0, 2, ("hb1", 0))
-        turn_wd(2, 0, 2, RING[1])
+        s21 = base(2, 1, RING[1])
+        p3 = base_pair(0, 3, SUMS[1])
+        gather_wd(2, 0, 2, ("hb2", 0))
+        turn_wd(2, 0, 2, SUMS[2])
         scores(15, RING[2])
         hinge(15)
         square(7)
-        p3 = base_pair(0, 3, SUMS[1])
-        s21 = base(2, 1, SUMS[2])
-        quant_h(2, ("wb10", 0))
+        quant_h(4, 6, ("wb10", 0))
+        gather_wd(3, 0, 1, ("wg10", 0))
         sign_wd(2, 0, 2, ("wd2", 0))
-        gather_wd(3, 0, 1, ("wg20", 0))
-        quant_wd(2, 0, 2)
-        gather_wd(3, 1, 2, ("hb2", 0))
+        turn_wd(3, 0, 1, RING[0])
         down(0, [4, 5], False)
         down(1, [4, 5], True)
-        turn_wd(3, 0, 1, RING[0])
+        s31 = base(3, 1, RING[2])
+        sign_wd(3, 0, 1, ("wg20", 0))
+        quant_wd(2, 0, 2)
+        quant_wd(3, 0, 1)
+        gather_wd(3, 1, 2, ("wb20", 0))
         down(2, [0, 2, 1, 3], True)
         down(2, [4, 5], False)
-        turn_wd(3, 1, 2, RING[1])
-        s31 = base(3, 1, RING[2])
-        sign_wd(3, 0, 1)
-        quant_h(3, ("wd3", 0))
-        sign_wd(3, 1, 2, ("hb3", 0))
-        quant_wd(3, 0, 1, ("hb3", 8 * W))
-        quant_wd(3, 1, 2)
-        for r in (6, 7):
-            for n in range(3):
-                down(n, [r], r == 7 and n > 0)
+        turn_wd(3, 1, 2, SUMS[2])
         down(3, [0, 2], False)
-        down(3, [4, 6], False)
+        down(3, [4], False)
+        quant_h(6, 7, ("wb30", 0))
+        sign_wd(3, 1, 2)
+        quant_h(7, 8)
+        quant_wd(3, 1, 2)
+        for n in range(NT):
+            down(n, [6], False)
         down(3, [1, 3], True)
-        down(3, [5, 7], True)
+        down(3, [5], False)
+        for n in range(NT):
+            down(n, [7], n > 0)
         store("resp2", p2, pair_rows(0, 2), "s", ("act7", 0))
         store("res20", s20, rows(2, 0), "s", ("act7", 4 * BANK))
+        store("res30", s30, rows(3, 0), "v")
         store("resp3", p3, pair_rows(0, 3), "s")
         store("res21", s21, rows(2, 1), "v")
-        store("res30", s30, rows(3, 0), "v")
         store("res31", s31, rows(3, 1), "s")

@@ -26,6 +26,10 @@ NT = N // P
 BANK = 512
 W = 256
 NC = M // W
+RUN = 4
+GROUP = 16
+QUADS = 4
+SMALL = 64
 TINY = 2.0 ** -100
 RING = (0, 1, 2)
 SUMS = (3, 4, 5, 6, 7)
@@ -33,15 +37,20 @@ SUMS = (3, 4, 5, 6, 7)
 
 def interleaved(dst, src):
     return (
-        dst.rearrange("p (c k) t -> p c t k", k=4),
-        src.rearrange("p t (c k) -> p c t k", k=4),
+        dst.rearrange("p (c k) t -> p c t k", k=RUN),
+        src.rearrange("p t (c k) -> p c t k", k=RUN),
     )
+
+
+def chunk(c):
+    return slice(c * W, (c + 1) * W)
 
 
 def tile_list_cardinality_margin_corrections_kernel(
     tc, tab_words, tab_scales, offs, x, g, wdT, w4_words, w4_scales, out
 ):
     nc = tc.nc
+    vector, scalar, gpsimd = nc.vector, nc.scalar, nc.gpsimd
     with ExitStack() as ctx:
         keep = ctx.enter_context(tc.tile_pool(name="keep", bufs=1))
         reuse = ctx.enter_context(tc.tile_pool(name="reuse", bufs=1))
@@ -50,441 +59,372 @@ def tile_list_cardinality_margin_corrections_kernel(
         def bank(i):
             return psum.tile([P, BANK], F32, name="bank%d" % i)
 
-        def sb(name, shape, dtype):
+        def kept(name, shape, dtype):
             return keep.tile(shape, dtype, name=name, align_bytes=64)
 
         place = {"end": 0}
 
-        def shared(name, shape, dtype, size, over=None):
-            if over is None:
+        def placed(name, shape, dtype, size, after=None):
+            if after is None:
                 place[name] = place["end"]
                 place["end"] = place["end"] + size
             else:
-                place[name] = place[over[0]] + over[1]
+                place[name] = place[after[0]] + after[1]
             return reuse.tile(shape, dtype, name=name, align_bytes=64, offset=place[name])
 
+        offsets = keep.tile([P, S // GROUP], U16, name="offsets")
+
         def list_part(b0, b1):
-            return offsets[:, b0 * (PASS // 16) : b1 * (PASS // 16)]
+            return offsets[:, b0 * (PASS // GROUP) : b1 * (PASS // GROUP)]
 
-        offsets = keep.tile([P, S // 16], U16, name="offsets")
-        gain = sb("gain", [P, JP, PACK], F32)
-        tsc = shared("tsc", [P, T], U8, T)
-        w4s = sb("w4s", [P, KP, N], U8)
-        w4w = sb("w4w", [P, KP, 2 * N], U8)
-        ident = sb("ident", [P, P], F32)
-        tab = [shared("tab%d" % a, [P, T], I32, 4 * T) for a in range(KP)]
-        wd = [shared("wd%d" % n, [P, T], F32, 4 * T) for n in range(NT)]
-        xraw = {(c, a): shared("xr%d%d" % (c, a), [P, PACK, W], F32, 16 * W) for c in range(NC) for a in range(KP)}
+        gain = kept("gain", [P, JP, PACK], F32)
+        tab_sc = placed("tab_sc", [P, T], U8, T)
+        w4_sc = kept("w4_sc", [P, KP, N], U8)
+        w4 = kept("w4", [P, KP, 2 * N], U8)
+        ident = kept("ident", [P, P], F32)
+        tab = [placed("tab%d" % a, [P, T], I32, 4 * T) for a in range(KP)]
+        wd = [placed("wd%d" % n, [P, T], F32, 4 * T) for n in range(NT)]
+        x_raw = {(c, a): placed("x_raw%d%d" % (c, a), [P, PACK, W], F32, 16 * W) for c in range(NC) for a in range(KP)}
 
-        nc.vector.memset(tsc[:].bitcast(I32), 0)
-        nc.gpsimd.memset(w4s[:].bitcast(I32), 0)
+        vector.memset(tab_sc[:].bitcast(I32), 0)
+        gpsimd.memset(w4_sc[:].bitcast(I32), 0)
 
-        def load_x(c, passes=range(KP)):
-            for a in passes:
-                rows = x[a * PASS : (a + 1) * PASS, c * W : (c + 1) * W]
-                nc.sync.dma_start(xraw[c, a][:], rows.rearrange("(p i) m -> p i m", i=PACK))
+        def load_x(c):
+            for a in range(KP):
+                src = x[a * PASS : (a + 1) * PASS, chunk(c)]
+                nc.sync.dma_start(x_raw[c, a][:], src.rearrange("(p t) m -> p t m", t=PACK))
 
         def load_tab(a):
-            nc.sync.dma_start(tab[a][:], tab_words[a].rearrange("p t i -> p (t i)").bitcast(I32))
-
-        def load_tab_scales():
-            for q in range(4):
-                nc.sync.dma_start(
-                    tsc[32 * q : 32 * q + 4 * KP, :].bitcast(I32),
-                    tab_scales[:, 4 * q : 4 * q + 4, :].bitcast(I32),
-                )
-
-        def load_gain():
-            nc.sync.dma_start(gain[:], g.rearrange("(b p t) -> p b t", b=JP, t=PACK))
+            nc.sync.dma_start(tab[a][:], tab_words[a].rearrange("p c t -> p (c t)").bitcast(I32))
 
         def load_wd(n):
             nc.sync.dma_start(wd[n][:], wdT[n * P : (n + 1) * P, :])
 
-        def load_w4_scales():
-            for q in range(4):
-                nc.sync.dma_start(
-                    w4s[32 * q : 32 * q + 4, :, :].bitcast(I32),
-                    w4_scales[:, 4 * q : 4 * q + 4, :].rearrange("a r c -> r a c").bitcast(I32),
-                )
-
-        def load_w4_words():
-            nc.sync.dma_start(w4w[:].bitcast(I32), w4_words.rearrange("a p c -> p a c").bitcast(I32))
-
         nc.sync.dma_start(offsets[:], offs)
-        load_gain()
-        load_tab_scales()
+        nc.sync.dma_start(gain[:], g.rearrange("(b p t) -> p b t", b=JP, t=PACK))
+        for q in range(QUADS):
+            nc.sync.dma_start(
+                tab_sc[32 * q : 32 * q + 4 * KP, :].bitcast(I32),
+                tab_scales[:, 4 * q : 4 * q + 4, :].bitcast(I32),
+            )
         load_tab(0)
         load_x(0)
         load_tab(1)
-        load_w4_scales()
+        for q in range(QUADS):
+            nc.sync.dma_start(
+                w4_sc[32 * q : 32 * q + 4, :, :].bitcast(I32),
+                w4_scales[:, 4 * q : 4 * q + 4, :].rearrange("a r c -> r a c").bitcast(I32),
+            )
         load_x(1)
         load_wd(0)
         load_x(2)
-        load_w4_words()
+        nc.sync.dma_start(w4[:].bitcast(I32), w4_words.rearrange("a p c -> p a c").bitcast(I32))
         load_wd(1)
         load_x(3)
         load_wd(2)
         load_wd(3)
         make_identity(nc, ident[:])
 
-        def small(name, dtype=F32):
-            return sb(name, [P, JP * PACK], dtype)
+        root, neg_root, root0, corr = [kept(name, [P, JP * PACK], F32) for name in ("root", "neg_root", "root0", "corr")]
+        mag = placed("mag", [P, JP * PACK], F32, SMALL)
+        inv = placed("inv", [P, JP * PACK], F32, SMALL, ("tab_sc", 0))
+        sign = placed("sign", [P, JP * PACK], BF16, SMALL, ("mag", 0))
+        gains = gain[:].rearrange("p b t -> p (b t)")
 
-        root, nroot = small("root"), small("nroot")
-
-        root0, corr = small("root0"), small("corr")
-        mag = shared("mag", [P, JP * PACK], F32, 64)
-        inv = shared("inv", [P, JP * PACK], F32, 64, ("tsc", 0))
-        sign = shared("sign", [P, JP * PACK], BF16, 64, ("mag", 0))
-        gv = gain[:].rearrange("p b t -> p (b t)")
-
-        tsg, tsp, tg = {}, {}, {}
+        sc_listed, sc_sorted, tab_listed = {}, {}, {}
 
         def gather_scales(b):
-            tsg[b] = sb("tsg%d" % b, [P, PASS], U8)
-            nc.vector.tensor_copy(tsg[b][:], tsc[:].indirect(list_part(b, b + 1)))
+            sc_listed[b] = kept("sc_listed%d" % b, [P, PASS], U8)
+            vector.tensor_copy(sc_listed[b][:], tab_sc[:].indirect(list_part(b, b + 1)))
 
         def sort_scales(b):
-            tsp[b] = sb("tsp%d" % b, [P, PACK, P], U8)
-            nc.vector.tensor_copy(tsp[b][:], tsg[b][:].rearrange("p (i t) -> p t i", t=PACK))
+            sc_sorted[b] = kept("sc_sorted%d" % b, [P, PACK, P], U8)
+            vector.tensor_copy(sc_sorted[b][:], sc_listed[b][:].rearrange("p (i t) -> p t i", t=PACK))
 
-        def gather_tab(a, b0, b1, over=None):
-            words = shared("tg%d%d" % (a, b0), [P, b1 - b0, PACK, P], U32, 4 * PASS * (b1 - b0), over)
-            nc.vector.tensor_copy(
-                words[:].rearrange("p b t i -> p b i t"), tab[a][:].bitcast(U32).indirect(list_part(b0, b1))
+        def gather_tab(a, b, after=None):
+            words = placed("tab_listed%d%d" % (a, b), [P, 1, PACK, P], U32, 4 * PASS, after)
+            vector.tensor_copy(
+                words[:].rearrange("p o t i -> p o i t"), tab[a][:].bitcast(U32).indirect(list_part(b, b + 1))
             )
-            for b in range(b0, b1):
-                tg[a, b] = words[:, b - b0]
-
-        xb, xq, xs, hb, hq, hs, act, score = {}, {}, {}, {}, {}, {}, {}, {}
-
-        def chunk(c):
-            return slice(c * W, (c + 1) * W)
-
-        def cast_x(c, a, engines, over=None):
-            xb[c, a] = shared("xb%d%d" % (c, a), [P, W, PACK], BF16, 8 * W, over)[:]
-            w = W // len(engines)
-            for i, eng in enumerate(engines):
-                cols = slice(i * w, (i + 1) * w)
-                dst, src = interleaved(xb[c, a][:, cols, :], xraw[c, a][:, :, cols])
-                if eng == "s":
-                    nc.scalar.copy(dst, src)
-                elif eng == "v":
-                    nc.vector.tensor_copy(dst, src)
-                else:
-                    nc.gpsimd.tensor_scalar(
-                        xb[c, a][:, cols, :],
-                        xraw[c, a][:, :, cols].rearrange("p t m -> p m t"),
-                        1.0,
-                        0.0,
-                        ALU.mult,
-                        ALU.add,
-                    )
+            tab_listed[a, b] = words[:, 0]
 
         def quantize(codes, scales, values):
-            nc.vector.quantize_mx(codes.bitcast(FP8X4), scales, values.rearrange("p m t -> p (m t)"))
+            vector.quantize_mx(codes.bitcast(FP8X4), scales, values.rearrange("p m t -> p (m t)"))
 
-        def quant_x(c, a, over=None):
-            h = c // 2
-            if c % 2 == 0:
-                xq[h, a] = shared("xq%d%d" % (h, a), [P, BANK], U32, 4 * BANK, over)
-                xs[h, a] = shared("xs%d%d" % (h, a), [P, BANK], U8, BANK)
-            quantize(xq[h, a][:, chunk(c % 2)], xs[h, a][:, chunk(c % 2)], xb[c, a])
+        x_bf, x_q, x_s = {}, {}, {}
 
-        def scores(u, bk):
+        def cast_x(c, a, engine, after=None):
+            x_bf[c, a] = placed("x_bf%d%d" % (c, a), [P, W, PACK], BF16, 8 * W, after)[:]
+            if engine is gpsimd:
+                src = x_raw[c, a][:].rearrange("p t m -> p m t")
+                engine.tensor_scalar(x_bf[c, a], src, 1.0, 0.0, ALU.mult, ALU.add)
+            elif engine is scalar:
+                engine.copy(*interleaved(x_bf[c, a], x_raw[c, a][:]))
+            else:
+                engine.tensor_copy(*interleaved(x_bf[c, a], x_raw[c, a][:]))
+
+        def quant_x(c):
+            for a in range(KP):
+                if c % 2 == 0:
+                    x_q[c // 2, a] = placed("x_q%d%d" % (c // 2, a), [P, BANK], U32, 4 * BANK)
+                    x_s[c // 2, a] = placed("x_s%d%d" % (c // 2, a), [P, BANK], U8, BANK)
+                quantize(x_q[c // 2, a][:, chunk(c % 2)], x_s[c // 2, a][:, chunk(c % 2)], x_bf[c, a])
+
+        score = {}
+
+        def score_pass(c, b, t, a, start):
+            nc.tensor.matmul_mx(
+                out=score[c, b, t],
+                lhsT=tab_listed[a, b][:, t, :].bitcast(FP8X4),
+                lhsT_scale=sc_sorted[b][4 * a : P, t, :],
+                rhs=x_q[c // 2, a][:, chunk(c % 2)].bitcast(FP8X4),
+                rhs_scale=x_s[c // 2, a][:, chunk(c % 2)],
+                start=start,
+                stop=not start,
+            )
+
+        def first_scores(a):
+            for b in range(JP):
+                for t in range(PACK):
+                    if a == 0:
+                        score[0, b, t] = bank(PACK * b + t)[:, chunk(0)]
+                    score_pass(0, b, t, a, a == 0)
+
+        act, h_bf, h_q, h_s = {}, {}, {}, {}
+
+        def hinge(u):
             c, b, i = u // 4, u // 2 % 2, u % 2
-            score[u] = bank(bk)
-            for e in range(2):
-                for a in reversed(range(KP)):
-                    nc.tensor.matmul_mx(
-                        out=score[u][:, chunk(e)],
-                        lhsT=tg[a, b][:, 2 * i + e, :].bitcast(FP8X4),
-                        lhsT_scale=tsp[b][4 * a : P, 2 * i + e, :],
-                        rhs=xq[c // 2, a][:, chunk(c % 2)].bitcast(FP8X4),
-                        rhs_scale=xs[c // 2, a][:, chunk(c % 2)],
-                        start=(a == KP - 1),
-                        stop=(a == 0),
-                    )
-
-        def first_scores(a, b, banks):
-            for t in range(PACK):
-                if a == 0:
-                    score[b, t] = bank(banks[t])
-                nc.tensor.matmul_mx(
-                    out=score[b, t][:, 0:W],
-                    lhsT=tg[a, b][:, t, :].bitcast(FP8X4),
-                    lhsT_scale=tsp[b][4 * a : P, t, :],
-                    rhs=xq[0, a][:, 0:W].bitcast(FP8X4),
-                    rhs_scale=xs[0, a][:, 0:W],
-                    start=(a == 0),
-                    stop=(a == KP - 1),
-                )
-
-        def hinge(u, over=None):
-            r, i = u // 2, u % 2
             if i == 0:
-                act[r] = shared("act%d" % r, [P, PACK, W], F32, 16 * W, over)
-            for e in range(2):
-                at = r % 2 * PACK + 2 * i + e
-                nc.scalar.activation(
-                    act[r][:, 2 * i + e, :],
-                    score[u][:, chunk(e)] if u in score else score[r, 2 * i + e][:, 0:W],
+                act[u // 2] = placed("act%d" % (u // 2), [P, PACK, W], F32, 16 * W)
+            for t in (2 * i, 2 * i + 1):
+                at = b * PACK + t
+                scalar.activation(
+                    act[u // 2][:, t, :],
+                    score[c, b, t],
                     ACT.Relu,
                     bias=root[:, at : at + 1],
-                    scale=nroot[:, at : at + 1],
+                    scale=neg_root[:, at : at + 1],
                 )
 
-        def rounded(r0, r1, over=None):
-            tile = shared("hb%d" % r0, [P, r1 - r0, W, PACK], BF16, 8 * W * (r1 - r0), over)
-            for r in range(r0, r1):
-                hb[r] = (tile, r - r0)
+        def step(u, bk):
+            c, b, i = u // 4, u // 2 % 2, u % 2
+            tile = bank(bk)
+            for e in range(2):
+                score[c, b, 2 * i + e] = tile[:, chunk(e)]
+                for a in reversed(range(KP)):
+                    score_pass(c, b, 2 * i + e, a, a == KP - 1)
+            hinge(u)
 
-        def square(r, eng="s"):
-            tile, i = hb[r]
-            dst, src = interleaved(tile[:, i], act[r][:])
-            if eng == "s":
-                nc.scalar.activation(dst, src, ACT.Square)
-            elif eng == "v":
-                nc.vector.tensor_tensor(dst, src, src, ALU.mult)
-            else:
-                src = act[r][:].rearrange("p t m -> p m t")
-                nc.gpsimd.tensor_tensor(tile[:, i], src, src, ALU.mult)
+        def square(r):
+            if r % JP == 0:
+                h_bf[r // JP] = placed("h_bf%d" % (r // JP), [P, JP, W, PACK], BF16, 8 * W * JP)
+            scalar.activation(*interleaved(h_bf[r // JP][:, r % JP], act[r][:]), ACT.Square)
 
-        def quant_h(r0, r1, over=None):
-            tile, i = hb[r0]
-            codes = shared("hq%d" % r0, [P, (r1 - r0) * W], U32, 4 * W * (r1 - r0), over)
-            scales = shared("hs%d" % r0, [P, (r1 - r0) * W], U8, W * (r1 - r0))
-            quantize(codes[:], scales[:], tile[:, i : i + r1 - r0].rearrange("p b m t -> p (b m) t"))
-            for r in range(r0, r1):
-                hq[r] = codes[:, chunk(r - r0)]
-                hs[r] = scales[:, chunk(r - r0)]
+        def quant_h(c, b0, b1, after=None):
+            codes = placed("h_q%d%d" % (c, b0), [P, (b1 - b0) * W], U32, 4 * W * (b1 - b0), after)
+            scales = placed("h_s%d%d" % (c, b0), [P, (b1 - b0) * W], U8, W * (b1 - b0))
+            quantize(codes[:], scales[:], h_bf[c][:, b0:b1].rearrange("p b m t -> p (b m) t"))
+            for b in range(b0, b1):
+                h_q[c, b] = codes[:, chunk(b - b0)]
+                h_s[c, b] = scales[:, chunk(b - b0)]
 
-        wg, wt, wb, wq, ws = {}, {}, {}, {}, {}
+        wd_listed, wd_turned, wd_bf, wd_q, wd_s = {}, {}, {}, {}, {}
 
-        def gather_wd(n, b0, b1, over=None):
-            wg[n, b0] = shared("wg%d%d" % (n, b0), [P, 2, (b1 - b0) * P, 2], BF16, 2 * S, over)
-            nc.vector.tensor_copy(wg[n, b0][:].rearrange("p u i e -> p i u e"), wd[n][:].indirect(list_part(b0, b1)))
+        def gather_wd(n, b0, b1, after):
+            tile = placed("wd_listed%d%d" % (n, b0), [P, 2, (b1 - b0) * P, 2], BF16, 2 * S, after)
+            wd_listed[n, b0] = tile
+            vector.tensor_copy(tile[:].rearrange("p u i e -> p i u e"), wd[n][:].indirect(list_part(b0, b1)))
 
         def turn_wd(n, b0, b1, bk):
-            wt[n, b0] = bank(bk)
-            words = wg[n, b0][:].rearrange("p u i e -> p (u i e)").bitcast(F32)
+            wd_turned[n, b0] = bank(bk)
+            words = wd_listed[n, b0][:].rearrange("p u i e -> p (u i e)").bitcast(F32)
             for at in range(0, 2 * (b1 - b0) * P, P):
-                nc.tensor.transpose(wt[n, b0][:, at : at + P], words[:, at : at + P], ident[:])
+                nc.tensor.transpose(wd_turned[n, b0][:, at : at + P], words[:, at : at + P], ident[:])
 
-        def sign_wd(n, b0, b1, over=None):
+        def sign_wd(n, b0, b1, after=None):
             nb = b1 - b0
-            wb[n, b0] = shared("wb%d%d" % (n, b0), [P, nb * P, PACK], BF16, 2 * S, over)
-            nc.vector.tensor_tensor(
-                wb[n, b0][:].rearrange("p (b c) (u e) -> p b c u e", b=nb, u=2),
-                wt[n, b0][:, 0 : nb * 2 * P].bitcast(BF16).rearrange("p (u b c e) -> p b c u e", u=2, b=nb, e=2),
+            wd_bf[n, b0] = placed("wd_bf%d%d" % (n, b0), [P, nb * P, PACK], BF16, 2 * S, after)
+            vector.tensor_tensor(
+                wd_bf[n, b0][:].rearrange("p (b c) (u e) -> p b c u e", b=nb, u=2),
+                wd_turned[n, b0][:, 0 : nb * 2 * P].bitcast(BF16).rearrange("p (u b c e) -> p b c u e", u=2, b=nb, e=2),
                 sign[:, b0 * PACK : b1 * PACK]
                 .rearrange("p (b o u e) -> p b o u e", b=nb, o=1, u=2)
                 .to_broadcast([P, nb, P, 2, 2]),
                 ALU.mult,
             )
 
-        def quant_wd(n, b0, b1, over=None, over_s=None):
-            codes = shared("wq%d%d" % (n, b0), [P, (b1 - b0) * P], U32, 4 * JP * P, over)
-            scales = shared("ws%d%d" % (n, b0), [P, (b1 - b0) * P], U8, JP * P, over_s)
-            quantize(codes[:], scales[:], wb[n, b0][:])
+        def quant_wd(n, b0, b1):
+            codes = placed("wd_q%d%d" % (n, b0), [P, (b1 - b0) * P], U32, 4 * JP * P)
+            scales = placed("wd_s%d%d" % (n, b0), [P, (b1 - b0) * P], U8, JP * P)
+            quantize(codes[:], scales[:], wd_bf[n, b0][:])
             for b in range(b0, b1):
-                wq[n, b] = codes[:, (b - b0) * P : (b - b0 + 1) * P]
-                ws[n, b] = scales[:, (b - b0) * P : (b - b0 + 1) * P]
+                wd_q[n, b] = codes[:, (b - b0) * P : (b - b0 + 1) * P]
+                wd_s[n, b] = scales[:, (b - b0) * P : (b - b0 + 1) * P]
 
         acc = {}
 
-        def base(n, h, bk):
+        def base_pass(dst, n, h, a, cols, start):
+            nc.tensor.matmul_mx(
+                out=dst,
+                lhsT=w4[:, a, 2 * n * P : 2 * (n + 1) * P].bitcast(FP4X4),
+                lhsT_scale=w4_sc[:, a, n * P : (n + 1) * P],
+                rhs=x_q[h, a][:, cols].bitcast(FP8X4),
+                rhs_scale=x_s[h, a][:, cols],
+                start=start,
+                stop=False,
+            )
+
+        def open_half(n, h, bk):
             tile = bank(bk)
             for i in range(2):
                 acc[n, 2 * h + i] = tile[:, chunk(i)]
             for a in reversed(range(KP)):
-                nc.tensor.matmul_mx(
-                    out=tile[:],
-                    lhsT=w4w[:, a, 2 * n * P : 2 * (n + 1) * P].bitcast(FP4X4),
-                    lhsT_scale=w4s[:, a, n * P : (n + 1) * P],
-                    rhs=xq[h, a][:].bitcast(FP8X4),
-                    rhs_scale=xs[h, a][:],
-                    start=(a == KP - 1),
-                    stop=False,
-                )
-            return tile
+                base_pass(tile[:], n, h, a, slice(0, BANK), a == KP - 1)
+            return tile, out[n * P : (n + 1) * P, h * BANK : (h + 1) * BANK].rearrange("p (n m) -> p n m", n=1)
 
-        def base_pair(n0, c, bk):
+        def open_chunk(c, bk):
             tile = bank(bk)
-            for i in range(2):
-                n = n0 + i
-                acc[n, c] = tile[:, chunk(i)]
+            for n in range(2):
+                acc[n, c] = tile[:, chunk(n)]
                 for a in reversed(range(KP)):
                     for e in range(0, W, P):
                         cols = slice(c % 2 * W + e, c % 2 * W + e + P)
-                        nc.tensor.matmul_mx(
-                            out=tile[:, i * W + e : i * W + e + P],
-                            lhsT=w4w[:, a, 2 * n * P : 2 * (n + 1) * P].bitcast(FP4X4),
-                            lhsT_scale=w4s[:, a, n * P : (n + 1) * P],
-                            rhs=xq[c // 2, a][:, cols].bitcast(FP8X4),
-                            rhs_scale=xs[c // 2, a][:, cols],
-                            start=(i == 0 and a == KP - 1 and e == 0),
-                            stop=False,
-                        )
-            return tile
+                        first = n == 0 and a == KP - 1 and e == 0
+                        base_pass(tile[:, n * W + e : n * W + e + P], n, c // 2, a, cols, first)
+            return tile, out[0 : 2 * P, chunk(c)].rearrange("(n p) m -> p n m", n=2)
 
-        def down(n, rs, last):
-            for r in rs:
-                c, b = r // 2, r % 2
+        def down(n, cs, bs, close=False):
+            for c, b in [(c, b) for b in bs for c in cs]:
                 nc.tensor.matmul_mx(
                     out=acc[n, c],
-                    lhsT=wq[n, b].bitcast(FP8X4),
-                    lhsT_scale=ws[n, b],
-                    rhs=hq[r].bitcast(FP8X4),
-                    rhs_scale=hs[r],
+                    lhsT=wd_q[n, b].bitcast(FP8X4),
+                    lhsT_scale=wd_s[n, b],
+                    rhs=h_q[c, b].bitcast(FP8X4),
+                    rhs_scale=h_s[c, b],
                     start=False,
-                    stop=(last and r == rs[-1]),
+                    stop=close and (c, b) == (cs[-1], bs[-1]),
                 )
 
-        def store(name, tile, dst, eng, over=None):
-            res = shared(name, [P, BANK], F32, 4 * BANK, over)
-            if eng == "s":
-                nc.scalar.copy(res[:], tile[:])
+        def store(name, total, engine, after=None, queue=nc.sync):
+            tile, dst = total
+            res = placed(name, [P, BANK], F32, 4 * BANK, after)
+            if engine is scalar:
+                engine.copy(res[:], tile[:])
             else:
-                nc.vector.tensor_copy(res[:], tile[:])
-            nc.sync.dma_start(dst, res[:].rearrange("p (n m) -> p n m", n=dst.shape[1]))
+                engine.tensor_copy(res[:], tile[:])
+            queue.dma_start(dst, res[:].rearrange("p (n m) -> p n m", n=dst.shape[1]))
 
-        def rows(n, h):
-            return out[n * P : (n + 1) * P, h * BANK : (h + 1) * BANK].rearrange("p (n m) -> p n m", n=1)
-
-        def pair_rows(n0, c):
-            return out[n0 * P : (n0 + 2) * P, chunk(c)].rearrange("(n p) m -> p n m", n=2)
-
-        turn = {"next": 0}
-
-        def ring():
-            bk = RING[turn["next"] % len(RING)]
-            turn["next"] = turn["next"] + 1
-            return bk
-
-        def unit(u):
-            scores(u, ring())
-            hinge(u)
-
-        nc.vector.scalar_tensor_tensor(mag[:], gv, -1.0, gv, ALU.mult, ALU.max)
-        nc.scalar.activation(root0[:], mag[:], ACT.Sqrt, bias=TINY)
+        vector.scalar_tensor_tensor(mag[:], gains, -1.0, gains, ALU.mult, ALU.max)
+        scalar.activation(root0[:], mag[:], ACT.Sqrt, bias=TINY)
         gather_scales(0)
         gather_scales(1)
         sort_scales(0)
-        nc.vector.reciprocal(inv[:], root0[:])
+        vector.reciprocal(inv[:], root0[:])
         sort_scales(1)
-        nc.vector.scalar_tensor_tensor(corr[:], mag[:], 0.5, inv[:], ALU.mult, ALU.mult)
-        gather_tab(0, 0, 1)
-        nc.scalar.activation(sign[:], gv, ACT.Sign)
-        nc.vector.scalar_tensor_tensor(root[:], root0[:], 0.5, corr[:], ALU.mult, ALU.add)
-        nc.vector.scalar_tensor_tensor(nroot[:], root0[:], -0.5, corr[:], ALU.mult, ALU.subtract)
-        gather_tab(0, 1, 2)
-        cast_x(0, 0, "s")
-        cast_x(0, 1, "s")
-        quant_x(0, 0)
-        quant_x(0, 1)
-        first_scores(0, 0, RING + SUMS[0:1])
-        first_scores(0, 1, SUMS[1:])
-        gather_tab(1, 0, 1, ("xb00", 0))
-        gather_tab(1, 1, 2, ("xb01", 0))
-        first_scores(1, 0, None)
-        first_scores(1, 1, None)
+        vector.scalar_tensor_tensor(corr[:], mag[:], 0.5, inv[:], ALU.mult, ALU.mult)
+        gather_tab(0, 0)
+        scalar.activation(sign[:], gains, ACT.Sign, bias=TINY)
+        vector.scalar_tensor_tensor(root[:], root0[:], 0.5, corr[:], ALU.mult, ALU.add)
+        vector.scalar_tensor_tensor(neg_root[:], root0[:], -0.5, corr[:], ALU.mult, ALU.subtract)
+        gather_tab(0, 1)
+        for a in range(KP):
+            cast_x(0, a, scalar)
+        quant_x(0)
+        first_scores(0)
+        for b in range(JP):
+            gather_tab(1, b, ("x_bf0%d" % b, 0))
+        first_scores(1)
 
-        hinge(0)
-        hinge(1)
-        hinge(2)
+        for u in range(3):
+            hinge(u)
+        square(0)
         hinge(3)
-        cast_x(1, 0, "g")
-        cast_x(1, 1, "v")
-        quant_x(1, 0)
-        quant_x(1, 1)
-        rounded(0, 2, ("xr11", 0))
-        square(0, "v")
-        unit(4)
+        cast_x(1, 0, gpsimd)
+        cast_x(1, 1, vector)
+        quant_x(1)
+
+        step(4, RING[0])
         square(1)
-        unit(5)
-        unit(6)
-        rounded(2, 4)
+        step(5, RING[1])
+        step(6, RING[2])
         square(2)
-        scores(7, SUMS[0])
-        hinge(7)
-        gather_wd(0, 0, 2, ("xb10", 0))
-        cast_x(2, 0, "g")
-        cast_x(2, 1, "v")
-        turn_wd(0, 0, 2, SUMS[4])
-        s00 = base(0, 0, SUMS[1])
-        s10 = base(1, 0, SUMS[2])
-        quant_x(2, 0)
-        quant_x(2, 1)
-        sign_wd(0, 0, 2, ("xb20", 0))
-        quant_h(0, 2, ("xb21", 0))
-        quant_wd(0, 0, 2)
-        unit(8)
+        step(7, SUMS[0])
+        gather_wd(0, 0, JP, ("x_bf10", 0))
+        cast_x(2, 0, gpsimd)
+        cast_x(2, 1, vector)
+        turn_wd(0, 0, JP, SUMS[4])
+        sum00 = open_half(0, 0, SUMS[1])
+        sum10 = open_half(1, 0, SUMS[2])
+        quant_x(2)
+        sign_wd(0, 0, JP, ("x_bf20", 0))
+        quant_h(0, 0, JP, ("x_bf21", 0))
+        quant_wd(0, 0, JP)
+
+        step(8, RING[0])
         square(3)
-        unit(9)
-        s20 = base(2, 0, SUMS[3])
-        unit(10)
-        rounded(4, 6)
+        step(9, RING[1])
+        sum20 = open_half(2, 0, SUMS[3])
+        step(10, RING[2])
         square(4)
-        p2 = base_pair(0, 2, SUMS[0])
-        down(0, [0, 1], False)
-        gather_wd(1, 0, 2, ("hb0", 0))
-        cast_x(3, 0, "g", ("wb00", 0))
-        cast_x(3, 1, "v")
-        turn_wd(1, 0, 2, SUMS[4])
-        quant_x(3, 0)
-        quant_x(3, 1)
-        sign_wd(1, 0, 2, ("xb30", 0))
-        quant_h(2, 4, ("xb31", 0))
-        quant_wd(1, 0, 2)
-        unit(11)
-        s30 = base(3, 0, SUMS[4])
-        unit(12)
-        down(0, [2, 3], True)
-        down(1, [0, 1, 2, 3], True)
-        store("res00", s00, rows(0, 0), "s")
+        pair2 = open_chunk(2, SUMS[0])
+        down(0, [0], [0, 1])
+        gather_wd(1, 0, JP, ("h_bf0", 0))
+        cast_x(3, 0, gpsimd, ("wd_bf00", 0))
+        cast_x(3, 1, vector)
+        turn_wd(1, 0, JP, SUMS[4])
+        quant_x(3)
+        sign_wd(1, 0, JP, ("x_bf30", 0))
+        quant_h(1, 0, JP, ("x_bf31", 0))
+        quant_wd(1, 0, JP)
+        step(11, RING[0])
+        sum30 = open_half(3, 0, SUMS[4])
+
+        step(12, RING[1])
+        down(0, [1], [0, 1], close=True)
+        down(1, [0], [0, 1])
+        down(1, [1], [0, 1], close=True)
+        store("res00", sum00, scalar)
         square(5)
-        unit(13)
-        store("res10", s10, rows(1, 0), "s")
-        unit(14)
-        rounded(6, 8)
+        step(13, RING[2])
+        store("res10", sum10, scalar)
+        step(14, RING[0])
         square(6)
-        s21 = base(2, 1, RING[1])
-        p3 = base_pair(0, 3, SUMS[1])
-        gather_wd(2, 0, 2, ("hb2", 0))
-        turn_wd(2, 0, 2, SUMS[2])
-        scores(15, RING[2])
-        hinge(15)
+        sum21 = open_half(2, 1, RING[1])
+        pair3 = open_chunk(3, SUMS[1])
+        gather_wd(2, 0, JP, ("h_bf1", 0))
+        turn_wd(2, 0, JP, SUMS[2])
+        step(15, RING[2])
         square(7)
-        quant_h(4, 6, ("wb10", 0))
-        gather_wd(3, 0, 1, ("wg10", 0))
-        sign_wd(2, 0, 2, ("wd2", 0))
+
+        quant_h(2, 0, JP, ("wd_bf10", 0))
+        gather_wd(3, 0, 1, ("wd_listed10", 0))
+        sign_wd(2, 0, JP, ("wd2", 0))
         turn_wd(3, 0, 1, RING[0])
-        down(0, [4, 5], False)
-        down(1, [4, 5], True)
-        s31 = base(3, 1, RING[2])
-        sign_wd(3, 0, 1, ("wg20", 0))
-        quant_wd(2, 0, 2)
+        down(0, [2], [0, 1])
+        down(1, [2], [0, 1], close=True)
+        sum31 = open_half(3, 1, RING[2])
+        sign_wd(3, 0, 1, ("wd_listed20", 0))
+        quant_wd(2, 0, JP)
         quant_wd(3, 0, 1)
-        gather_wd(3, 1, 2, ("wb20", 0))
-        down(2, [0, 2, 1, 3], True)
-        down(2, [4, 5], False)
+        gather_wd(3, 1, 2, ("wd_bf20", 0))
+        down(2, [0, 1], [0, 1], close=True)
+        down(2, [2], [0, 1])
         turn_wd(3, 1, 2, SUMS[2])
-        down(3, [0, 2], False)
-        down(3, [4], False)
-        quant_h(6, 7, ("wb30", 0))
+        down(3, [0, 1, 2], [0])
+        quant_h(3, 0, 1, ("wd_bf30", 0))
         sign_wd(3, 1, 2)
-        quant_h(7, 8)
+        quant_h(3, 1, 2)
         quant_wd(3, 1, 2)
         for n in range(NT):
-            down(n, [6], False)
-        down(3, [1, 3], True)
-        down(3, [5], False)
+            down(n, [3], [0])
+        down(3, [0, 1], [1], close=True)
+        down(3, [2], [1])
         for n in range(NT):
-            down(n, [7], n > 0)
-        store("resp2", p2, pair_rows(0, 2), "s", ("act7", 0))
-        store("res20", s20, rows(2, 0), "s", ("act7", 4 * BANK))
-        store("res30", s30, rows(3, 0), "v")
-        store("resp3", p3, pair_rows(0, 3), "s")
-        store("res21", s21, rows(2, 1), "v")
-        store("res31", s31, rows(3, 1), "s")
+            down(n, [3], [1], close=n > 0)
+
+        store("res_pair2", pair2, scalar, ("act7", 0))
+        store("res20", sum20, scalar, ("act7", 4 * BANK))
+        store("res30", sum30, vector)
+        store("res_pair3", pair3, scalar)
+        store("res21", sum21, vector)
+        store("res31", sum31, scalar, queue=scalar)

@@ -125,7 +125,8 @@ def tile_list_cardinality_margin_corrections_kernel(
         load_wd(3)
         make_identity(nc, ident[:])
 
-        root, neg_root, root0, corr = [kept(name, [P, JP * PACK], F32) for name in ("root", "neg_root", "root0", "corr")]
+        names = ("root", "neg_root", "root0", "corr", "twice")
+        root, neg_root, root0, corr, twice = [kept(name, [P, JP * PACK], F32) for name in names]
         mag = placed("mag", [P, JP * PACK], F32, SMALL)
         inv = placed("inv", [P, JP * PACK], F32, SMALL, ("tab_sc", 0))
         sign = placed("sign", [P, JP * PACK], BF16, SMALL, ("mag", 0))
@@ -321,11 +322,12 @@ def tile_list_cardinality_margin_corrections_kernel(
         sort_scales(0)
         vector.reciprocal(inv[:], root0[:])
         sort_scales(1)
-        vector.scalar_tensor_tensor(corr[:], mag[:], 0.5, inv[:], ALU.mult, ALU.mult)
+        gpsimd.tensor_tensor(corr[:], mag[:], inv[:], ALU.mult)
+        gpsimd.tensor_tensor(twice[:], corr[:], root0[:], ALU.add)
         gather_tab(0, 0)
         scalar.activation(sign[:], gains, ACT.Sign, bias=TINY)
-        vector.scalar_tensor_tensor(root[:], root0[:], 0.5, corr[:], ALU.mult, ALU.add)
-        vector.scalar_tensor_tensor(neg_root[:], root0[:], -0.5, corr[:], ALU.mult, ALU.subtract)
+        gpsimd.tensor_scalar(root[:], twice[:], 0.5, 0.0, ALU.mult, ALU.add)
+        gpsimd.tensor_scalar(neg_root[:], twice[:], -0.5, 0.0, ALU.mult, ALU.add)
         gather_tab(0, 1)
         for a in range(KP):
             cast_x(0, a, scalar)

@@ -84,7 +84,7 @@ def tile_list_cardinality_margin_corrections_kernel(
         ident = kept("ident", [P, P], F32)
         tab = [placed("tab%d" % a, [P, T], I32, 4 * T) for a in range(KP)]
         wd = [placed("wd%d" % n, [P, T], F32, 4 * T) for n in range(NT)]
-        x_raw = {(c, a): placed("x_raw%d%d" % (c, a), [P, PACK, W], F32, 16 * W) for c in range(NC) for a in range(KP)}
+        x_raw = [placed("x_raw%d" % c, [P, KP, PACK, W], F32, 16 * W * KP) for c in range(NC)]
 
         vector.memset(tab_sc[:].bitcast(I32), 0)
         gpsimd.memset(w4_sc[:].bitcast(I32), 0)
@@ -92,7 +92,7 @@ def tile_list_cardinality_margin_corrections_kernel(
         def load_x(c):
             for a in range(KP):
                 src = x[a * PASS : (a + 1) * PASS, chunk(c)]
-                nc.sync.dma_start(x_raw[c, a][:], src.rearrange("(p t) m -> p t m", t=PACK))
+                nc.sync.dma_start(x_raw[c][:, a], src.rearrange("(p t) m -> p t m", t=PACK))
 
         def load_tab(a):
             nc.sync.dma_start(tab[a][:], tab_words[a].rearrange("p c t -> p (c t)").bitcast(I32))
@@ -100,13 +100,13 @@ def tile_list_cardinality_margin_corrections_kernel(
         def load_wd(n):
             nc.sync.dma_start(wd[n][:], wdT[n * P : (n + 1) * P, :])
 
-        nc.sync.dma_start(offsets[:], offs)
         nc.sync.dma_start(gain[:], g.rearrange("(b p t) -> p b t", b=JP, t=PACK))
         for q in range(QUADS):
             nc.sync.dma_start(
                 tab_sc[32 * q : 32 * q + 4 * KP, :].bitcast(I32),
                 tab_scales[:, 4 * q : 4 * q + 4, :].bitcast(I32),
             )
+        nc.sync.dma_start(offsets[:], offs)
         load_tab(0)
         load_x(0)
         load_tab(1)
@@ -125,11 +125,12 @@ def tile_list_cardinality_margin_corrections_kernel(
         load_wd(3)
         make_identity(nc, ident[:])
 
-        names = ("root", "neg_root", "root0", "corr", "twice")
-        root, neg_root, root0, corr, twice = [kept(name, [P, JP * PACK], F32) for name in names]
-        mag = placed("mag", [P, JP * PACK], F32, SMALL)
-        inv = placed("inv", [P, JP * PACK], F32, SMALL, ("tab_sc", 0))
-        sign = placed("sign", [P, JP * PACK], BF16, SMALL, ("mag", 0))
+        names = ("root", "neg_root", "root0", "corr", "inv")
+        root, neg_root, root0, corr, inv = [kept(name, [P, JP * PACK], F32) for name in names]
+        mag = placed("mag", [P, 2 * SMALL // 4], F32, SMALL + 2 * S)[:, 0 : JP * PACK]
+        last_sign = placed("last_sign", [P, JP * PACK], BF16, SMALL, ("mag", 0))
+        sign = placed("sign", [P, JP * PACK], BF16, SMALL, ("mag", SMALL))
+        signs = (sign, last_sign)
         gains = gain[:].rearrange("p b t -> p (b t)")
 
         sc_listed, sc_sorted, tab_listed = {}, {}, {}
@@ -154,22 +155,36 @@ def tile_list_cardinality_margin_corrections_kernel(
 
         x_bf, x_q, x_s = {}, {}, {}
 
-        def cast_x(c, a, engine, after=None):
-            x_bf[c, a] = placed("x_bf%d%d" % (c, a), [P, W, PACK], BF16, 8 * W, after)[:]
-            if engine is gpsimd:
-                src = x_raw[c, a][:].rearrange("p t m -> p m t")
-                engine.tensor_scalar(x_bf[c, a], src, 1.0, 0.0, ALU.mult, ALU.add)
-            elif engine is scalar:
-                engine.copy(*interleaved(x_bf[c, a], x_raw[c, a][:]))
-            else:
-                engine.tensor_copy(*interleaved(x_bf[c, a], x_raw[c, a][:]))
+        def cast_first(a):
+            x_bf[0, a] = placed("x_bf0%d" % a, [P, W, PACK], BF16, 8 * W)[:]
+            scalar.copy(*interleaved(x_bf[0, a], x_raw[0][:, a]))
+
+        def cast_x(c):
+            tile = placed("x_bf%d" % c, [P, 2, KP, P, PACK], BF16, 8 * W * KP)
+            for e in range(2):
+                vector.tensor_copy(
+                    tile[:, e].rearrange("p a (c k) t -> p a c t k", k=RUN),
+                    x_raw[c][:, :, :, e * P : (e + 1) * P].rearrange("p a t (c k) -> p a c t k", k=RUN),
+                )
+            x_bf[c] = tile
+
+        def open_x(h):
+            for a in range(KP):
+                x_q[h, a] = placed("x_q%d%d" % (h, a), [P, BANK], U32, 4 * BANK)
+                x_s[h, a] = placed("x_s%d%d" % (h, a), [P, BANK], U8, BANK)
+
+        def quant_first():
+            open_x(0)
+            for a in range(KP):
+                quantize(x_q[0, a][:, chunk(0)], x_s[0, a][:, chunk(0)], x_bf[0, a])
 
         def quant_x(c):
-            for a in range(KP):
-                if c % 2 == 0:
-                    x_q[c // 2, a] = placed("x_q%d%d" % (c // 2, a), [P, BANK], U32, 4 * BANK)
-                    x_s[c // 2, a] = placed("x_s%d%d" % (c // 2, a), [P, BANK], U8, BANK)
-                quantize(x_q[c // 2, a][:, chunk(c % 2)], x_s[c // 2, a][:, chunk(c % 2)], x_bf[c, a])
+            if c % 2 == 0:
+                open_x(c // 2)
+            for e in range(2):
+                cols = slice(c % 2 * W + e * P, c % 2 * W + (e + 1) * P)
+                for a in range(KP):
+                    quantize(x_q[c // 2, a][:, cols], x_s[c // 2, a][:, cols], x_bf[c][:, e, a])
 
         score = {}
 
@@ -231,10 +246,12 @@ def tile_list_cardinality_margin_corrections_kernel(
 
         wd_listed, wd_turned, wd_bf, wd_q, wd_s = {}, {}, {}, {}, {}
 
-        def gather_wd(n, b0, b1, after):
-            tile = placed("wd_listed%d%d" % (n, b0), [P, 2, (b1 - b0) * P, 2], BF16, 2 * S, after)
-            wd_listed[n, b0] = tile
-            vector.tensor_copy(tile[:].rearrange("p u i e -> p i u e"), wd[n][:].indirect(list_part(b0, b1)))
+        def gather_wd(n, b0, b1, after=None, whole=None):
+            first, nb = whole or (b0, b1 - b0)
+            if b0 == first:
+                wd_listed[n, b0] = placed("wd_listed%d%d" % (n, b0), [P, 2, nb * P, 2], BF16, 2 * S, after)
+            part = wd_listed[n, first][:, :, (b0 - first) * P : (b1 - first) * P, :]
+            vector.tensor_copy(part.rearrange("p u i e -> p i u e"), wd[n][:].indirect(list_part(b0, b1)))
 
         def turn_wd(n, b0, b1, bk):
             wd_turned[n, b0] = bank(bk)
@@ -248,14 +265,14 @@ def tile_list_cardinality_margin_corrections_kernel(
             vector.tensor_tensor(
                 wd_bf[n, b0][:].rearrange("p (b c) (u e) -> p b c u e", b=nb, u=2),
                 wd_turned[n, b0][:, 0 : nb * 2 * P].bitcast(BF16).rearrange("p (u b c e) -> p b c u e", u=2, b=nb, e=2),
-                sign[:, b0 * PACK : b1 * PACK]
+                signs[n // (NT - 1)][:, b0 * PACK : b1 * PACK]
                 .rearrange("p (b o u e) -> p b o u e", b=nb, o=1, u=2)
                 .to_broadcast([P, nb, P, 2, 2]),
                 ALU.mult,
             )
 
-        def quant_wd(n, b0, b1):
-            codes = placed("wd_q%d%d" % (n, b0), [P, (b1 - b0) * P], U32, 4 * JP * P)
+        def quant_wd(n, b0, b1, after=None):
+            codes = placed("wd_q%d%d" % (n, b0), [P, (b1 - b0) * P], U32, 4 * JP * P, after)
             scales = placed("wd_s%d%d" % (n, b0), [P, (b1 - b0) * P], U8, JP * P)
             quantize(codes[:], scales[:], wd_bf[n, b0][:])
             for b in range(b0, b1):
@@ -315,118 +332,106 @@ def tile_list_cardinality_margin_corrections_kernel(
                 engine.tensor_copy(res[:], tile[:])
             queue.dma_start(dst, res[:].rearrange("p (n m) -> p n m", n=dst.shape[1]))
 
-        vector.scalar_tensor_tensor(mag[:], gains, -1.0, gains, ALU.mult, ALU.max)
-        scalar.activation(root0[:], mag[:], ACT.Sqrt, bias=TINY)
+        vector.scalar_tensor_tensor(mag, gains, -1.0, gains, ALU.mult, ALU.max)
+        scalar.activation(root0[:], mag, ACT.Sqrt, bias=TINY)
+        vector.reciprocal(inv[:], root0[:])
+        vector.scalar_tensor_tensor(corr[:], mag, 0.5, inv[:], ALU.mult, ALU.mult)
+        vector.scalar_tensor_tensor(root[:], root0[:], 0.5, corr[:], ALU.mult, ALU.add)
+        vector.scalar_tensor_tensor(neg_root[:], root0[:], -0.5, corr[:], ALU.mult, ALU.subtract)
+        for tile in signs:
+            scalar.activation(tile[:], gains, ACT.Sign, bias=TINY)
         gather_scales(0)
         gather_scales(1)
         sort_scales(0)
-        vector.reciprocal(inv[:], root0[:])
         sort_scales(1)
-        gpsimd.tensor_tensor(corr[:], mag[:], inv[:], ALU.mult)
-        gpsimd.tensor_tensor(twice[:], corr[:], root0[:], ALU.add)
         gather_tab(0, 0)
-        scalar.activation(sign[:], gains, ACT.Sign, bias=TINY)
-        gpsimd.tensor_scalar(root[:], twice[:], 0.5, 0.0, ALU.mult, ALU.add)
-        gpsimd.tensor_scalar(neg_root[:], twice[:], -0.5, 0.0, ALU.mult, ALU.add)
         gather_tab(0, 1)
         for a in range(KP):
-            cast_x(0, a, scalar)
-        quant_x(0)
+            cast_first(a)
+        quant_first()
         first_scores(0)
         for b in range(JP):
             gather_tab(1, b, ("x_bf0%d" % b, 0))
         first_scores(1)
 
-        for u in range(3):
+        for u in range(4):
             hinge(u)
         square(0)
-        hinge(3)
-        cast_x(1, 0, gpsimd)
-        cast_x(1, 1, vector)
-        quant_x(1)
-
-        step(4, RING[0])
         square(1)
-        step(5, RING[1])
-        step(6, RING[2])
+        cast_x(1)
+        quant_x(1)
+        for u in range(4, 8):
+            step(u, u - 4)
         square(2)
-        step(7, SUMS[0])
-        gather_wd(0, 0, JP, ("x_bf10", 0))
-        cast_x(2, 0, gpsimd)
-        cast_x(2, 1, vector)
-        turn_wd(0, 0, JP, SUMS[4])
-        sum00 = open_half(0, 0, SUMS[1])
-        sum10 = open_half(1, 0, SUMS[2])
-        quant_x(2)
-        sign_wd(0, 0, JP, ("x_bf20", 0))
-        quant_h(0, 0, JP, ("x_bf21", 0))
-        quant_wd(0, 0, JP)
-
-        step(8, RING[0])
         square(3)
-        step(9, RING[1])
-        sum20 = open_half(2, 0, SUMS[3])
-        step(10, RING[2])
-        square(4)
-        pair2 = open_chunk(2, SUMS[0])
+        gather_wd(0, 0, JP)
+        quant_h(0, 0, 1, ("wd0", 0))
+        cast_x(2)
+        turn_wd(0, 0, JP, 7)
+        sum00 = open_half(0, 0, 4)
+        sum10 = open_half(1, 0, 5)
+        sum20 = open_half(2, 0, 6)
+        quant_x(2)
+        sign_wd(0, 0, JP, ("x_raw2", 0))
+        quant_h(0, 1, 2, ("x_bf2", 0))
+        quant_wd(0, 0, JP)
+        step(8, 0)
+        step(9, 1)
+        step(10, 2)
+        step(11, 3)
         down(0, [0], [0, 1])
-        gather_wd(1, 0, JP, ("h_bf0", 0))
-        cast_x(3, 0, gpsimd, ("wd_bf00", 0))
-        cast_x(3, 1, vector)
-        turn_wd(1, 0, JP, SUMS[4])
-        quant_x(3)
-        sign_wd(1, 0, JP, ("x_bf30", 0))
-        quant_h(1, 0, JP, ("x_bf31", 0))
-        quant_wd(1, 0, JP)
-        step(11, RING[0])
-        sum30 = open_half(3, 0, SUMS[4])
-
-        step(12, RING[1])
-        down(0, [1], [0, 1], close=True)
-        down(1, [0], [0, 1])
-        down(1, [1], [0, 1], close=True)
-        store("res00", sum00, scalar)
+        pair2 = open_chunk(2, 0)
+        square(4)
         square(5)
-        step(13, RING[2])
+        gather_wd(1, 0, JP)
+        cast_x(3)
+        turn_wd(1, 0, JP, 7)
+        sum30 = open_half(3, 0, 1)
+        quant_x(3)
+        sign_wd(1, 0, JP, ("x_raw3", 0))
+        quant_h(1, 0, JP, ("x_bf3", 0))
+        quant_wd(1, 0, JP)
+        step(12, 2)
+        down(0, [1], [0, 1], close=True)
+        store("res00", sum00, scalar)
+        step(13, 3)
+        down(1, [0, 1], [0, 1], close=True)
         store("res10", sum10, scalar)
-        step(14, RING[0])
+        step(14, 7)
+        step(15, 2)
         square(6)
-        sum21 = open_half(2, 1, RING[1])
-        pair3 = open_chunk(3, SUMS[1])
-        gather_wd(2, 0, JP, ("h_bf1", 0))
-        turn_wd(2, 0, JP, SUMS[2])
-        step(15, RING[2])
         square(7)
-
-        quant_h(2, 0, JP, ("wd_bf10", 0))
-        gather_wd(3, 0, 1, ("wd_listed10", 0))
-        sign_wd(2, 0, JP, ("wd2", 0))
-        turn_wd(3, 0, 1, RING[0])
+        gather_wd(2, 0, JP)
+        quant_h(2, 0, JP, ("wd2", 0))
+        sum21 = open_half(2, 1, 4)
+        turn_wd(2, 0, JP, 5)
+        pair3 = open_chunk(3, 3)
         down(0, [2], [0, 1])
         down(1, [2], [0, 1], close=True)
-        sum31 = open_half(3, 1, RING[2])
-        sign_wd(3, 0, 1, ("wd_listed20", 0))
+        gather_wd(3, 0, 1)
+        sign_wd(2, 0, JP)
         quant_wd(2, 0, JP)
-        quant_wd(3, 0, 1)
-        gather_wd(3, 1, 2, ("wd_bf20", 0))
+        sum31 = open_half(3, 1, 7)
+        turn_wd(3, 0, 1, 5)
         down(2, [0, 1], [0, 1], close=True)
+        gather_wd(3, 1, 2, ("sign", 0))
+        turn_wd(3, 1, 2, 2)
         down(2, [2], [0, 1])
-        turn_wd(3, 1, 2, SUMS[2])
-        down(3, [0, 1, 2], [0])
-        quant_h(3, 0, 1, ("wd_bf30", 0))
-        sign_wd(3, 1, 2)
+        sign_wd(3, 0, 1)
+        quant_h(3, 0, 1)
         quant_h(3, 1, 2)
+        sign_wd(3, 1, 2, ("act7", 0))
+        quant_wd(3, 0, 1, ("act7", 2048))
         quant_wd(3, 1, 2)
-        for n in range(NT):
-            down(n, [3], [0])
-        down(3, [0, 1], [1], close=True)
-        down(3, [2], [1])
-        for n in range(NT):
-            down(n, [3], [1], close=n > 0)
-
-        store("res_pair2", pair2, scalar, ("act7", 0))
-        store("res20", sum20, scalar, ("act7", 4 * BANK))
-        store("res30", sum30, vector)
+        for b in range(JP):
+            down(0, [3], [b])
+            down(1, [3], [b], close=b == 1)
+            down(2, [3], [b], close=b == 1)
+        down(3, [0, 1], [0, 1], close=True)
+        down(3, [2, 3], [0, 1], close=True)
+        store("res_pair2", pair2, scalar, ("act6", 0))
+        store("res20", sum20, scalar, ("act6", 2048))
         store("res_pair3", pair3, scalar)
         store("res21", sum21, vector)
-        store("res31", sum31, scalar, queue=scalar)
+        store("res30", sum30, scalar)
+        store("res31", sum31, vector)

@@ -365,7 +365,6 @@ def tile_list_cardinality_margin_corrections_kernel(
         square(2)
         square(3)
         gather_wd(0, 0, JP)
-        quant_h(0, 0, 1, ("wd0", 0))
         cast_x(2)
         turn_wd(0, 0, JP, 7)
         sum00 = open_half(0, 0, 4)
@@ -373,7 +372,7 @@ def tile_list_cardinality_margin_corrections_kernel(
         sum20 = open_half(2, 0, 6)
         quant_x(2)
         sign_wd(0, 0, JP, ("x_raw2", 0))
-        quant_h(0, 1, 2, ("x_bf2", 0))
+        quant_h(0, 0, JP, ("x_bf2", 0))
         quant_wd(0, 0, JP)
         step(8, 0)
         step(9, 1)
@@ -392,31 +391,31 @@ def tile_list_cardinality_margin_corrections_kernel(
         quant_h(1, 0, JP, ("x_bf3", 0))
         quant_wd(1, 0, JP)
         step(12, 2)
-        down(0, [1], [0, 1], close=True)
-        store("res00", sum00, scalar)
         step(13, 3)
+        down(0, [1], [0, 1], close=True)
         down(1, [0, 1], [0, 1], close=True)
+        store("res00", sum00, scalar)
         store("res10", sum10, scalar)
         step(14, 7)
         step(15, 2)
         square(6)
         square(7)
         gather_wd(2, 0, JP)
-        quant_h(2, 0, JP, ("wd2", 0))
-        sum21 = open_half(2, 1, 4)
-        turn_wd(2, 0, JP, 5)
         pair3 = open_chunk(3, 3)
-        down(0, [2], [0, 1])
-        down(1, [2], [0, 1], close=True)
+        turn_wd(2, 0, JP, 4)
+        sum21 = open_half(2, 1, 5)
+        sum31 = open_half(3, 1, 7)
         gather_wd(3, 0, 1)
         sign_wd(2, 0, JP)
+        quant_h(2, 0, JP, ("wd_listed20", 0))
         quant_wd(2, 0, JP)
-        sum31 = open_half(3, 1, 7)
-        turn_wd(3, 0, 1, 5)
+        turn_wd(3, 0, 1, 4)
+        down(0, [2], [0, 1])
+        down(1, [2], [0, 1], close=True)
         down(2, [0, 1], [0, 1], close=True)
         gather_wd(3, 1, 2, ("sign", 0))
-        turn_wd(3, 1, 2, 2)
         down(2, [2], [0, 1])
+        turn_wd(3, 1, 2, 2)
         sign_wd(3, 0, 1)
         quant_h(3, 0, 1)
         quant_h(3, 1, 2)
@@ -433,5 +432,5 @@ def tile_list_cardinality_margin_corrections_kernel(
         store("res20", sum20, scalar, ("act6", 2048))
         store("res_pair3", pair3, scalar)
         store("res21", sum21, vector)
-        store("res30", sum30, scalar)
-        store("res31", sum31, vector)
+        store("res30", sum30, vector)
+        store("res31", sum31, scalar, queue=scalar)

@@ -86,7 +86,7 @@ def tile_list_cardinality_margin_corrections_kernel(
         wd = [placed("wd%d" % n, [P, T], F32, 4 * T) for n in range(NT)]
         x_raw = [placed("x_raw%d" % c, [P, KP, PACK, W], F32, 16 * W * KP) for c in range(NC)]
 
-        vector.memset(tab_sc[:].bitcast(I32), 0)
+        gpsimd.memset(tab_sc[:].bitcast(I32), 0)
         gpsimd.memset(w4_sc[:].bitcast(I32), 0)
 
         def load_x(c):
@@ -125,8 +125,9 @@ def tile_list_cardinality_margin_corrections_kernel(
         load_wd(3)
         make_identity(nc, ident[:])
 
-        names = ("root", "neg_root", "root0", "corr", "inv")
-        root, neg_root, root0, corr, inv = [kept(name, [P, JP * PACK], F32) for name in names]
+        inv = placed("inv", [P, JP * PACK], F32, SMALL, ("tab_sc", 0))
+        names = ("root", "neg_root", "root0", "corr")
+        root, neg_root, root0, corr = [kept(name, [P, JP * PACK], F32) for name in names]
         mag = placed("mag", [P, 2 * SMALL // 4], F32, SMALL + 2 * S)[:, 0 : JP * PACK]
         last_sign = placed("last_sign", [P, JP * PACK], BF16, SMALL, ("mag", 0))
         sign = placed("sign", [P, JP * PACK], BF16, SMALL, ("mag", SMALL))
@@ -200,23 +201,28 @@ def tile_list_cardinality_margin_corrections_kernel(
             )
 
         def first_scores(a):
-            for b in range(JP):
-                for t in range(PACK):
-                    if a == 0:
-                        score[0, b, t] = bank(PACK * b + t)[:, chunk(0)]
-                    score_pass(0, b, t, a, a == 0)
+            for t in range(PACK):
+                if a == 0:
+                    score[0, 0, t] = bank(t)[:, chunk(0)]
+                score_pass(0, 0, t, a, a == 0)
+
+        def later_scores():
+            for t in range(PACK):
+                score[0, 1, t] = bank(PACK + t)[:, chunk(0)]
+                for a in reversed(range(KP)):
+                    score_pass(0, 1, t, a, a == KP - 1)
 
         act, h_bf, h_q, h_s = {}, {}, {}, {}
 
         def hinge(u):
             c, b, i = u // 4, u // 2 % 2, u % 2
             if i == 0:
-                act[u // 2] = placed("act%d" % (u // 2), [P, PACK, W], F32, 16 * W)
+                act[u // 2] = placed("act%d" % (u // 2), [P, W // RUN, PACK, RUN], F32, 16 * W)
             for t in (2 * i, 2 * i + 1):
                 at = b * PACK + t
                 scalar.activation(
-                    act[u // 2][:, t, :],
-                    score[c, b, t],
+                    act[u // 2][:, :, t, :],
+                    score[c, b, t].rearrange("p (c k) -> p c k", k=RUN),
                     ACT.Relu,
                     bias=root[:, at : at + 1],
                     scale=neg_root[:, at : at + 1],
@@ -234,7 +240,7 @@ def tile_list_cardinality_margin_corrections_kernel(
         def square(r):
             if r % JP == 0:
                 h_bf[r // JP] = placed("h_bf%d" % (r // JP), [P, JP, W, PACK], BF16, 8 * W * JP)
-            scalar.activation(*interleaved(h_bf[r // JP][:, r % JP], act[r][:]), ACT.Square)
+            scalar.activation(h_bf[r // JP][:, r % JP].rearrange("p (c k) t -> p c t k", k=RUN), act[r][:], ACT.Square)
 
         def quant_h(c, b0, b1, after=None):
             codes = placed("h_q%d%d" % (c, b0), [P, (b1 - b0) * W], U32, 4 * W * (b1 - b0), after)
@@ -334,17 +340,17 @@ def tile_list_cardinality_margin_corrections_kernel(
 
         vector.scalar_tensor_tensor(mag, gains, -1.0, gains, ALU.mult, ALU.max)
         scalar.activation(root0[:], mag, ACT.Sqrt, bias=TINY)
+        gather_scales(0)
+        gather_scales(1)
+        sort_scales(0)
         vector.reciprocal(inv[:], root0[:])
+        sort_scales(1)
         vector.scalar_tensor_tensor(corr[:], mag, 0.5, inv[:], ALU.mult, ALU.mult)
+        gather_tab(0, 0)
         vector.scalar_tensor_tensor(root[:], root0[:], 0.5, corr[:], ALU.mult, ALU.add)
         vector.scalar_tensor_tensor(neg_root[:], root0[:], -0.5, corr[:], ALU.mult, ALU.subtract)
         for tile in signs:
             scalar.activation(tile[:], gains, ACT.Sign, bias=TINY)
-        gather_scales(0)
-        gather_scales(1)
-        sort_scales(0)
-        sort_scales(1)
-        gather_tab(0, 0)
         gather_tab(0, 1)
         for a in range(KP):
             cast_first(a)
@@ -353,6 +359,7 @@ def tile_list_cardinality_margin_corrections_kernel(
         for b in range(JP):
             gather_tab(1, b, ("x_bf0%d" % b, 0))
         first_scores(1)
+        later_scores()
 
         for u in range(4):
             hinge(u)

@@ -84,7 +84,7 @@ def tile_list_cardinality_margin_corrections_kernel(
         ident = kept("ident", [P, P], F32)
         tab = [placed("tab%d" % a, [P, T], I32, 4 * T) for a in range(KP)]
         wd = [placed("wd%d" % n, [P, T], F32, 4 * T) for n in range(NT)]
-        x_raw = [placed("x_raw%d" % c, [P, KP, PACK, W], F32, 16 * W * KP) for c in range(NC)]
+        x_raw = {c: placed("x_raw%d" % c, [P, KP, PACK, W], F32, 16 * W * KP) for c in (0, 1, 3)}
 
         gpsimd.memset(tab_sc[:].bitcast(I32), 0)
         gpsimd.memset(w4_sc[:].bitcast(I32), 0)
@@ -93,6 +93,13 @@ def tile_list_cardinality_margin_corrections_kernel(
             for a in range(KP):
                 src = x[a * PASS : (a + 1) * PASS, chunk(c)]
                 nc.sync.dma_start(x_raw[c][:, a], src.rearrange("(p t) m -> p t m", t=PACK))
+
+        x_pass = [placed("x_pass%d" % a, [P, PACK, W], F32, 16 * W) for a in range(KP)]
+
+        def load_passes(c):
+            for a in range(KP):
+                src = x[a * PASS : (a + 1) * PASS, chunk(c)]
+                nc.sync.dma_start(x_pass[a][:], src.rearrange("(p t) m -> p t m", t=PACK))
 
         def load_tab(a):
             nc.sync.dma_start(tab[a][:], tab_words[a].rearrange("p c t -> p (c t)").bitcast(I32))
@@ -110,14 +117,14 @@ def tile_list_cardinality_margin_corrections_kernel(
         load_tab(0)
         load_x(0)
         load_tab(1)
-        for q in range(QUADS):
+        for r in range(4):
             nc.sync.dma_start(
-                w4_sc[32 * q : 32 * q + 4, :, :].bitcast(I32),
-                w4_scales[:, 4 * q : 4 * q + 4, :].rearrange("a r c -> r a c").bitcast(I32),
+                w4_sc[r:P:32, :, :].bitcast(I32),
+                w4_scales[:, r:16:4, :].rearrange("a q c -> q a c").bitcast(I32),
             )
         load_x(1)
         load_wd(0)
-        load_x(2)
+        load_passes(2)
         nc.sync.dma_start(w4[:].bitcast(I32), w4_words.rearrange("a p c -> p a c").bitcast(I32))
         load_wd(1)
         load_x(3)
@@ -161,17 +168,33 @@ def tile_list_cardinality_margin_corrections_kernel(
             scalar.copy(*interleaved(x_bf[0, a], x_raw[0][:, a]))
 
         def cast_x(c):
-            tile = placed("x_bf%d" % c, [P, 2, KP, P, PACK], BF16, 8 * W * KP)
             for e in range(2):
+                x_bf[c, e] = placed("x_bf%d%d" % (c, e), [P, KP, P, PACK], BF16, 4 * W * KP)
                 vector.tensor_copy(
-                    tile[:, e].rearrange("p a (c k) t -> p a c t k", k=RUN),
+                    x_bf[c, e][:].rearrange("p a (c k) t -> p a c t k", k=RUN),
                     x_raw[c][:, :, :, e * P : (e + 1) * P].rearrange("p a t (c k) -> p a c t k", k=RUN),
                 )
-            x_bf[c] = tile
 
-        def open_x(h):
+        def cast_pass(c, a, engines):
+            width = W // len(engines)
+            for e, engine in enumerate(engines):
+                x_one[c, a, e] = placed("x_one%d%d%d" % (c, a, e), [P, width, PACK], BF16, 8 * width)[:]
+                dst, src = interleaved(x_one[c, a, e], x_pass[a][:, :, e * width : (e + 1) * width])
+                if engine is scalar:
+                    scalar.copy(dst, src)
+                else:
+                    vector.tensor_copy(dst, src)
+
+        def quant_pass(c, a, e):
+            width = x_one[c, a, e].shape[1]
+            cols = slice(c % 2 * W + e * width, c % 2 * W + (e + 1) * width)
+            quantize(x_q[c // 2, a][:, cols], x_s[c // 2, a][:, cols], x_one[c, a, e])
+
+        x_one = {}
+
+        def open_x(h, after=None):
             for a in range(KP):
-                x_q[h, a] = placed("x_q%d%d" % (h, a), [P, BANK], U32, 4 * BANK)
+                x_q[h, a] = placed("x_q%d%d" % (h, a), [P, BANK], U32, 4 * BANK, after if a == 0 else None)
                 x_s[h, a] = placed("x_s%d%d" % (h, a), [P, BANK], U8, BANK)
 
         def quant_first():
@@ -185,7 +208,7 @@ def tile_list_cardinality_margin_corrections_kernel(
             for e in range(2):
                 cols = slice(c % 2 * W + e * P, c % 2 * W + (e + 1) * P)
                 for a in range(KP):
-                    quantize(x_q[c // 2, a][:, cols], x_s[c // 2, a][:, cols], x_bf[c][:, e, a])
+                    quantize(x_q[c // 2, a][:, cols], x_s[c // 2, a][:, cols], x_bf[c, e][:, a])
 
         score = {}
 
@@ -238,14 +261,17 @@ def tile_list_cardinality_margin_corrections_kernel(
             hinge(u)
 
         def square(r):
-            if r % JP == 0:
-                h_bf[r // JP] = placed("h_bf%d" % (r // JP), [P, JP, W, PACK], BF16, 8 * W * JP)
-            scalar.activation(h_bf[r // JP][:, r % JP].rearrange("p (c k) t -> p c t k", k=RUN), act[r][:], ACT.Square)
+            c, b = r // JP, r % JP
+            apart = c == NC - 1
+            if apart or b == 0:
+                h_bf[c, b] = placed("h_bf%d%d" % (c, b), [P, 1 if apart else JP, W, PACK], BF16, 8 * W * JP)
+            dst = h_bf[c, b][:, 0] if apart else h_bf[c, 0][:, b]
+            scalar.activation(dst.rearrange("p (c k) t -> p c t k", k=RUN), act[r][:], ACT.Square)
 
         def quant_h(c, b0, b1, after=None):
             codes = placed("h_q%d%d" % (c, b0), [P, (b1 - b0) * W], U32, 4 * W * (b1 - b0), after)
             scales = placed("h_s%d%d" % (c, b0), [P, (b1 - b0) * W], U8, W * (b1 - b0))
-            quantize(codes[:], scales[:], h_bf[c][:, b0:b1].rearrange("p b m t -> p (b m) t"))
+            quantize(codes[:], scales[:], h_bf[c, b0][:].rearrange("p b m t -> p (b m) t"))
             for b in range(b0, b1):
                 h_q[c, b] = codes[:, chunk(b - b0)]
                 h_s[c, b] = scales[:, chunk(b - b0)]
@@ -311,10 +337,7 @@ def tile_list_cardinality_margin_corrections_kernel(
             for n in range(2):
                 acc[n, c] = tile[:, chunk(n)]
                 for a in reversed(range(KP)):
-                    for e in range(0, W, P):
-                        cols = slice(c % 2 * W + e, c % 2 * W + e + P)
-                        first = n == 0 and a == KP - 1 and e == 0
-                        base_pass(tile[:, n * W + e : n * W + e + P], n, c // 2, a, cols, first)
+                    base_pass(acc[n, c], n, c // 2, a, chunk(c % 2), n == 0 and a == KP - 1)
             return tile, out[0 : 2 * P, chunk(c)].rearrange("(n p) m -> p n m", n=2)
 
         def down(n, cs, bs, close=False):
@@ -372,14 +395,18 @@ def tile_list_cardinality_margin_corrections_kernel(
         square(2)
         square(3)
         gather_wd(0, 0, JP)
-        cast_x(2)
+        cast_pass(2, 0, [vector])
+        cast_pass(2, 1, [vector, vector])
         turn_wd(0, 0, JP, 7)
         sum00 = open_half(0, 0, 4)
         sum10 = open_half(1, 0, 5)
         sum20 = open_half(2, 0, 6)
-        quant_x(2)
-        sign_wd(0, 0, JP, ("x_raw2", 0))
-        quant_h(0, 0, JP, ("x_bf2", 0))
+        open_x(1, ("x_pass1", 0))
+        quant_pass(2, 1, 0)
+        quant_pass(2, 0, 0)
+        quant_pass(2, 1, 1)
+        sign_wd(0, 0, JP, ("x_pass1", 2048))
+        quant_h(0, 0, JP, ("x_one210", 0))
         quant_wd(0, 0, JP)
         step(8, 0)
         step(9, 1)
@@ -395,7 +422,7 @@ def tile_list_cardinality_margin_corrections_kernel(
         sum30 = open_half(3, 0, 1)
         quant_x(3)
         sign_wd(1, 0, JP, ("x_raw3", 0))
-        quant_h(1, 0, JP, ("x_bf3", 0))
+        quant_h(1, 0, JP, ("x_bf31", 0))
         quant_wd(1, 0, JP)
         step(12, 2)
         step(13, 3)

@@ -132,9 +132,8 @@ def tile_list_cardinality_margin_corrections_kernel(
         load_wd(3)
         make_identity(nc, ident[:])
 
-        inv = placed("inv", [P, JP * PACK], F32, SMALL, ("tab_sc", 0))
-        names = ("root", "neg_root", "root0", "corr")
-        root, neg_root, root0, corr = [kept(name, [P, JP * PACK], F32) for name in names]
+        names = ("root", "neg_root")
+        root, neg_root = [kept(name, [P, JP * PACK], F32) for name in names]
         mag = placed("mag", [P, 2 * SMALL // 4], F32, SMALL + 2 * S)[:, 0 : JP * PACK]
         last_sign = placed("last_sign", [P, JP * PACK], BF16, SMALL, ("mag", 0))
         sign = placed("sign", [P, JP * PACK], BF16, SMALL, ("mag", SMALL))
@@ -362,16 +361,13 @@ def tile_list_cardinality_margin_corrections_kernel(
             queue.dma_start(dst, res[:].rearrange("p (n m) -> p n m", n=dst.shape[1]))
 
         vector.scalar_tensor_tensor(mag, gains, -1.0, gains, ALU.mult, ALU.max)
-        scalar.activation(root0[:], mag, ACT.Sqrt, bias=TINY)
+        scalar.activation(root[:], mag, ACT.Sqrt)
+        scalar.activation(neg_root[:], root[:], ACT.Copy, scale=-1.0)
         gather_scales(0)
         gather_scales(1)
         sort_scales(0)
-        vector.reciprocal(inv[:], root0[:])
         sort_scales(1)
-        vector.scalar_tensor_tensor(corr[:], mag, 0.5, inv[:], ALU.mult, ALU.mult)
         gather_tab(0, 0)
-        vector.scalar_tensor_tensor(root[:], root0[:], 0.5, corr[:], ALU.mult, ALU.add)
-        vector.scalar_tensor_tensor(neg_root[:], root0[:], -0.5, corr[:], ALU.mult, ALU.subtract)
         for tile in signs:
             scalar.activation(tile[:], gains, ACT.Sign, bias=TINY)
         gather_tab(0, 1)

@@ -108,22 +108,22 @@ def tile_list_cardinality_margin_corrections_kernel(
             nc.sync.dma_start(wd[n][:], wdT[n * P : (n + 1) * P, :])
 
         nc.sync.dma_start(gain[:], g.rearrange("(b p t) -> p b t", b=JP, t=PACK))
+        nc.sync.dma_start(offsets[:], offs)
         for q in range(QUADS):
             nc.sync.dma_start(
                 tab_sc[32 * q : 32 * q + 4 * KP, :].bitcast(I32),
                 tab_scales[:, 4 * q : 4 * q + 4, :].bitcast(I32),
             )
-        nc.sync.dma_start(offsets[:], offs)
         load_tab(0)
         load_x(0)
         load_tab(1)
+        load_x(1)
+        load_wd(0)
         for r in range(4):
             nc.sync.dma_start(
                 w4_sc[r:P:32, :, :].bitcast(I32),
                 w4_scales[:, r:16:4, :].rearrange("a q c -> q a c").bitcast(I32),
             )
-        load_x(1)
-        load_wd(0)
         load_passes(2)
         nc.sync.dma_start(w4[:].bitcast(I32), w4_words.rearrange("a p c -> p a c").bitcast(I32))
         load_wd(1)
@@ -431,8 +431,8 @@ def tile_list_cardinality_margin_corrections_kernel(
         square(6)
         square(7)
         gather_wd(2, 0, JP)
-        pair3 = open_chunk(3, 3)
         turn_wd(2, 0, JP, 4)
+        pair3 = open_chunk(3, 3)
         sum21 = open_half(2, 1, 5)
         sum31 = open_half(3, 1, 7)
         gather_wd(3, 0, 1)

from contextlib import ExitStack

import concourse.mybir as mybir
from concourse.masks import make_identity

K, T, S, M, N = 1024, 2048, 1024, 1024, 512
FLOPS = 2 * M * (K * S + S * N + K * N)

F32 = mybir.dt.float32
BF16 = mybir.dt.bfloat16
I32 = mybir.dt.int32
U32 = mybir.dt.uint32
U16 = mybir.dt.uint16
U8 = mybir.dt.uint8
FP8X4 = mybir.dt.float8_e4m3fn_x4
FP4X4 = mybir.dt.float4_e2m1fn_x4
ALU = mybir.AluOpType
ACT = mybir.ActivationFunctionType

P = 128
PACK = 4
PASS = P * PACK
KP = K // PASS
JP = S // PASS
NT = N // P
BANK = 512
W = 256
NC = M // W
RUN = 4
GROUP = 16
QUADS = 4
SMALL = 64
TINY = 2.0 ** -100
RING = (0, 1, 2)
SUMS = (3, 4, 5, 6, 7)


def interleaved(dst, src):
    return (
        dst.rearrange("p (c k) t -> p c t k", k=RUN),
        src.rearrange("p t (c k) -> p c t k", k=RUN),
    )


def chunk(c):
    return slice(c * W, (c + 1) * W)


def tile_list_cardinality_margin_corrections_kernel(
    tc, tab_words, tab_scales, offs, x, g, wdT, w4_words, w4_scales, out
):
    nc = tc.nc
    vector, scalar, gpsimd = nc.vector, nc.scalar, nc.gpsimd
    with ExitStack() as ctx:
        keep = ctx.enter_context(tc.tile_pool(name="keep", bufs=1))
        reuse = ctx.enter_context(tc.tile_pool(name="reuse", bufs=1))
        psum = ctx.enter_context(tc.psum_pool(name="psum", bufs=1))

        def bank(i):
            return psum.tile([P, BANK], F32, name="bank%d" % i)

        def kept(name, shape, dtype):
            return keep.tile(shape, dtype, name=name, align_bytes=64)

        place = {"end": 0}

        def placed(name, shape, dtype, size, after=None):
            if after is None:
                place[name] = place["end"]
                place["end"] = place["end"] + size
            else:
                place[name] = place[after[0]] + after[1]
            return reuse.tile(shape, dtype, name=name, align_bytes=64, offset=place[name])

        offsets = keep.tile([P, S // GROUP], U16, name="offsets")

        def list_part(b0, b1):
            return offsets[:, b0 * (PASS // GROUP) : b1 * (PASS // GROUP)]

        gain = kept("gain", [P, JP, PACK], F32)
        tab_sc = placed("tab_sc", [P, T], U8, T)
        w4_sc = kept("w4_sc", [P, KP, N], U8)
        w4 = kept("w4", [P, KP, 2 * N], U8)
        ident = kept("ident", [P, P], F32)
        tab = [placed("tab%d" % a, [P, T], I32, 4 * T) for a in range(KP)]
        wd = [placed("wd%d" % n, [P, T], F32, 4 * T) for n in range(NT)]
        x_raw = {c: placed("x_raw%d" % c, [P, KP, PACK, W], F32, 16 * W * KP) for c in (0, 1, 3)}

        gpsimd.memset(tab_sc[:].bitcast(I32), 0)
        gpsimd.memset(w4_sc[:].bitcast(I32), 0)

        def load_x(c):
            for a in range(KP):
                src = x[a * PASS : (a + 1) * PASS, chunk(c)]
                nc.sync.dma_start(x_raw[c][:, a], src.rearrange("(p t) m -> p t m", t=PACK))

        x_pass = [placed("x_pass%d" % a, [P, PACK, W], F32, 16 * W) for a in range(KP)]

        def load_passes(c):
            for a in range(KP):
                src = x[a * PASS : (a + 1) * PASS, chunk(c)]
                nc.sync.dma_start(x_pass[a][:], src.rearrange("(p t) m -> p t m", t=PACK))

        def load_tab(a):
            nc.sync.dma_start(tab[a][:], tab_words[a].rearrange("p c t -> p (c t)").bitcast(I32))

        def load_wd(n):
            nc.sync.dma_start(wd[n][:], wdT[n * P : (n + 1) * P, :])

        nc.sync.dma_start(gain[:], g.rearrange("(b p t) -> p b t", b=JP, t=PACK))
        nc.sync.dma_start(offsets[:], offs)
        for q in range(QUADS):
            nc.sync.dma_start(
                tab_sc[32 * q : 32 * q + 4 * KP, :].bitcast(I32),
                tab_scales[:, 4 * q : 4 * q + 4, :].bitcast(I32),
            )
        load_tab(0)
        load_x(0)
        load_tab(1)
        load_x(1)
        load_wd(0)
        for r in range(4):
            nc.sync.dma_start(
                w4_sc[r:P:32, :, :].bitcast(I32),
                w4_scales[:, r:16:4, :].rearrange("a q c -> q a c").bitcast(I32),
            )
        load_passes(2)
        nc.sync.dma_start(w4[:].bitcast(I32), w4_words.rearrange("a p c -> p a c").bitcast(I32))
        load_wd(1)
        load_x(3)
        load_wd(2)
        load_wd(3)
        make_identity(nc, ident[:])

        names = ("root", "neg_root")
        root, neg_root = [kept(name, [P, JP * PACK], F32) for name in names]
        mag = placed("mag", [P, 2 * SMALL // 4], F32, SMALL + 2 * S)[:, 0 : JP * PACK]
        last_sign = placed("last_sign", [P, JP * PACK], BF16, SMALL, ("mag", 0))
        sign = placed("sign", [P, JP * PACK], BF16, SMALL, ("mag", SMALL))
        signs = (sign, last_sign)
        gains = gain[:].rearrange("p b t -> p (b t)")

        sc_listed, sc_sorted, tab_listed = {}, {}, {}

        def gather_scales(b):
            sc_listed[b] = kept("sc_listed%d" % b, [P, PASS], U8)
            vector.tensor_copy(sc_listed[b][:], tab_sc[:].indirect(list_part(b, b + 1)))

        def sort_scales(b):
            sc_sorted[b] = kept("sc_sorted%d" % b, [P, PACK, P], U8)
            vector.tensor_copy(sc_sorted[b][:], sc_listed[b][:].rearrange("p (i t) -> p t i", t=PACK))

        def gather_tab(a, b, after=None):
            words = placed("tab_listed%d%d" % (a, b), [P, 1, PACK, P], U32, 4 * PASS, after)
            vector.tensor_copy(
                words[:].rearrange("p o t i -> p o i t"), tab[a][:].bitcast(U32).indirect(list_part(b, b + 1))
            )
            tab_listed[a, b] = words[:, 0]

        def quantize(codes, scales, values):
            vector.quantize_mx(codes.bitcast(FP8X4), scales, values.rearrange("p m t -> p (m t)"))

        x_bf, x_q, x_s = {}, {}, {}

        def cast_first(a):
            x_bf[0, a] = placed("x_bf0%d" % a, [P, W, PACK], BF16, 8 * W)[:]
            scalar.copy(*interleaved(x_bf[0, a], x_raw[0][:, a]))

        def cast_x(c):
            for e in range(2):
                x_bf[c, e] = placed("x_bf%d%d" % (c, e), [P, KP, P, PACK], BF16, 4 * W * KP)
                vector.tensor_copy(
                    x_bf[c, e][:].rearrange("p a (c k) t -> p a c t k", k=RUN),
                    x_raw[c][:, :, :, e * P : (e + 1) * P].rearrange("p a t (c k) -> p a c t k", k=RUN),
                )

        def cast_pass(c, a, engines):
            width = W // len(engines)
            for e, engine in enumerate(engines):
                x_one[c, a, e] = placed("x_one%d%d%d" % (c, a, e), [P, width, PACK], BF16, 8 * width)[:]
                dst, src = interleaved(x_one[c, a, e], x_pass[a][:, :, e * width : (e + 1) * width])
                if engine is scalar:
                    scalar.copy(dst, src)
                else:
                    vector.tensor_copy(dst, src)

        def quant_pass(c, a, e):
            width = x_one[c, a, e].shape[1]
            cols = slice(c % 2 * W + e * width, c % 2 * W + (e + 1) * width)
            quantize(x_q[c // 2, a][:, cols], x_s[c // 2, a][:, cols], x_one[c, a, e])

        x_one = {}

        def open_x(h, after=None):
            for a in range(KP):
                x_q[h, a] = placed("x_q%d%d" % (h, a), [P, BANK], U32, 4 * BANK, after if a == 0 else None)
                x_s[h, a] = placed("x_s%d%d" % (h, a), [P, BANK], U8, BANK)

        def quant_first():
            open_x(0)
            for a in range(KP):
                quantize(x_q[0, a][:, chunk(0)], x_s[0, a][:, chunk(0)], x_bf[0, a])

        def quant_x(c):
            if c % 2 == 0:
                open_x(c // 2)
            for e in range(2):
                cols = slice(c % 2 * W + e * P, c % 2 * W + (e + 1) * P)
                for a in range(KP):
                    quantize(x_q[c // 2, a][:, cols], x_s[c // 2, a][:, cols], x_bf[c, e][:, a])

        score = {}

        def score_pass(c, b, t, a, start):
            nc.tensor.matmul_mx(
                out=score[c, b, t],
                lhsT=tab_listed[a, b][:, t, :].bitcast(FP8X4),
                lhsT_scale=sc_sorted[b][4 * a : P, t, :],
                rhs=x_q[c // 2, a][:, chunk(c % 2)].bitcast(FP8X4),
                rhs_scale=x_s[c // 2, a][:, chunk(c % 2)],
                start=start,
                stop=not start,
            )

        def first_scores(a):
            for t in range(PACK):
                if a == 0:
                    score[0, 0, t] = bank(t)[:, chunk(0)]
                score_pass(0, 0, t, a, a == 0)

        def later_scores():
            for t in range(PACK):
                score[0, 1, t] = bank(PACK + t)[:, chunk(0)]
                for a in reversed(range(KP)):
                    score_pass(0, 1, t, a, a == KP - 1)

        act, h_bf, h_q, h_s = {}, {}, {}, {}

        def hinge(u):
            c, b, i = u // 4, u // 2 % 2, u % 2
            if i == 0:
                act[u // 2] = placed("act%d" % (u // 2), [P, W // RUN, PACK, RUN], F32, 16 * W)
            for t in (2 * i, 2 * i + 1):
                at = b * PACK + t
                scalar.activation(
                    act[u // 2][:, :, t, :],
                    score[c, b, t].rearrange("p (c k) -> p c k", k=RUN),
                    ACT.Relu,
                    bias=root[:, at : at + 1],
                    scale=neg_root[:, at : at + 1],
                )

        def step(u, bk):
            c, b, i = u // 4, u // 2 % 2, u % 2
            tile = bank(bk)
            for e in range(2):
                score[c, b, 2 * i + e] = tile[:, chunk(e)]
                for a in reversed(range(KP)):
                    score_pass(c, b, 2 * i + e, a, a == KP - 1)
            hinge(u)

        def square(r):
            c, b = r // JP, r % JP
            apart = c == NC - 1
            if apart or b == 0:
                h_bf[c, b] = placed("h_bf%d%d" % (c, b), [P, 1 if apart else JP, W, PACK], BF16, 8 * W * JP)
            dst = h_bf[c, b][:, 0] if apart else h_bf[c, 0][:, b]
            scalar.activation(dst.rearrange("p (c k) t -> p c t k", k=RUN), act[r][:], ACT.Square)

        def quant_h(c, b0, b1, after=None):
            codes = placed("h_q%d%d" % (c, b0), [P, (b1 - b0) * W], U32, 4 * W * (b1 - b0), after)
            scales = placed("h_s%d%d" % (c, b0), [P, (b1 - b0) * W], U8, W * (b1 - b0))
            quantize(codes[:], scales[:], h_bf[c, b0][:].rearrange("p b m t -> p (b m) t"))
            for b in range(b0, b1):
                h_q[c, b] = codes[:, chunk(b - b0)]
                h_s[c, b] = scales[:, chunk(b - b0)]

        wd_listed, wd_turned, wd_bf, wd_q, wd_s = {}, {}, {}, {}, {}

        def gather_wd(n, b0, b1, after=None, whole=None):
            first, nb = whole or (b0, b1 - b0)
            if b0 == first:
                wd_listed[n, b0] = placed("wd_listed%d%d" % (n, b0), [P, 2, nb * P, 2], BF16, 2 * S, after)
            part = wd_listed[n, first][:, :, (b0 - first) * P : (b1 - first) * P, :]
            vector.tensor_copy(part.rearrange("p u i e -> p i u e"), wd[n][:].indirect(list_part(b0, b1)))

        def turn_wd(n, b0, b1, bk):
            wd_turned[n, b0] = bank(bk)
            words = wd_listed[n, b0][:].rearrange("p u i e -> p (u i e)").bitcast(F32)
            for at in range(0, 2 * (b1 - b0) * P, P):
                nc.tensor.transpose(wd_turned[n, b0][:, at : at + P], words[:, at : at + P], ident[:])

        def sign_wd(n, b0, b1, after=None):
            nb = b1 - b0
            wd_bf[n, b0] = placed("wd_bf%d%d" % (n, b0), [P, nb * P, PACK], BF16, 2 * S, after)
            vector.tensor_tensor(
                wd_bf[n, b0][:].rearrange("p (b c) (u e) -> p b c u e", b=nb, u=2),
                wd_turned[n, b0][:, 0 : nb * 2 * P].bitcast(BF16).rearrange("p (u b c e) -> p b c u e", u=2, b=nb, e=2),
                signs[n // (NT - 1)][:, b0 * PACK : b1 * PACK]
                .rearrange("p (b o u e) -> p b o u e", b=nb, o=1, u=2)
                .to_broadcast([P, nb, P, 2, 2]),
                ALU.mult,
            )

        def quant_wd(n, b0, b1, after=None):
            codes = placed("wd_q%d%d" % (n, b0), [P, (b1 - b0) * P], U32, 4 * JP * P, after)
            scales = placed("wd_s%d%d" % (n, b0), [P, (b1 - b0) * P], U8, JP * P)
            quantize(codes[:], scales[:], wd_bf[n, b0][:])
            for b in range(b0, b1):
                wd_q[n, b] = codes[:, (b - b0) * P : (b - b0 + 1) * P]
                wd_s[n, b] = scales[:, (b - b0) * P : (b - b0 + 1) * P]

        acc = {}

        def base_pass(dst, n, h, a, cols, start):
            nc.tensor.matmul_mx(
                out=dst,
                lhsT=w4[:, a, 2 * n * P : 2 * (n + 1) * P].bitcast(FP4X4),
                lhsT_scale=w4_sc[:, a, n * P : (n + 1) * P],
                rhs=x_q[h, a][:, cols].bitcast(FP8X4),
                rhs_scale=x_s[h, a][:, cols],
                start=start,
                stop=False,
            )

        def open_half(n, h, bk):
            tile = bank(bk)
            for i in range(2):
                acc[n, 2 * h + i] = tile[:, chunk(i)]
            for a in reversed(range(KP)):
                base_pass(tile[:], n, h, a, slice(0, BANK), a == KP - 1)
            return tile, out[n * P : (n + 1) * P, h * BANK : (h + 1) * BANK].rearrange("p (n m) -> p n m", n=1)

        def open_chunk(c, bk):
            tile = bank(bk)
            for n in range(2):
                acc[n, c] = tile[:, chunk(n)]
                for a in reversed(range(KP)):
                    base_pass(acc[n, c], n, c // 2, a, chunk(c % 2), n == 0 and a == KP - 1)
            return tile, out[0 : 2 * P, chunk(c)].rearrange("(n p) m -> p n m", n=2)

        def down(n, cs, bs, close=False):
            for c, b in [(c, b) for b in bs for c in cs]:
                nc.tensor.matmul_mx(
                    out=acc[n, c],
                    lhsT=wd_q[n, b].bitcast(FP8X4),
                    lhsT_scale=wd_s[n, b],
                    rhs=h_q[c, b].bitcast(FP8X4),
                    rhs_scale=h_s[c, b],
                    start=False,
                    stop=close and (c, b) == (cs[-1], bs[-1]),
                )

        def store(name, total, engine, after=None, queue=nc.sync):
            tile, dst = total
            res = placed(name, [P, BANK], F32, 4 * BANK, after)
            if engine is scalar:
                engine.copy(res[:], tile[:])
            else:
                engine.tensor_copy(res[:], tile[:])
            queue.dma_start(dst, res[:].rearrange("p (n m) -> p n m", n=dst.shape[1]))

        vector.scalar_tensor_tensor(mag, gains, -1.0, gains, ALU.mult, ALU.max)
        scalar.activation(root[:], mag, ACT.Sqrt)
        scalar.activation(neg_root[:], root[:], ACT.Copy, scale=-1.0)
        gather_scales(0)
        gather_scales(1)
        sort_scales(0)
        sort_scales(1)
        gather_tab(0, 0)
        for tile in signs:
            scalar.activation(tile[:], gains, ACT.Sign, bias=TINY)
        gather_tab(0, 1)
        for a in range(KP):
            cast_first(a)
        quant_first()
        first_scores(0)
        for b in range(JP):
            gather_tab(1, b, ("x_bf0%d" % b, 0))
        first_scores(1)
        later_scores()

        for u in range(4):
            hinge(u)
        square(0)
        square(1)
        cast_x(1)
        quant_x(1)
        for u in range(4, 8):
            step(u, u - 4)
        square(2)
        square(3)
        gather_wd(0, 0, JP)
        cast_pass(2, 0, [vector])
        cast_pass(2, 1, [vector, vector])
        turn_wd(0, 0, JP, 7)
        sum00 = open_half(0, 0, 4)
        sum10 = open_half(1, 0, 5)
        sum20 = open_half(2, 0, 6)
        open_x(1, ("x_pass1", 0))
        quant_pass(2, 1, 0)
        quant_pass(2, 0, 0)
        quant_pass(2, 1, 1)
        sign_wd(0, 0, JP, ("x_pass1", 2048))
        quant_h(0, 0, JP, ("x_one210", 0))
        quant_wd(0, 0, JP)
        step(8, 0)
        step(9, 1)
        step(10, 2)
        step(11, 3)
        down(0, [0], [0, 1])
        pair2 = open_chunk(2, 0)
        square(4)
        square(5)
        gather_wd(1, 0, JP)
        cast_x(3)
        turn_wd(1, 0, JP, 7)
        sum30 = open_half(3, 0, 1)
        quant_x(3)
        sign_wd(1, 0, JP, ("x_raw3", 0))
        quant_h(1, 0, JP, ("x_bf31", 0))
        quant_wd(1, 0, JP)
        step(12, 2)
        step(13, 3)
        down(0, [1], [0, 1], close=True)
        down(1, [0, 1], [0, 1], close=True)
        store("res00", sum00, scalar)
        store("res10", sum10, scalar)
        step(14, 7)
        step(15, 2)
        square(6)
        square(7)
        gather_wd(2, 0, JP)
        turn_wd(2, 0, JP, 4)
        pair3 = open_chunk(3, 3)
        sum21 = open_half(2, 1, 5)
        sum31 = open_half(3, 1, 7)
        gather_wd(3, 0, 1)
        sign_wd(2, 0, JP)
        quant_h(2, 0, JP, ("wd_listed20", 0))
        quant_wd(2, 0, JP)
        turn_wd(3, 0, 1, 4)
        down(0, [2], [0, 1])
        down(1, [2], [0, 1], close=True)
        down(2, [0, 1], [0, 1], close=True)
        gather_wd(3, 1, 2, ("sign", 0))
        down(2, [2], [0, 1])
        turn_wd(3, 1, 2, 2)
        sign_wd(3, 0, 1)
        quant_h(3, 0, 1)
        quant_h(3, 1, 2)
        sign_wd(3, 1, 2, ("act7", 0))
        quant_wd(3, 0, 1, ("act7", 2048))
        quant_wd(3, 1, 2)
        for b in range(JP):
            down(0, [3], [b])
            down(1, [3], [b], close=b == 1)
            down(2, [3], [b], close=b == 1)
        down(3, [0, 1], [0, 1], close=True)
        down(3, [2, 3], [0, 1], close=True)
        store("res_pair2", pair2, scalar, ("act6", 0))
        store("res20", sum20, scalar, ("act6", 2048))
        store("res_pair3", pair3, scalar)
        store("res21", sum21, vector)
        store("res30", sum30, vector)
        store("res31", sum31, scalar, queue=scalar)
